import numpy as np, ml_dtypes
CORES = [10,34,74,98]
N = 4
BF = ml_dtypes.bfloat16
def f(rng, *shape):
    return (rng.standard_normal(shape, dtype=np.float32) * np.exp2(rng.integers(-2, 3, shape[:-1] + (1,)))).astype(BF)
def wide(rng, *shape):
    v = f(rng, *shape).astype(np.float32); k = shape[:-2] + (1, shape[-1])
    return (v * np.exp2(rng.integers(-6, 7, k)) * (rng.random(k) > 0.0625)).astype(BF)
S, U, HB, M, CAP, TH, RO = 4096, 2048, 512, 256, 16, 9, 4
def stand(rng):
    birth = np.arange(U)[None, :] // HB; pw = rng.choice(np.array([0.7, 1.0, 1.4]), (8, 1))
    any_ = np.minimum((N * rng.random((8, U)) ** pw).astype(np.int64), N - 1)
    w = np.where(rng.random((8, U)) < 0.4, (birth + rng.integers(0, N, (8, 1))) % N, any_)
    return np.where(rng.random((8, U)) < 0.04, -1, w)
def fair(rng):
    w = np.zeros((8, U), np.int64)
    for g in range(8):
        for e in range(2): w[g, e + 2 * rng.permutation(U // 2)] = np.arange(U // 2) // (HB // 2)
    return w
def lay(rng, w):
    b = np.full((N, 8, S), U, np.int64)
    for g in range(8):
        for r in range(N):
            u = np.flatnonzero(w[g] == r); b[r, g, rng.permutation(S)[:len(u)]] = u
    return b
def squares(b):
    at = np.full((8, U), -1, np.int64)
    for g in range(8):
        for r in range(N):
            s = np.flatnonzero(b[r, g] < U); at[g, b[r, g, s]] = s
    return at
def homes(rng):
    return np.array(np.argsort(rng.random((8, N, S)), axis=-1)[..., :HB]).reshape(8, U)
def trade(c, i, s):
    x, y = int(c[i]), int(c[s]); c[i] = y; c[s] = x
def put(c, u, s):
    trade(c, int(np.flatnonzero(c == u)[0]), s)
def rehome(hm, g, u, s):
    lo = u // HB * HB; i = np.flatnonzero(hm[g, lo:lo + HB] == s)
    if len(i): hm[g, lo + int(i[0])] = hm[g, u]
    hm[g, u] = s
def ranks(v):
    return np.array(np.broadcast_to(np.asarray(v).reshape(-1, 128, U), (N, 128, U)))
def pack(b, xs, ds, hm):
    h = np.asarray(hm).astype(np.int32)
    return {"board": b.astype(np.int32), "xs": ranks(xs).astype(BF), "ds": ranks(ds).astype(np.int32), "hm": np.stack([h] * N)}
def setup_inputs(rng):
    b = lay(rng, stand(rng))
    return pack(b, f(rng, N, 128, U), rng.integers(0, S, (N, 128, U)), homes(rng))
def setup_inputs_spread(rng):
    b = lay(rng, stand(rng)); v = np.minimum(np.exp2(np.log2(S) * rng.random((N, 128, U))).astype(np.int64), S - 1)
    return pack(b, wide(rng, N, 128, U), np.where(rng.random((N, 128, U)) < 0.5, v, S - v), homes(rng))
def setup_inputs_ends(rng):
    w = fair(rng); b = np.full((N, 8, S), U, np.int64); top = np.zeros(8, np.int64)
    ds = (S - 1) * rng.integers(0, 2, (8, 16, U)) * (rng.random((8, 1, U)) > 0.125); kind = rng.choice(np.array([0, 1, 2, 3]), (8, U), p=np.array([0.3, 0.35, 0.2, 0.15]))
    for g in range(8):
        for u, r in ((0, g % N), (U - 1, (N + g - 8) % N)):
            v = int(np.flatnonzero((w[g] == r) & (np.arange(U) % 2 == u % 2))[0]); w[g, v] = w[g, u]; w[g, u] = r
        for r in range(N):
            u = np.flatnonzero(w[g] == r); e = int(np.max(u[u % 2 == 0])); o = int(np.max(u[u % 2 == 1]))
            c = np.concatenate([np.array([0, S // 8 - 1]), 1 + rng.permutation(S // 8 - 2)[:HB // 6 - 1]])
            cells = (8 * c[:, None] + np.arange(8)[None, :]).reshape(-1); cells = cells[(cells > 0) & (cells < S - 2)]
            rest = rng.permutation(u[(u != e) & (u != o)])
            b[r, g, rng.permutation(cells)[:len(rest)]] = rest; b[r, g, 0] = e; b[r, g, S - 1] = o
            kind[g, e] = 0; kind[g, o] = 1
            if r == g % N: top[g] = e
            for v in (e, o): ds[g, :, v] = 0; ds[g, 15, v] = S - 1
    order = np.argsort(np.argsort(rng.random((8, 16, U)), axis=1), axis=1)
    xs = np.where(order < np.array([16, 0, TH, TH - 1])[kind][:, None, :], 2.0 ** 20, -2.0 ** 20)
    pool = np.concatenate([np.arange(HB // 2), S - HB // 2 + np.arange(HB // 2)])
    hm = np.stack([np.concatenate([rng.permutation(pool) for p in range(N)]) for g in range(8)])
    for g in range(8):
        e = int(top[g]); lo = e // HB * HB; i = lo + int(np.flatnonzero(hm[g, lo:lo + HB] == S - 1)[0])
        hm[g, i] = hm[g, e]; hm[g, e] = S - 1
    return pack(b, xs, ds, hm)
def setup_inputs_corners(rng):
    xs = f(rng, 128, U).astype(np.float32).reshape(8, 16, U); ds = rng.integers(0, S, (8, 16, U)); hm = homes(rng); w = fair(rng)
    ds = np.where(rng.random(ds.shape) < 0.1, rng.choice(np.array([0, 1, S - 1, S // 2]), ds.shape), ds)
    gp = rng.permutation(8); off = int(rng.integers(0, 6)); ev = 2 * np.arange(U // 2); K = M // N
    pats = ([0, M + 1, M - 1], [1, M, M + 1], [0, M, M - 1], [M + 1, 1, M])
    for i in range(8):
        g = int(gp[i]); w[g, ev] = -1
        if i < 4:
            for p in range(N):
                u = p * HB + 2 * rng.permutation(HB // 2); w[g, u[:N * K]] = np.repeat(np.arange(N), K)
        else:
            c = list(pats[i - 4]); c = c + [(U // 2 - sum(c)) // (N - 3)] * (N - 3)
            w[g, rng.permutation(ev)[:sum(c)]] = np.repeat(rng.permutation(N), c)
    b = lay(rng, w); at = squares(b)
    for i in range(8):
        g = int(gp[i])
        if i < 4:
            for r in range(N):
                vic = rng.permutation(np.flatnonzero((w[g] == r) & (np.arange(U) % 2 == 1))); used = 0
                e = ev[w[g, ev] == r]; xs[g][:, e] = -64.0
                for p in range(N):
                    n = (0, 1, CAP - 1, CAP, CAP + 1, K)[(r + 2 * p + i + off) % 6]
                    a = rng.permutation(e[e // HB == p])[:n]; v = vic[used:used + n]; used += n
                    xs[g][:, a] = 64.0; ds[g, 0, a] = (at[g, v] - at[g, a]) & (S - 1)
        else:
            for p in range(N):
                u = np.arange(p * HB, (p + 1) * HB); own = u[w[g, u] == p]; oth = u[w[g, u] != p]
                left = rng.permutation(np.setdiff1d(np.arange(S), at[g, own]))
                hm[g, own] = at[g, own]; hm[g, oth] = left[:len(oth)]
    return pack(b, xs, ds, hm)
def setup_inputs_crowd(rng):
    xs = f(rng, 128, U).astype(np.float32).reshape(8, 16, U); ds = rng.integers(0, S, (8, 16, U)); hm = homes(rng); w = fair(rng)
    gp = rng.permutation(8); off = int(rng.integers(0, 6)); ev = 2 * np.arange(U // 2); od = ev + 1; K = M // N
    ga, gb, gc = int(gp[0]), int(gp[1]), int(gp[2]); o = [int(v) for v in rng.permutation(N)]; r0, r1, rd = o[0], o[1], o[2]
    w[ga, ev] = -1
    for i in (0, 2):
        w[ga, ev[ev // HB == o[i + 1]]] = o[i]; w[ga, od[w[ga, od] == o[i + 1]]] = o[i]
    w[ga, U - 1] = o[0]
    w[gb, ev] = -1
    for p in range(N):
        u = p * HB + 2 * rng.permutation(HB // 2)[:N * K]; w[gb, u] = np.repeat(np.arange(N), K)
    w[gc, od[w[gc, od] == r0]] = r1; w[gc, ev[w[gc, ev] == r1]] = r0
    z = rd * HB + 1 + 2 * int(rng.integers(0, HB // 2)); w[gc, z] = rd; w[gc, 0] = rd
    b = lay(rng, w); put(b[rd, gc], z, 0); put(b[rd, gc], 0, S - 1)
    for i in range(3, 8):
        for r in range(N):
            c = b[r, int(gp[i])]; mode = (i + r + off) % 6; place = (0, S - 1, S - 1, 0, S - 1, 0)[mode]
            u = rng.permutation(c[c < U]); e = u[u % 2 == 0]; v = u[u % 2 == 1]
            if mode < 2: put(c, int(v[0]), place)
            else: trade(c, int(rng.choice(np.flatnonzero(c == U))), place)
            if place > 0: put(c, int(e[0]), 0); put(c, int(e[1]), 1)
    at = squares(b)
    for i in range(3, 8):
        g = int(gp[i])
        for r in range(N):
            c = b[r, g]; mode = (i + r + off) % 6; place = (0, S - 1, S - 1, 0, S - 1, 0)[mode]
            u = c[c < U]; e = u[u % 2 == 0]; vic = rng.permutation(u[u % 2 == 1]); emp = rng.permutation(np.flatnonzero(c == U))
            if mode < 2: vic = np.concatenate([c[place:place + 1], vic[vic != c[place]]])
            else: emp = np.concatenate([np.array([place]), emp[emp != place]])
            j = int(rng.integers(2, M))
            if mode < 2:
                xs[g][:, e] = 64.0; to = np.full(len(e), at[g, vic[0]])
                if mode == 1: to[j] = at[g, vic[1]]
            elif mode < 4:
                xs[g][:, e] = -64.0; to = np.full(len(e), emp[0])
                if mode == 3: to[j] = emp[1]
            else:
                xs[g][:, e] = 64.0; v = vic[:len(e)]; to = at[g, v]; back = np.full(len(e), emp[0])
                if mode == 5: back[j] = emp[1]
                ds[g, 0, v] = (back - to) & (S - 1)
            ds[g, 0, e] = (to - at[g, e]) & (S - 1)
    for i in (0, 2):
        c = b[o[i], ga]; u = c[c < U]; e = u[u % 2 == 0]; v = rng.permutation(u[u % 2 == 1])
        if i == 0: v = np.concatenate([np.array([U - 1]), v[v != U - 1]]); rehome(hm, ga, int(e[0]), S - 2)
        v = v[:len(e)]; xs[ga][:, e] = 64.0; ds[ga, 0, e] = (at[ga, v] - at[ga, e]) & (S - 1)
        if i == 2: xs[ga][:, int(e[int(rng.integers(0, M))])] = -64.0
    for r in range(N):
        c = b[r, gb]; s = np.flatnonzero((c < U) & (c % 2 == 0)); e = c[s]; v = rng.permutation(c[(c < U) & (c % 2 == 1)])[:len(e)]
        xs[gb][:, e] = 64.0; ds[gb, 0, e] = (at[gb, v] - s) & (S - 1)
        u = np.arange(r * HB, (r + 1) * HB); m = (u % 2 == 0) & (w[gb, u] >= 0)
        hm[gb, u[m]] = rng.permutation(s); hm[gb, u[~m]] = rng.permutation(np.setdiff1d(np.arange(S), s))[:HB - len(s)]
    c = b[r0, gc]; e = c[c < U]; xs[gc][:, ev] = -64.0
    ds[gc, 0, e] = (int(rng.choice(np.flatnonzero(c == U))) - at[gc, e]) & (S - 1)
    xs[gc][:, 0] = 64.0; xs[gc][:, z] = 128.0; ds[gc, :, 0] = 0; ds[gc, :, z] = S - 1; rehome(hm, gc, z, 0)
    return pack(b, xs, ds, hm)
def setup_inputs_heap(rng):
    w = np.tile(((np.arange(8) + int(rng.integers(0, N))) % N)[:, None], (1, U))
    xs = rng.integers(-2, 3, (N, 128, U)).astype(np.float32) * rng.choice(np.array([-1.0, 1.0], np.float32), (N, 128, U))
    return pack(lay(rng, w), xs, rng.integers(0, S, (N, 128, U)), homes(rng))
def check_inputs(d):
    bad = []
    for k, lo, hi in (("board", 0, U), ("ds", 0, S - 1), ("hm", 0, S - 1)):
        if np.min(d[k]) < lo or np.max(d[k]) > hi: bad.append("range of " + k)
    v = np.abs(np.asarray(d["xs"]).astype(np.float32))
    if not np.all((v == 0) | ((v >= 2.0 ** -100) & (v <= 2.0 ** 20))): bad.append("range of xs")
    b = np.asarray(d["board"]).astype(np.int64); h = np.asarray(d["hm"]).astype(np.int64)
    if not np.all(h == h[:1]): bad.append("ranks alike in hm")
    for g in range(8):
        v = b[:, g].reshape(-1); v = v[v != U]
        if len(np.unique(v)) != len(v): bad.append("units of board stand once (group " + str(g) + ")")
    for q in range(h.shape[0]):
        v = np.sort(h[q].reshape(8, N, HB), axis=-1)
        if np.any(v[..., 1:] == v[..., :-1]): bad.append("distinct homes in hm (rank " + str(q) + ")")
    return bad
def first_of(keys, ok):
    w = np.zeros(len(keys), bool); i = np.flatnonzero(ok); u, at = np.unique(keys[i], return_index=True); w[i[at]] = True
    return w
def reference(board, xs, ds, hm):
    bd = np.array(board).astype(np.int64)
    x = np.asarray(xs).astype(np.float32).reshape(N, 8, 16, U); d = np.asarray(ds).astype(np.int64).reshape(N, 8, 16, U); home = np.asarray(hm).astype(np.int64)
    for t in range(RO):
        new = np.array(bd); born = []
        for r in range(N):
            for g in range(8):
                c = bd[r, g]; X = x[r, g]; D = d[r, g]
                s = np.flatnonzero((c < U) & ((c & 1) == (t & 1)))[:M]; a = c[s]; n = len(a); j = np.arange(n)
                if n == 0: continue
                q = (s[None, :] + D[:, a]) & (S - 1)
                v = c[q]; more = np.add.reduce((X[:, a][:, None, :] > X[:, np.minimum(v, U - 1)]).astype(np.int64), axis=0)
                can = (v < U) & ((v & 1) != (t & 1)) & (more >= TH)
                claim = np.any(can, axis=0); sq = q[np.argmax(can, axis=0), j]
                won = first_of(sq, claim)
                at = np.where(won, sq, s); who = np.where(won, c[sq], a)
                w = (at[None, :] + D[:, np.minimum(who, U - 1)]) & (S - 1)
                free = c[w] == U; to = w[np.argmax(free, axis=0), j]
                go = first_of(to, np.any(free, axis=0) & (won | ~claim))
                new[r, g, s] = U; new[r, g, sq[won]] = U; new[r, g, np.where(go, to, at)] = a
                for p in range(N):
                    i = np.flatnonzero(won & (a // HB == p))[:CAP]
                    born.append((p, g, home[r, g, a[i]], c[sq[i]]))
        for p, g, h, b in born:
            e = new[p, g, h] == U; new[p, g, h[e]] = b[e]
        bd = new
    return {"y": bd.astype(np.float32)}

@@ -1,0 +1,827 @@
+from concourse.bass import DstId, RemoteDMATransfer
+from concourse.mybir import AluOpType as A, AxisListType, ActivationFunctionType as F
+
+HT = "float16"
+AM = "22222222"
+NLS = 2
+QW = True
+LATE_A = True
+BIG = 2.0 ** 40
+TW = 4416
+MUL = 2.0 ** 30
+
+POOL = {"PF": ("float32", 13312), "PB": ("bfloat16", 18432), "PH": (HT, 6144), "PI": ("int32", 2048), "PU": ("uint16", 4096)}
+SCRATCH = {k: ("sbuf", [128, v[1]], v[0]) for k, v in POOL.items()}
+SCRATCH.update({
+    "LB": ("sbuf", [128, 2, 8, 16], "int32"), "CV": ("sbuf", [128, 8, 32], "int32"),
+    "X": ("sbuf", [128, 2064], "bfloat16"), "D": ("sbuf", [128, 2064], "int32"), "HM": ("sbuf", [128, 2064], "int32"),
+    "UT": ("sbuf", [128, 4608], "float32"), "B": ("sbuf", [128, TW], "float32"),
+    "XB0": ("sbuf", [128, TW], "bfloat16"), "XB1": ("sbuf", [128, TW], "bfloat16"),
+    "XE": ("sbuf", [128, 4096], "bfloat16"), "CM": ("sbuf", [128, 4096], "bfloat16"),
+    "FC": ("sbuf", [128, 16, 256], "bfloat16"), "RV": ("sbuf", [128, 64], "float32"),
+})
+for _b in ("pA", "pZ", "pK", "pS", "pC", "pE", "pW", "pX"):
+    SCRATCH[_b] = ("psum", [128, 512], "float32")
+NDMA = 24
+SEMAPHORES = ["cv", "cs", "cp", "cg", "loc", "ar0", "ar1", "ar2", "ar3"] + ["d%d" % i for i in range(NDMA)]
+WID = {"float32": 4, "bfloat16": 2, "float16": 2, "int32": 4, "uint16": 2}
+CY = 1.04
+PEC = 0.6
+HOP = 90.0
+HOP_SAME = 60.0
+GAT = 1.56
+SCA = 3.8
+TRIES = 5000
+AIM = 0.8
+WIN = 8000
+AMP = 2000
+JUST = 10
+TOL = 40.0
+LEAN = 2500.0
+SEED = 1
+KEPT = {}
+
+
+def build(T, rank):
+    ops = []
+    place = {}
+    top = {k: 0 for k in POOL}
+
+    def R(name, a, b, st=1):
+        d = SCRATCH[name]
+        ap = T[name][:, a:b] if st == 1 else T[name][:, a:b:st]
+        return {"ap": ap, "reg": (name, a, b), "n": len(range(a, b, st)), "w": WID[d[2]], "ps": d[0] == "psum", "nm": name, "a": a}
+
+    def RX(name, ap, lo, hi, n):
+        d = SCRATCH[name]
+        return {"ap": ap, "reg": (name, lo, hi), "n": n, "w": WID[d[2]], "ps": False, "nm": name, "a": lo}
+
+    def buf(pool, key, n):
+        if key not in place:
+            place[key] = top[pool]
+            top[pool] += (n + 15) // 16 * 16
+            assert top[pool] <= POOL[pool][1], pool
+        return R(pool, place[key], place[key] + n)
+
+    def sub(r, a, b, st=1):
+        return R(r["nm"], r["a"] + a, r["a"] + b, st)
+
+    def ind(win, off):
+        return {"ap": win["ap"].indirect(off["ap"]), "reg": win["reg"], "off": off, "n": 16 * off["n"], "w": 4, "ps": False}
+
+    def add(eng, fn, rd, wr, dur, lat=0.0, kind="c", ext=None):
+        reads = []
+        writes = []
+        for r in rd:
+            if isinstance(r, dict):
+                (writes if r["ps"] else reads).append((r["reg"][0], 0, 512) if r["ps"] else r["reg"])
+                if "off" in r:
+                    reads.append(r["off"]["reg"])
+        for r in wr:
+            writes.append((r["reg"][0], 0, 512) if r["ps"] else r["reg"])
+            if "off" in r:
+                reads.append(r["off"]["reg"])
+        ops.append({"eng": eng, "fn": fn, "rd": reads, "wr": writes, "dur": dur, "lat": lat, "kind": kind, "ext": ext})
+        return len(ops) - 1
+
+    def val(x):
+        return x["ap"] if isinstance(x, dict) else x
+
+    def vcost(out, ins, rate):
+        if "off" in out:
+            return 50 + out["n"] * SCA * CY
+        if "off" in ins[0]:
+            return 50 + out["n"] * GAT * CY
+        return 20 + max(64, out["n"] * rate) * CY
+
+    def half(*s):
+        return 0.5 if all(x["w"] == 2 for x in s) else 1.0
+
+    def cp(out, i):
+        add("v", lambda g: g.vector.tensor_copy(out["ap"], i["ap"]), [i], [out], vcost(out, [i], half(out, i)))
+
+    def ts(out, i, s1, op0, s2=None, op1=None):
+        if op1 is None:
+            fn = lambda g: g.vector.tensor_scalar(out["ap"], i["ap"], val(s1), None, op0)
+        else:
+            fn = lambda g: g.vector.tensor_scalar(out["ap"], i["ap"], val(s1), val(s2), op0, op1)
+        add("v", fn, [i, s1, s2], [out], vcost(out, [i], half(out, i)))
+
+    def tt(out, i0, i1, op, more=()):
+        add("v", lambda g: g.vector.tensor_tensor(out["ap"], i0["ap"], i1["ap"], op), [i0, i1] + list(more), [out],
+            vcost(out, [i0], 1.0 if i0["ps"] or i1["ps"] else 2.0))
+
+    def scan(out, d0, d1, op0, op1):
+        add("v", lambda g: g.vector.tensor_tensor_scan(out["ap"], d0["ap"], d1["ap"], 0.0, op0, op1), [d0, d1], [out],
+            vcost(out, [d0], half(out, d0, d1)))
+
+    def ms(out, c):
+        add("v", lambda g: g.vector.memset(out["ap"], c), [], [out], vcost(out, [out], half(out)))
+
+    def act(out, i, func, bias=None, scale=None, acc=None, more=()):
+        kw = {}
+        if bias is not None:
+            kw["bias"] = val(bias)
+        if scale is not None:
+            kw["scale"] = val(scale)
+        if acc is not None:
+            kw["accum_out"] = acc["ap"]
+        add("s", lambda g: g.scalar.activation(out["ap"], i["ap"], func, **kw), [i, bias, scale],
+            [out] + ([acc] if acc else []) + list(more), 20 + vcost(out, [i], 1.0))
+        o, x, fn = out["ap"], i["ap"], None
+        if acc is not None:
+            if func == F.Copy:
+                fn = lambda g: g.vector.tensor_reduce(acc["ap"], x, AxisListType.X, A.add)
+        elif func in (F.Copy, F.Silu):
+            fn = lambda g: g.vector.tensor_copy(o, x)
+        elif func == F.Identity:
+            fn = lambda g: g.vector.tensor_scalar(o, x, 1.0 if scale is None else val(scale), val(bias), A.mult, A.add)
+        elif func == F.Relu and scale is None:
+            fn = lambda g: g.vector.tensor_scalar(o, x, val(bias), 0.0, A.add, A.max)
+        elif func == F.Relu and bias is None:
+            fn = lambda g: g.vector.tensor_scalar(o, x, scale, 0.0, A.mult, A.max)
+        elif func == F.Relu:
+            fn = lambda g: g.vector.tensor_scalar(o, x, BIG, None, A.is_lt)
+        if fn:
+            ops[-1]["alt"] = {"s": (ops[-1]["fn"], ops[-1]["dur"]), "v": (fn, vcost(out, [i], half(out, i)))}
+
+    def gat(eng, out, i):
+        act(out, i, F.Copy)
+
+    def mm(out, l, r, start, stop, join=False):
+        add("p", lambda g: g.tensor.matmul(out["ap"], l["ap"], r["ap"], start, stop), [l, r], [out],
+            max(64, r["n"]) * PEC * (4 if l["w"] == 4 else 1))
+        if join:
+            b = ops.pop(); x = ops[-1]
+            x["fn"] = lambda g, f1=x["fn"], f2=b["fn"]: (f1(g), f2(g))[1]
+            x["rd"] = sorted(set(x["rd"] + b["rd"])); x["wr"] = sorted(set(x["wr"] + b["wr"])); x["dur"] += b["dur"]
+
+    def iota(out, pat, base, cm, small=True):
+        if small:
+            fn = lambda g: g.iota(out["ap"], pat, base, cm, allow_small_or_imprecise_dtypes=True)
+        else:
+            fn = lambda g: g.iota(out["ap"], pat, base, cm)
+        add("g", fn, [], [out], 130 + 2 * out["n"] * CY)
+
+    def asel(out, i, pat, op, base, cm):
+        add("g", lambda g: g.affine_select(out["ap"], i["ap"], pat, op, 0.0, base, cm), [i], [out], 170 + 2 * out["n"] * CY)
+
+    def dma(q, out, i, rd, wr, lat):
+        if q == "y":
+            fn = lambda g: g.sync.dma_start(out, i)
+        else:
+            fn = lambda g: g.scalar.dma_start(out, i)
+        add(q, fn, rd, wr, 60.0, lat, "d")
+
+    fb = lambda k, n=256: buf("PF", k, n)
+    bb = lambda k, n=256: buf("PB", k, n)
+    hb = lambda k, n=256: buf("PH", k, n)
+    ib = lambda k, n=256: buf("PI", k, n)
+    ub = lambda k, n=256: buf("PU", k, n)
+    P = lambda k, a=0, b=256: R(k, a, b)
+    L = lambda r: sub(r, 0, 256)
+    Bw = R("B", 0, TW)
+    XBw = [R("XB0", 0, TW), R("XB1", 0, TW)]
+    Xw = R("X", 0, 2064)
+    Dw = R("D", 0, 2064)
+    UTs = R("UT", 0, 2064)
+    UTw = R("UT", 0, TW)
+
+    for h in range(2):
+        dma("ys"[h], T.LB[:, h], T.board[h::2, :], [], [RX("LB", None, 128 * h, 128 * h + 128, 128)], 2200)
+    dma("y", T.X[:, 0:2048], T.xs[:], [], [R("X", 0, 2048)], 4500)
+    dma("y", T.D[:, 0:2048], T.ds[:], [], [R("D", 0, 2048)], 8000)
+    for i in range(16):
+        dma("y", T.HM[i::16, 0:512], T.hm[:, 512 * rank:512 * rank + 512], [], [RX("HM", None, 3000 + i, 3001 + i, 1)], 9000)
+    hw = 2064 - 512 * rank
+    HMw = R("HM", 0, hw)
+    HMall = RX("HM", None, 3000, 3016, 1)
+
+    ONES = bb("ones"); ms(ONES, 1.0)
+    O128 = sub(ONES, 0, 128)
+    IOT = bb("iot"); iota(IOT, [[1, 256]], 0, 0)
+    PI_ = ib("pi", 1); iota(PI_, [[0, 1]], 0, 1, False)
+    J = fb("J", 320); iota(J, [[0, 20], [1, 16]], 0, 0)
+    J4 = fb("J4", 64); iota(J4, [[0, 16], [1, 4]], 0, 0)
+    tb = bb("tb", 128); BLK = bb("blk", 128); TRI = bb("tri", 128); TRU = bb("tru", 128)
+    ROW15 = bb("row15", 128); IDB = bb("idb", 128)
+    gp = [[-16, 8], [0, 16]]
+    asel(tb, O128, gp, A.is_ge, 0, 1)
+    asel(BLK, tb, [[16, 8], [0, 16]], A.is_ge, 15, -1)
+    asel(TRI, BLK, [[1, 128]], A.is_ge, 0, -1)
+    asel(TRU, BLK, [[-1, 128]], A.is_gt, 0, 1)
+    asel(ROW15, O128, gp, A.is_equal, -15, 1)
+    asel(IDB, O128, [[-1, 128]], A.is_equal, 0, 1)
+    RM = bb("rm", 2048)
+    for j in range(8):
+        asel(sub(RM, 256 * j, 256 * j + 256), ONES, [[-1, 16], [0, 16]], A.is_equal, -16 * j, 1)
+    JP = fb("jp", 64); iota(JP, [[1, 16], [0, 4]], 0, 0)
+    DUMP = fb("dump", 64); iota(DUMP, [[1, 64]], 4352, 0)
+    iota(R("HM", 512, 2064), [[0, 1552]], 1 << 20, 0, False)
+    for k in range(4):
+        iota(R("UT", 1104 * k, 1104 * k + 1104), [[1, 1104]], 1104 * k, 0)
+    RI = ib("ri", 1); ts(RI, PI_, 15, A.bitwise_and)
+    RF = fb("rf", 1); cp(RF, RI)
+    i2 = ib("i2", 1); ts(i2, RI, 2, A.arith_shift_right)
+    RQ4 = fb("rq4", 1); cp(RQ4, i2)
+    i3 = ib("i3", 1); ts(i3, RI, 3, A.bitwise_and)
+
+    def picker(key, jt, col, last, n):
+        c1 = fb(key + "c1", 1); ts(c1, col, 1.0, A.add)
+        sc = fb(key + "sc", 1); ts(sc, col, last - 0.5, A.is_gt, 1.0 / MUL, A.max)
+        x = bb(key + "x", n); y = bb(key + "y", n); o = bb(key, n)
+        ts(x, jt, col, A.not_equal); ts(y, jt, c1, A.is_equal, MUL, A.mult); tt(o, x, y, A.max)
+        return o, sc
+    SP, SCL = picker("sp", L(J), RF, 15, 256)
+    SQ, SCQ = picker("sq", J4, RQ4, 3, 64)
+    SCQ16 = fb("scq16", 1); ts(SCQ16, SCQ, 1.0 / 16, A.mult)
+    ISC = fb("isc", 1); ts(ISC, RF, 14.5, A.is_lt, MUL, A.mult); ts(ISC, ISC, 1.0, A.max)
+    MH = fb("mh"); ts(MH, IOT, 0.5, A.add, ISC, A.mult)
+    C256 = bb("c256"); ms(C256, 256.0)
+    CBIG = bb("cbig"); ms(CBIG, BIG)
+    CE = fb("ce"); ms(CE, 2048.0)
+
+    def scaled(key, src, c, pool="PB"):
+        o = buf(pool, key, 128); ts(o, src, c, A.mult); return o
+
+    def quad(key, src, c, pool):
+        y = buf(pool, key, 132); ms(y, 0.0)
+        ts(sub(y, 3, 131, 4), sub(src, 3, 128, 4), c, A.mult)
+        return [sub(y, 3 - r, 131 - r) for r in range(4)]
+    Q8n = quad("q8n", BLK, -8.0, "PB"); QH = quad("qhh", BLK, 1.0, "PH"); Q15 = quad("q15", ROW15, 1.0, "PH")
+    QF = quad("qf", ROW15, 1.0, "PF")
+    NB = scaled("nb", BLK, -16384.0); B4n = scaled("b4n", BLK, -4096.0)
+    BLKh = scaled("bh", BLK, 1.0, "PH"); IDH = scaled("idh", IDB, 1.0, "PH")
+    ID8K = scaled("id8k", IDB, 8192.0, "PF")
+    I16 = scaled("i16", IDB, 16.0); I16n = scaled("i16n", IDB, -16384.0); I4n = scaled("i4n", IDB, -4096.0)
+    zt = scaled("zt", TRI, -4096.0); zi = scaled("zi", IDB, 8192.0); ZM = bb("zm", 128); tt(ZM, zt, zi, A.add)
+    ZC = fb("zc", 1); ts(ZC, RF, 1.0, A.add, -4096.0, A.mult)
+    tri2 = bb("tri2", 128); tt(tri2, TRI, IDB, A.subtract); TRS = scaled("trs", tri2, -16384.0)
+    Z = bb("z", 144); ms(Z, 0.0); cp(sub(Z, 15, 143, 16), sub(BLK, 0, 128, 16))
+    ZK = [sub(Z, 15 - k, 143 - k) for k in range(16)]
+    MD = bb("md"); ts(MD, L(J), RF, A.not_equal, 2.0 ** 23, A.mult); ts(MD, MD, 32768.0, A.max)
+    MP = fb("mp", 64); ts(MP, JP, RF, A.is_equal)
+    f2 = fb("f2", 1); ts(f2, i2, -2.0, A.mult, -1.0, A.add)
+    SLB = fb("slb", 4); ts(SLB, sub(J, 0, 4), -8.0, A.mult, f2, A.add)
+    QB = quad("qb", BLK, 1.0, "PB"); QB5 = quad("qb5", BLK, 0.5, "PB")
+    B128n = scaled("b128n", BLK, -128.0); B16h = scaled("b16h", BLK, 16.0, "PH"); R15h = scaled("r15h", ROW15, 1.0, "PH")
+    EQ = fb("eq16", 16); ts(EQ, sub(J, 0, 16), RF, A.is_equal)
+    ROWS = bb("rows", 2048)
+    for r in range(16):
+        act(sub(ROWS, 128 * r, 128 * r + 128), BLK, F.Identity, bias=0.0, scale=sub(EQ, r, r + 1))
+    S01 = fb("s01", 128); ms(S01, 0.0); cp(sub(S01, 1, 128, 16), sub(ROW15, 0, 128, 16))
+    SHI = bb("shi", 128); ms(SHI, 0.0); cp(sub(SHI, 0, 128, 16), sub(ROW15, 0, 128, 16))
+    ts(sub(SHI, 1, 128, 16), sub(ROW15, 0, 128, 16), -1.0, A.mult)
+    CEN = fb("cen", 1); ts(CEN, i3, -512.0, A.mult, -255.5, A.add)
+    j16 = fb("j16", 4); ts(j16, sub(J, 0, 4), 16.0, A.mult, RF, A.add)
+    VC = fb("vc", 4); ts(VC, j16, 1280.0, A.add)
+    f3 = fb("f3", 1); cp(f3, i3)
+    IOQ = bb("ioq", 64); ts(IOQ, sub(IOT, 0, 64), 4.0, A.mult, f3, A.add)
+    SM = bb("sm", 320); ms(SM, 1.0); ms(sub(SM, 0, 320, 80), 0.0); ms(sub(SM, 16, 320, 80), -1024.0)
+    IN1 = fb("in1", 320)
+    for j in range(4):
+        ts(sub(IN1, 80 * j, 80 * j + 16), sub(J, 0, 16), RF, A.not_equal, 2048.0, A.add)
+    IOU = ub("iou")
+    if "1" in AM:
+        cp(IOU, IOT)
+    Fb = bb("fb", 272); ms(sub(Fb, 0, 16), 0.0)
+    T3 = bb("t3", 272); ms(sub(T3, 256, 272), 512.0)
+    SC = fb("sc", 272); ms(sub(SC, 256, 272), 1e13)
+    PAY = fb("pay", 272); ms(sub(PAY, 256, 272), 2048.0 * 8192 + 2048)
+    ms(R("X", 2048, 2064), BIG); ms(R("X", 2048, 2049), -BIG); ms(R("D", 2048, 2064), 0)
+    ms(R("B", 4096, 4352), 2048.0); ms(R("B", 4352, TW), 0.0)
+    ms(R("XB0", 4096, TW), BIG); ms(R("XB1", 4096, TW), BIG)
+    CN = {c: c for c in (-8.5, -8.0, -65536.0, -4095.0, -2047.0, 0.5, 128.0)}
+
+    def wrap(key, src, n=256, plus=0.25):
+        s = fb("w_" + key, n); scan(s, sub(SP, 0, n), src, A.mult, A.add)
+        u = ub("u_" + key, n // 16); ts(u, sub(s, 15, n, 16), SCL, A.mult, plus, A.add)
+        return u
+
+    def qmm(bank, terms, first=True):
+        for x, (l, r) in enumerate(terms):
+            for k in range(4):
+                mm(P(bank, 0, 64), l[k], sub(r, k, 256, 4), first and x == 0 and k == 0, x == len(terms) - 1 and k == 3, k > 0)
+
+    def qwrap(key, bank, plus=0.25, scale=None):
+        s = fb("w_" + key, 64); scan(s, SQ, P(bank, 0, 64), A.mult, A.add)
+        u = ub("u_" + key, 16); ts(u, sub(s, 3, 64, 4), scale or SCQ, A.mult, plus, A.add)
+        return u
+
+    WI = ib("wi")
+    for h in range(2):
+        cp(RX("CV", T.CV[:, :, 16 * h:16 * h + 16], 0, 256, 128), RX("LB", T.LB[:, h], 128 * h, 128 * h + 128, 128))
+    for b in range(8):
+        o = sub(WI, b, 256, 8); i = RX("CV", T.CV[:, b, :], 0, 256, 32)
+        o["reg"] = ("PI", WI["a"] + 32 * b, WI["a"] + 32 * b + 32)
+        add("v", lambda g, o=o, i=i: g.vector.transpose(o["ap"], i["ap"]), [i], [o], 90.0)
+    WH = bb("wh"); cp(WH, WI)
+    WL = bb("wl"); tt(WL, WI, WH, A.subtract)
+    for r in range(16):
+        o = P(("pA", "pZ", "pK", "pC")[r % 4]); l = sub(ROWS, 128 * r, 128 * r + 128)
+        mm(o, l, WH, True, False); mm(o, l, WL, False, True)
+        d = R("B", r, 4096, 16); d["reg"] = ("B", 256 * r, 256 * r + 256)
+        act(d, o, F.Copy)
+    w1 = ib("w1"); ts(w1, WI, 2049, A.bitwise_and)
+    Fm = sub(Fb, 16, 272)
+    ts(Fm, w1, 0.0, A.is_equal)
+    OO = [ub("o0"), ub("o1")]
+    for e in (1, 0):
+        u = fb("oa"); ts(u, w1, float(e), A.not_equal, 4096.0, A.mult)
+        v = fb("oc"); tt(v, u, WI, A.add)
+        ts(OO[e], v, 2049.0, A.min)
+
+    def table(name, win, off, engs):
+        n = len(engs); w = 256 // n
+        for c in range(n):
+            gat(engs[c], R(name, 16 * w * c, 16 * w * (c + 1)), ind(win, sub(off, w * c, w * (c + 1))))
+    table("XB1", Xw, OO[1], "ssssssssssssssss")
+    table("XB0", Xw, OO[0], "ssssssssssssssss")
+
+    CS = fb("cs", 320); CA = fb("ca", 320); CQ = fb("cq", 320); CX = bb("cx", 320)
+
+    def select(b1, b2, b3, b4):
+        mm(P("pW"), TRI, Fm, True, False); mm(P("pW"), TRU, sub(Fb, 15, 271), False, True)
+        scan(L(T3), P("pW"), C256, A.add, A.min)
+        mm(P("pW", 256, 512), ROW15, L(T3), True, True)
+        s1 = fb("s1", 16); scan(s1, sub(SP, 0, 16), R("pW", 271, 512, 16), A.mult, A.add)
+        c1 = bb("c1"); act(c1, MH, F.Sign, bias=sub(s1, 15, 16), scale=-1.0)
+        scan(L(SC), SP, P("pW", 256, 512), A.mult, A.add)
+        qmm(b1, [(Q8n, c1)])
+        u1 = qwrap("l1", b1, 143.25)
+        q1 = bb("q1", 64); act(q1, P(b1, 0, 64), F.Identity, bias=CN[128.0])
+        iv = hb("iv"); ts(iv, IOT, sub(s1, 15, 16), A.subtract, 0.0, A.max)
+        c2 = hb("c2"); tt(c2, ind(SC, u1), MH, A.is_le)
+        mm(P(b2, 0, 64), IDB, q1, True, False); qmm(b2, [(QH, c2)], False)
+        u2 = qwrap("l2", b2)
+        q2 = bb("q2", 64); act(q2, P(b2, 0, 64), F.Copy)
+        c3 = hb("c3"); tt(c3, ind(T3, u2), IOT, A.is_le)
+        mm(P(b3, 0, 64), I16, q2, True, False); qmm(b3, [(Q15, iv), (QH, c3)], False)
+        u = qwrap("l3", b3)
+        o = P(b4)
+        mm(o, B128n, c1, True, False); mm(o, R15h, iv, False, False); mm(o, B16h, c2, False, False); mm(o, BLKh, c3, False, True)
+        act(L(CS), o, F.Identity, bias=2048.0)
+        return u
+
+    def targets(out, off, at, n, key):
+        q = ib("qa" + key, n); tt(q, ind(Dw, off), at, A.add)
+        q2 = ib("qb" + key, n); ts(q2, q, 4095, A.bitwise_and)
+        cp(out, q2)
+
+    def cand(u, out, t):
+        gat("s" if t else "v", L(CA), ind(Bw, u))
+        if t and QW:
+            qmm("pW", [(QF, L(CA))]); au = qwrap("a", "pW")
+        else:
+            au = wrap("a0", L(CA))
+        targets(out, au, L(CS), 256, "l")
+        act(L(CX), ind(Xw, au), F.Copy)
+
+    def first(cut, key):
+        sg = bb("good"); act(sg, P("pA"), F.Sign, bias=CN[cut])
+        mm(P("pZ"), ZM, sg, False, True); mm(P("pS"), B4n, sg, False, True)
+        mx = hb("mx"); ts(mx, P("pZ"), ZC, A.add, -2048.0, A.max)
+        s2 = bb("s2"); act(s2, P("pS"), F.Relu, bias=-65536.0)
+        qmm("pK", [(QH, mx), (QB, s2)])
+        u = qwrap(key, "pK", 32768.25)
+        wf = fb("wf", 16); cp(wf, u)
+        o = P("pZ", 256, 512)
+        mm(o, BLKh, mx, True, False); mm(o, BLK, s2, False, True)
+        ru = ub("ru"); ts(ru, o, 32768.0, A.add)
+        r = None
+        if key == "at":
+            r = fb(key); act(r, o, F.Identity, bias=32768.0)
+        mm(P("pC"), BLKh, mx, r is None, False); mm(P("pC"), BLK, s2, False, False)
+        return r, u, wf, ru
+
+    def fallback(x):
+        hi = bb("hi"); act(hi, x, F.Relu, bias=-16.0)
+        mm(P("pS"), S01, x, True, False); mm(P("pS"), SHI, hi, False, False)
+
+    def preload(qu):
+        qh = hb("qh"); ts(qh, qu, -2048.0, A.add)
+        mm(P("pZ"), IDH, qh, True, False)
+
+    def rivals(ru, wf, other, key, plus):
+        for c in range(16):
+            n = 256 - 16 * c
+            ts(RX("FC", T.FC[:, c, 0:n], 256 * c, 256 * c + n, n), sub(ru, 16 * c, 256), sub(wf, c, c + 1), A.is_equal)
+            if c < 15:
+                mm(P("pC", 16 * c + 16, 256), NB, RX("FC", T.FC[:, c, 16:n], 256 * c + 16, 256 * c + n, n - 16), False, False)
+            if c in (11, 15):
+                a = 0 if c == 11 else 12
+                mm(P("pC", 16 * a, 16 * c + 16), TRS, RX("FC", T.FC[:, a:c + 1, 0:16], 256 * a, 256 * c + 16, 16 * (c + 1 - a)), False, c == 15)
+        s = fb("w_" + key); scan(s, SP, P("pC"), A.mult, A.add)
+        x = fb("rx", 16); ts(x, sub(s, 15, 256, 16), SCL, A.mult, plus, A.add)
+        y = ib("ry", 16); tt(y, x, other, A.max)
+        z = ib("rz" + key, 16); ts(z, y, 8191, A.bitwise_and)
+        u = ub("u_" + key, 16); cp(u, z)
+        return z, u
+
+    Qu = ub("qu")
+    sU = select("pE", "pX", "pS", "pE")
+    sW = (sub(fb("w_l3", 64), 3, 64, 4), SCQ)
+    cand(sU, Qu, 0)
+    s, a, Xa = L(CS), L(CA), L(CX)
+    for t in range(4):
+        e = t & 1
+        XE_, XO = XBw[e], XBw[1 - e]
+        XT = bb("xt")
+        for h in range(2):
+            if "2" in AM[4 * h:4 * h + 4]:
+                mm(P("pW", 128 * h, 128 * h + 128), sub(Xa, 128 * h, 128 * h + 128), IDB, True, True)
+                act(sub(XT, 128 * h, 128 * h + 128), P("pW", 128 * h, 128 * h + 128), F.Copy)
+        if t == 0:
+            s0, a0, x0 = fb("s0"), fb("a0"), bb("x0")
+            act(s0, s, F.Copy); act(a0, a, F.Copy); act(x0, Xa, F.Copy)
+            s, a, Xa = s0, a0, x0
+        preload(Qu)
+        fallback(s)
+        for c in range(8):
+            xe = R("XE", 512 * c, 512 * c + 512); bank = P(("pE", "pX", "pW")[c % 3], 0, 512)
+            if AM[c] == "1":
+                act(xe, ind(Xa, sub(IOU, 32 * c, 32 * c + 32)), F.Copy)
+                tt(R("CM", 512 * c, 512 * c + 512), ind(XO, sub(Qu, 32 * c, 32 * c + 32)), xe, A.is_lt)
+            else:
+                act(xe, ind(XO, sub(Qu, 32 * c, 32 * c + 32)), F.Copy)
+                mm(bank, sub(XT, 128 * (c // 4), 128 * (c // 4) + 128), sub(RM, 512 * (c % 4), 512 * (c % 4) + 512), True, True)
+                tt(R("CM", 512 * c, 512 * c + 512), xe, bank, A.is_lt)
+            if c % 2:
+                cm = R("CM", 512 * c - 512, 512 * c + 512)
+                for k in range(16):
+                    mm(P("pA", 32 * c - 32, 32 * c + 32), ZK[k], sub(cm, k, 1024, 16), k == 0, k == 15, k % 8 > 0)
+        ivf = bb("ivf"); act(ivf, s, F.Relu, bias=CN[-4095.0])
+        dd = fb("dd"); act(dd, a, F.Abs, bias=CEN)
+        sF = fb("sF", 16); act(sF, sW[0], F.Identity, bias=0.25, scale=sW[1])
+        ds = bb("dsg"); act(ds, dd, F.Sign, bias=-256.0)
+        mm(P("pC"), IDB, MD, True, False); mm(P("pC"), I16n, ivf, False, False)
+        at, atU, wf, ru = first(-8.5, "at")
+        ncs = bb("ncs"); act(ncs, P("pS"), F.Sign, bias=-63000.0)
+        who = hb("who"); cp(who, ind(Bw, atU))
+        qmm("pX", [(QH, who)]); whoU = qwrap("who", "pX", 0.25, SCQ16)
+        Wu = ub("wu"); targets(Wu, whoU, at, 256, "w")
+        preload(Wu)
+        baseI, baseU = rivals(ru, wf, sF, "base", 8192.25)
+        E = bb("e"); act(E, P("pC"), F.Relu, scale=-1.0 / 16384)
+        base = fb("base"); act(base, ind(UTw, baseU), F.Copy)
+        fallback(base)
+        mm(P("pE"), I4n, ds, True, False); mm(P("pE"), I4n, ncs, False, False); mm(P("pE"), NB, E, False, True)
+        fl = bb("fl"); act(fl, P("pE"), F.Sign, bias=-4096.0)
+        mm(P("pX", 256, 512), ID8K, a, True, False); mm(P("pX", 256, 512), IDH, who, False, True)
+        act(L(PAY), P("pX", 256, 512), F.Copy)
+        pf = bb("pf"); scan(pf, fl, ONES, A.add, A.add)
+        acc = fb("acc", 4); junk = bb("junk")
+        for j in range(4):
+            act(junk, pf, F.Sign, bias=sub(SLB, j, j + 1), acc=sub(acc, j, j + 1))
+        ix = ub("ix", 4); ts(ix, acc, -0.5, A.mult, 128.25, A.add)
+        G = fb("g", 64); SD = fb("sd%d" % t, 4); jf = fb("jf", 64)
+        tt(G, ind(PAY, ix), MP, A.mult)
+        for p in range(4):
+            c = 16 * t + 4 * rank
+            act(sub(jf, 16 * p, 16 * p + 16), sub(G, p, 64, 4), F.Copy, acc=R("RV", c, c + 1) if p == rank else sub(SD, p, p + 1),
+                more=[R("RV", 16 * t + 4 * p, 16 * t + 4 * p + 1), sub(SD, p, p + 1)])
+        snd = add("g", ("send", t, SD), [SD], [], 300.0, 4500.0, "r")
+        for c in range(8):
+            cm = R("CM", 512 * c, 512 * c + 512); src = ind(Bw, sub(Wu, 32 * c, 32 * c + 32))
+            act(cm, src, F.Relu, bias=-2047.0)
+        for c in range(4):
+            cm = R("CM", 1024 * c, 1024 * c + 1024)
+            for k in range(16):
+                mm(P("pA", 64 * c, 64 * c + 64), ZK[k], sub(cm, k, 1024, 16), k == 0, False, k % 8 > 0)
+            mm(P("pA", 64 * c, 64 * c + 64), NB, sub(E, 64 * c, 64 * c + 64), False, True)
+        for u in (sU, baseU):
+            act(ind(Bw, u), CE, F.Silu)
+        if t < 3:
+            cp(ind(XE_, sU), CBIG)
+            cp(ind(XO, baseU), CBIG)
+            for k in range(16):
+                mm(P("pW"), ZK[k], R(XO["nm"], k, 4096, 16), k == 0, k == 15, k % 2 > 0)
+            act(Fm, P("pW"), F.Relu, bias=1.0, scale=-1.0 / BIG)
+            lU = select("pW", "pW", "pW", "pX")
+            if not LATE_A:
+                cand(lU, L(CQ), 1)
+        k2, k2U, wf, ru = first(-8.0, "k2")
+        endI, endU = rivals(ru, wf, baseI, "end", 40960.25)
+        cp(ind(Bw, endU), a)
+        if t < 3:
+            if LATE_A:
+                cand(lU, L(CQ), 1)
+            cp(ind(XE_, endU), Xa)
+        raU = ub("raU", 4); rv = R("RV", 16 * t, 16 * t + 16, 4)
+        add("v", lambda g, o=raU, i=rv: g.vector.tensor_scalar(o["ap"], i["ap"], 1.0 / 8192, 0.1 - 512.0 * rank, A.mult, A.add),
+            [rv], [raU], 90.0, ext=("ar%d" % t, snd))
+        pi = ib("rpi", 4); add("v", lambda g, o=pi, i=rv: g.vector.tensor_copy(o["ap"], i["ap"]), [rv, raU], [pi], 90.0)
+        rvv = ib("rvv", 4); ts(rvv, pi, 8191, A.bitwise_and)
+        rvU = ub("rvU", 4); cp(rvU, rvv)
+        RS, RA, RQ, RXX = sub(CS, 256, 320), sub(CA, 256, 320), sub(CQ, 256, 320), sub(CX, 256, 320)
+        tt(RS, ind(HMw, raU), DUMP, A.min, [HMall])
+        hU = wrap("h", RS, 64)
+        act(RA, ind(UTs, rvU), F.Copy)
+        vm = fb("vm", 64); act(vm, RA, F.Identity, bias=-2048.0)
+        if t < 3:
+            act(RXX, ind(Xw, rvU), F.Copy)
+            targets(RQ, rvU, RS, 64, "r")
+            hF = fb("hF", 4); act(hF, sub(fb("w_h", 64), 15, 64, 16), F.Identity, bias=-0.25, scale=SCL)
+            H20 = ub("h20", 20)
+            cp(sub(H20, 0, 20, 5), hU)
+            for j in range(4):
+                cp(sub(H20, 5 * j + 1, 5 * j + 5), hU)
+                ts(sub(IN1, 80 * j + 16, 80 * j + 80), RS, sub(hF, j, j + 1), A.is_ge, 2048.0, A.add)
+            hb_ = fb("hb", 4); act(hb_, hF, F.Identity, bias=0.25, scale=-1.0)
+            ac2 = fb("ac2", 4); jk2 = bb("jk2")
+            for j in range(4):
+                act(jk2, L(CS), F.Sign, bias=sub(hb_, j, j + 1), acc=sub(ac2, j, j + 1))
+            PK = fb("pk", 4); act(PK, ac2, F.Identity, bias=1152.0, scale=-0.5)
+            PK5 = fb("pk5", 4); act(PK5, ac2, F.Identity, bias=1152.5, scale=-0.5)
+            vl = fb("vl", 4); tt(vl, VC, PK, A.subtract)
+            G5 = bb("g5", 320); tt(G5, ind(Bw, H20), IN1, A.is_ge)
+            sc = fb("msc", 320); scan(sc, SM, G5, A.mult, A.add)
+            rk = fb("rk", 4); tt(rk, sub(sc, 79, 320, 80), PK, A.add)
+            mm(P("pE", 0, 64), IDB, IOQ, True, False)
+            rk5 = fb("rk5", 4); tt(rk5, sub(sc, 79, 320, 80), PK5, A.add)
+            terms = []
+            for j in range(4):
+                eq = hb("eq%d" % j); ts(eq, IOT, sub(rk, j, j + 1), A.is_equal, sub(vl, j, j + 1), A.mult)
+                if j < NLS:
+                    lt = bb("ls%d" % j); act(lt, IOT, F.Sign, bias=sub(rk5, j, j + 1), scale=-1.0)
+                    terms += [(QH, eq), (QB5, lt)]
+                else:
+                    lt = hb("lt%d" % j); ts(lt, IOT, sub(rk, j, j + 1), A.is_gt, -1.0, A.mult)
+                    terms += [(QH, eq), (QH, lt)]
+            qmm("pE", terms, False)
+            srcU = qwrap("src", "pE", 0.25 - 8 * NLS)
+            n = str((t + 1) & 1)
+            s_, a_, X_ = fb("s" + n), fb("a" + n), bb("x" + n)
+            act(X_, ind(CX, srcU), F.Copy)
+            cp(Qu, ind(CQ, srcU))
+        old = fb("old", 64); act(old, ind(Bw, hU), F.Copy)
+        ok = fb("ok", 64); act(ok, ind(Bw, hU), F.Relu, bias=-2047.0)
+        tv = fb("tv", 64); tt(tv, ok, vm, A.mult)
+        tt(ind(Bw, hU), old, tv, A.add)
+        if t < 2:
+            ox = bb("ox", 64); act(ox, ind(XO, hU), F.Copy)
+            nk = bb("nk", 64); act(nk, ok, F.Identity, bias=1.0, scale=-1.0)
+            xa = bb("xa", 64); tt(xa, ok, RXX, A.mult)
+            xb = bb("xb", 64); tt(xb, nk, ox, A.mult)
+            tt(ind(XO, hU), xa, xb, A.add)
+        if t < 3:
+            s, a, Xa = s_, a_, X_
+            act(s, ind(CS, srcU), F.Copy); act(a, ind(CA, srcU), F.Copy)
+            if QW:
+                qmm("pK", [(QF, s)]); sU = qwrap("s" + n, "pK"); sW = (sub(fb("w_s" + n, 64), 3, 64, 4), SCQ)
+            else:
+                sU = wrap("t" + n, s); sW = (sub(fb("w_t" + n), 15, 256, 16), SCL)
+    for h in range(2):
+        dma("ys"[h], T.y[:, 2048 * h:2048 * h + 2048], T.B[0::16, 2048 * h:2048 * h + 2048], [R("B", 2048 * h, 2048 * h + 2048)], [], 2500)
+    return ops
+
+
+def schedule(ops):
+    n = len(ops)
+    hist = {}
+    pred = [set() for _ in range(n)]
+    for i, o in enumerate(ops):
+        for w, regs in ((False, o["rd"]), (True, o["wr"])):
+            for (nm, lo, hi) in regs:
+                for (j, l2, h2, w2) in hist.get(nm, []):
+                    if j != i and (w or w2) and l2 < hi and lo < h2:
+                        pred[i].add(j)
+        for (nm, lo, hi) in o["wr"]:
+            hist[nm] = [x for x in hist.get(nm, []) if not (lo <= x[1] and x[2] <= hi)] + [(i, lo, hi, True)]
+        for (nm, lo, hi) in o["rd"]:
+            hist.setdefault(nm, []).append((i, lo, hi, False))
+    fake = [[o["ext"][1]] if o["ext"] else [] for o in ops]
+
+    lats = [o["lat"] for o in ops]
+    fwd = [[(j, lats[j]) for j in sorted(pred[i]) + fake[i]] for i in range(n)]
+    bwd = [[] for _ in range(n)]
+    for i in range(n):
+        for j, h in fwd[i]:
+            bwd[j].append((i, h))
+    alts = [[(e, x[1]) for e, x in sorted(o["alt"].items())] if "alt" in o else [(o["eng"], o["dur"])] for o in ops]
+
+    def put(seq, edges, rel, fixed, lean):
+        busy = {e: [] for e in "vspgy"}
+        st = [0.0] * n
+        en = [0.0] * n
+        eng = [None] * n
+        for i in seq:
+            pick = None
+            for e, d in alts[i]:
+                if fixed and fixed[i] != e:
+                    continue
+                t = rel[i]
+                same = 0.0 if e == "p" else HOP_SAME
+                for j, h in edges[i]:
+                    x = en[j] + h + (same if eng[j] == e else HOP)
+                    if x > t:
+                        t = x
+                lst = busy[e]
+                lo = 0
+                hi = len(lst)
+                while lo < hi:
+                    m = (lo + hi) // 2
+                    if lst[m][1] <= t:
+                        lo = m + 1
+                    else:
+                        hi = m
+                while lo < len(lst) and t + d > lst[lo][0]:
+                    t = lst[lo][1]
+                    lo += 1
+                c = t + d + (lean[i] if e == "v" else 0.0)
+                if pick is None or c < pick[0]:
+                    pick = (c, e, t, d, lo)
+            c, e, t, d, lo = pick
+            busy[e].insert(lo, (t, t + d))
+            st[i] = t
+            en[i] = t + d
+            eng[i] = e
+        return st, en, eng
+    zero = [0.0] * n
+    span = lambda en: max(en[i] + lats[i] for i in range(n))
+    seed = [SEED]
+
+    def rnd():
+        seed[0] = (seed[0] * 1103515245 + 12345) % 2147483648
+        return seed[0] / 2147483648.0
+
+    def ordered(key):
+        for i in range(n):
+            for j, h in fwd[i]:
+                if key[j] >= key[i]:
+                    key[i] = key[j] + 0.001
+        return sorted(range(n), key=lambda k: key[k])
+
+    def settle(key, lean):
+        r1 = put(ordered(key), fwd, zero, None, lean)
+        r2 = put(sorted(range(n), key=lambda k: (-r1[1][k], -k)), bwd, lats, r1[2], zero)
+        r3 = put(ordered([-x for x in r2[1]]), fwd, zero, r1[2], zero)
+        return r1 if span(r1[1]) < span(r3[1]) else r3
+
+    def blocks(r):
+        st, en, eng = r
+        last = {}
+        before = {}
+        for i in sorted(range(n), key=lambda k: st[k]):
+            before[i] = last.get(eng[i])
+            last[eng[i]] = i
+        out = []
+        i = max(range(n), key=lambda k: en[k] + lats[k])
+        while True:
+            d = None
+            for j, h in fwd[i]:
+                x = en[j] + h + ((0.0 if eng[i] == "p" else HOP_SAME) if eng[j] == eng[i] else HOP)
+                if d is None or x > d[0]:
+                    d = (x, j)
+            if d is not None and d[0] >= st[i] - 0.01:
+                i = d[1]
+            elif before[i] is not None:
+                out.append((before[i], i))
+                i = before[i]
+            else:
+                return out
+    if "best" not in KEPT:
+        bl = [0.0] * n
+        for i in range(n - 1, -1, -1):
+            bl[i] += ops[i]["dur"] + (0.0 if bwd[i] else lats[i])
+            for j, h in fwd[i]:
+                bl[j] = max(bl[j], bl[i] + h + HOP)
+        flex = [i for i in range(n) if len(alts[i]) > 1]
+        lean = [LEAN] * n
+        best = settle([-x for x in bl], lean)
+        cur = best
+        for it in range(TRIES):
+            lo = rnd() * span(cur[1]) - 2000; hi = lo + 1500 + WIN * rnd(); amp = 100 + AMP * rnd()
+            key = [x + (amp * (rnd() - 0.5) if lo <= x < hi else 0.0) for x in cur[0]]
+            l2 = [(-1e9 if cur[2][i] == "v" else 1e9) for i in range(n)]
+            if rnd() < AIM:
+                if KEPT.get("of") is not cur:
+                    KEPT["of"] = cur
+                    KEPT["blocks"] = blocks(cur)
+                bs = KEPT["blocks"]
+                key = list(cur[0])
+                for x in range(1 + int(2.5 * rnd() ** 2)):
+                    b, i = bs[int(rnd() * len(bs))]
+                    u = rnd()
+                    if u < 0.25 and len(alts[b]) > 1:
+                        l2[b] = -l2[b]
+                    elif u < 0.4 and len(alts[i]) > 1:
+                        l2[i] = -l2[i]
+                    elif u < 0.75:
+                        key[b] = key[i] + 1 + 1500 * rnd() ** 2
+                    else:
+                        d = key[i] - key[b] + 1 + 1500 * rnd() ** 2
+                        todo = [i]
+                        key[i] -= d
+                        while todo:
+                            k = todo.pop()
+                            for j, h in fwd[k]:
+                                if key[j] >= key[k]:
+                                    key[j] = key[k] - 0.001
+                                    todo.append(j)
+            else:
+                for i in flex:
+                    if lo <= cur[0][i] < hi and rnd() < 0.3:
+                        l2[i] = LEAN * (2.5 * rnd() - 0.5)
+            r = settle(key, l2) if it % JUST == 0 else put(ordered(key), fwd, zero, None, l2)
+            if span(r[1]) <= span(cur[1]) + TOL * (1.0 - it / TRIES):
+                cur = r
+                if span(r[1]) < span(best[1]):
+                    best = r
+        KEPT["best"] = best
+    best = KEPT["best"]
+    for i in range(n):
+        if "alt" in ops[i]:
+            ops[i]["eng"] = best[2][i]
+            ops[i]["fn"], ops[i]["dur"] = ops[i]["alt"][best[2][i]]
+    start = best[0]
+    end = [best[1][i] + lats[i] for i in range(n)]
+    order = {}
+    for i in sorted(range(n), key=lambda k: (start[k], k)):
+        order.setdefault(ops[i]["eng"], []).append(i)
+    return pred, order, start, end
+
+
+def rank_program(g, core, T, topo):
+    rank = T.rank_of(core)
+    if rank is None:
+        return
+    ops = build(T, rank)
+    pred, order, start, end = schedule(ops)
+    Q = {"v": g.vector, "s": g.scalar, "p": g.tensor, "g": g, "y": g.sync}
+    CNT = {"v": "cv", "s": "cs", "p": "cp", "g": "cg"}
+    pos = {}
+    for e in order:
+        for x, i in enumerate(order[e]):
+            pos[i] = x
+    need = {}
+    marked = set()
+    for e in order:
+        seen = {}
+        for i in order[e]:
+            w = []
+            best = {}
+            for j in pred[i]:
+                ej = ops[j]["eng"]
+                if ops[j]["kind"] == "d":
+                    if ("d", j) not in seen:
+                        seen[("d", j)] = 1
+                        w.append(j)
+                elif ops[j]["kind"] == "c" and not (ej == "p" and e == "p"):
+                    if pos[j] > seen.get(ej, -1) and pos[j] > pos.get(best.get(ej, -1), -1):
+                        best[ej] = j
+            for ej, j in best.items():
+                seen[ej] = pos[j]
+                w.append(j)
+                marked.add(j)
+            need[i] = w
+    tick = {}
+    total = {}
+    nd = 0
+    for e in order:
+        comp = [i for i in order[e] if ops[i]["kind"] == "c"]
+        if comp:
+            marked.add(comp[-1])
+        c = 0
+        for i in order[e]:
+            if ops[i]["kind"] == "d":
+                tick[i] = ("d%d" % nd, 16)
+                nd += 1
+            elif i in marked:
+                c += 1
+                tick[i] = (CNT[e], c)
+        if comp:
+            total[CNT[e]] = c
+    peers = [p for p in range(len(T.cores)) if p != rank]
+    sent = 0
+    for i in sorted(range(len(ops)), key=lambda k: (start[k], k)):
+        o = ops[i]
+        q = Q[o["eng"]]
+        for j in need[i]:
+            q.wait_ge(T.sem[tick[j][0]], tick[j][1])
+        if o["ext"]:
+            q.wait_ge(T.sem[o["ext"][0]], 2 * len(peers))
+        if o["kind"] == "r":
+            t, sd = o["fn"][1], o["fn"][2]
+            trs = []
+            for x, p in enumerate(peers):
+                dst = T.cores[p]
+                rid, pid, _ = topo.addr(dst)
+                en = topo.engines(core, dst)
+                c = 16 * t + 4 * rank
+                trs.append(RemoteDMATransfer(dst_ids=[DstId(rid=rid, pnc=pid)], dma_engine_mask=(1 << en[2 * x]) | (1 << en[2 * x + 1]),
+                                             remote_sem=T.sem["ar%d" % t], src=T.PF[:, sd["a"] + p:sd["a"] + p + 1], dst=T.RV[:, c:c + 1]))
+            g.remote_dma_fused(trs, local_sem=T.sem.loc)
+            sent += 2 * len(peers)
+        else:
+            ins = o["fn"](g)
+            if o["kind"] == "d":
+                ins.then_inc(T.sem[tick[i][0]], 16)
+            elif i in marked:
+                ins.then_inc(T.sem[tick[i][0]], 1)
+    g.wait_ge(T.sem.loc, sent)
+    for k, c in total.items():
+        g.wait_ge(T.sem[k], c)
+    for i in tick:
+        if ops[i]["kind"] == "d":
+            g.wait_ge(T.sem[tick[i][0]], 16)

@@ -25,13 +25,13 @@ for _b in ("pA", "pZ", "pK", "pS", "pC", "pE", "pW", "pX"):
 NDMA = 24
 SEMAPHORES = ["cv", "cs", "cp", "cg", "loc", "ar0", "ar1", "ar2", "ar3"] + ["d%d" % i for i in range(NDMA)]
 WID = {"float32": 4, "bfloat16": 2, "float16": 2, "int32": 4, "uint16": 2}
-CY = 1.04
-PEC = 0.6
-HOP = 90.0
-HOP_SAME = 60.0
+CY = 0.9
+PEC = 0.46
+HOP = 200.0
+HOP_SAME = 200.0
 GAT = 1.56
 SCA = 3.8
-TRIES = 5000
+TRIES = 7000
 AIM = 0.8
 WIN = 8000
 AMP = 2000

@@ -2,27 +2,27 @@ from concourse.bass import DstId, RemoteDMATransfer
 from concourse.mybir import AluOpType as A, AxisListType, ActivationFunctionType as F
 
 HT = "float16"
-AM = "22222222"
+FUSE = (0, 0)
 NLS = 2
-QW = True
-LATE_A = True
-BIG = 2.0 ** 40
-TW = 4416
+BIG = 2.0 ** 60
+FAR = 2.0 ** 30
+TW = 4480
 MUL = 2.0 ** 30
+KOFF = 38912.0
 
-POOL = {"PF": ("float32", 13312), "PB": ("bfloat16", 18432), "PH": (HT, 6144), "PI": ("int32", 2048), "PU": ("uint16", 4096)}
+POOL = {"PF": ("float32", 11264), "PB": ("bfloat16", 22528), "PH": (HT, 8192), "PI": ("int32", 3072), "PU": ("uint16", 3072)}
 SCRATCH = {k: ("sbuf", [128, v[1]], v[0]) for k, v in POOL.items()}
 SCRATCH.update({
-    "LB": ("sbuf", [128, 2, 8, 16], "int32"), "CV": ("sbuf", [128, 8, 32], "int32"),
-    "X": ("sbuf", [128, 2064], "bfloat16"), "D": ("sbuf", [128, 2064], "int32"), "HM": ("sbuf", [128, 2064], "int32"),
-    "UT": ("sbuf", [128, 4608], "float32"), "B": ("sbuf", [128, TW], "float32"),
+    "LB": ("sbuf", [128, 2, 8, 16], "int32"), "CV": ("sbuf", [128, 8, 32], "int32"), "LN": ("sbuf", [128, 256], "int32"),
+    "X": ("sbuf", [128, 2064], "bfloat16"), "D": ("sbuf", [128, 2064], "int32"), "HM": ("sbuf", [128, 528], "int32"),
+    "UT": ("sbuf", [128, 2064], "float32"), "B": ("sbuf", [128, TW], "float32"),
     "XB0": ("sbuf", [128, TW], "bfloat16"), "XB1": ("sbuf", [128, TW], "bfloat16"),
-    "XE": ("sbuf", [128, 4096], "bfloat16"), "CM": ("sbuf", [128, 4096], "bfloat16"),
+    "XE": ("sbuf", [128, 5120], "bfloat16"), "CM": ("sbuf", [128, 5120], "bfloat16"), "XR": ("sbuf", [128, 4096], "bfloat16"),
     "FC": ("sbuf", [128, 16, 256], "bfloat16"), "RV": ("sbuf", [128, 64], "float32"),
 })
 for _b in ("pA", "pZ", "pK", "pS", "pC", "pE", "pW", "pX"):
     SCRATCH[_b] = ("psum", [128, 512], "float32")
-NDMA = 24
+NDMA = 26
 SEMAPHORES = ["cv", "cs", "cp", "cg", "loc", "ar0", "ar1", "ar2", "ar3"] + ["d%d" % i for i in range(NDMA)]
 WID = {"float32": 4, "bfloat16": 2, "float16": 2, "int32": 4, "uint16": 2}
 CY = 0.9
@@ -31,7 +31,7 @@ HOP = 200.0
 HOP_SAME = 200.0
 GAT = 1.56
 SCA = 3.8
-TRIES = 7000
+TRIES = 12000
 AIM = 0.8
 WIN = 8000
 AMP = 2000
@@ -58,10 +58,11 @@ def build(T, rank):
 
     def buf(pool, key, n):
         if key not in place:
-            place[key] = top[pool]
+            place[key] = (pool, top[pool], n)
             top[pool] += (n + 15) // 16 * 16
             assert top[pool] <= POOL[pool][1], pool
-        return R(pool, place[key], place[key] + n)
+        assert place[key][0] == pool and place[key][2] >= n, key
+        return R(pool, place[key][1], place[key][1] + n)
 
     def sub(r, a, b, st=1):
         return R(r["nm"], r["a"] + a, r["a"] + b, st)
@@ -74,7 +75,7 @@ def build(T, rank):
         writes = []
         for r in rd:
             if isinstance(r, dict):
-                (writes if r["ps"] else reads).append((r["reg"][0], 0, 512) if r["ps"] else r["reg"])
+                (writes if r["ps"] and "share" not in r else reads).append((r["reg"][0], 0, 512) if r["ps"] else r["reg"])
                 if "off" in r:
                     reads.append(r["off"]["reg"])
         for r in wr:
@@ -106,19 +107,29 @@ def build(T, rank):
         else:
             fn = lambda g: g.vector.tensor_scalar(out["ap"], i["ap"], val(s1), val(s2), op0, op1)
         add("v", fn, [i, s1, s2], [out], vcost(out, [i], half(out, i)))
+        form = {(A.mult, None): (s1, 0.0), (A.add, None): (1.0, s1), (A.mult, A.add): (s1, s2)}.get((op0, op1))
+        if form and "off" not in out and i["nm"] not in ("PI", "PU", "RV"):
+            alt = lambda g: g.scalar.activation(out["ap"], i["ap"], F.Identity, bias=val(form[1]), scale=val(form[0]))
+            ops[-1]["alt"] = {"v": (fn, ops[-1]["dur"]), "s": (alt, 20 + vcost(out, [i], 1.0))}
 
     def tt(out, i0, i1, op, more=()):
         add("v", lambda g: g.vector.tensor_tensor(out["ap"], i0["ap"], i1["ap"], op), [i0, i1] + list(more), [out],
             vcost(out, [i0], 1.0 if i0["ps"] or i1["ps"] else 2.0))
 
-    def scan(out, d0, d1, op0, op1):
-        add("v", lambda g: g.vector.tensor_tensor_scan(out["ap"], d0["ap"], d1["ap"], 0.0, op0, op1), [d0, d1], [out],
+    def scan(out, d0, d1, op0, op1, init=0.0):
+        add("v", lambda g: g.vector.tensor_tensor_scan(out["ap"], d0["ap"], d1["ap"], init, op0, op1), [d0, d1], [out],
             vcost(out, [d0], half(out, d0, d1)))
 
     def ms(out, c):
         add("v", lambda g: g.vector.memset(out["ap"], c), [], [out], vcost(out, [out], half(out)))
+        if "ones" in place and out["n"] <= 256 and out["nm"] in ("PF", "PB", "PH", "X", "B", "UT", "XB0", "XB1"):
+            one = buf("PB", "ones", out["n"])
+            alt = lambda g: g.scalar.activation(out["ap"], one["ap"], F.Identity, bias=0.0, scale=c)
+            if one["reg"][:2] != out["reg"][:2]:
+                ops[-1]["rd"].append(one["reg"])
+                ops[-1]["alt"] = {"v": (ops[-1]["fn"], ops[-1]["dur"]), "s": (alt, 20 + vcost(out, [out], 1.0))}
 
-    def act(out, i, func, bias=None, scale=None, acc=None, more=()):
+    def act(out, i, func, bias=None, scale=None, acc=None, more=(), unit=False):
         kw = {}
         if bias is not None:
             kw["bias"] = val(bias)
@@ -138,15 +149,16 @@ def build(T, rank):
             fn = lambda g: g.vector.tensor_scalar(o, x, 1.0 if scale is None else val(scale), val(bias), A.mult, A.add)
         elif func == F.Relu and scale is None:
             fn = lambda g: g.vector.tensor_scalar(o, x, val(bias), 0.0, A.add, A.max)
-        elif func == F.Relu and bias is None:
-            fn = lambda g: g.vector.tensor_scalar(o, x, scale, 0.0, A.mult, A.max)
-        elif func == F.Relu:
-            fn = lambda g: g.vector.tensor_scalar(o, x, BIG, None, A.is_lt)
+        elif func == F.Sign and unit:
+            fn = lambda g: g.vector.tensor_scalar(o, x, -1.0, 1.0, A.max, A.min)
         if fn:
             ops[-1]["alt"] = {"s": (ops[-1]["fn"], ops[-1]["dur"]), "v": (fn, vcost(out, [i], half(out, i)))}
 
-    def gat(eng, out, i):
+    def mv(out, i):
         act(out, i, F.Copy)
+
+    def lin(out, i, scale, bias):
+        act(out, i, F.Identity, bias=bias, scale=scale)
 
     def mm(out, l, r, start, stop, join=False):
         add("p", lambda g: g.tensor.matmul(out["ap"], l["ap"], r["ap"], start, stop), [l, r], [out],
@@ -163,8 +175,8 @@ def build(T, rank):
             fn = lambda g: g.iota(out["ap"], pat, base, cm)
         add("g", fn, [], [out], 130 + 2 * out["n"] * CY)
 
-    def asel(out, i, pat, op, base, cm):
-        add("g", lambda g: g.affine_select(out["ap"], i["ap"], pat, op, 0.0, base, cm), [i], [out], 170 + 2 * out["n"] * CY)
+    def asel(out, i, pat, op, base, cm, fill=0.0):
+        add("g", lambda g: g.affine_select(out["ap"], i["ap"], pat, op, fill, base, cm), [i], [out], 170 + 2 * out["n"] * CY)
 
     def dma(q, out, i, rd, wr, lat):
         if q == "y":
@@ -184,42 +196,42 @@ def build(T, rank):
     XBw = [R("XB0", 0, TW), R("XB1", 0, TW)]
     Xw = R("X", 0, 2064)
     Dw = R("D", 0, 2064)
-    UTs = R("UT", 0, 2064)
-    UTw = R("UT", 0, TW)
+    UTw = R("UT", 0, 2064)
 
     for h in range(2):
         dma("ys"[h], T.LB[:, h], T.board[h::2, :], [], [RX("LB", None, 128 * h, 128 * h + 128, 128)], 2200)
-    dma("y", T.X[:, 0:2048], T.xs[:], [], [R("X", 0, 2048)], 4500)
+    dma("y", T.LN[:], T.board[:], [], [R("LN", 0, 256)], 2600)
+    dma("y", T.X[:, 0:2048], T.xs[:], [], [R("X", 0, 2048)], 4800)
     dma("y", T.D[:, 0:2048], T.ds[:], [], [R("D", 0, 2048)], 8000)
     for i in range(16):
-        dma("y", T.HM[i::16, 0:512], T.hm[:, 512 * rank:512 * rank + 512], [], [RX("HM", None, 3000 + i, 3001 + i, 1)], 9000)
-    hw = 2064 - 512 * rank
-    HMw = R("HM", 0, hw)
+        dma("y", T.HM[i::16, 16:528], T.hm[:, 512 * rank:512 * rank + 512], [], [RX("HM", None, 3000 + i, 3001 + i, 1)], 9000)
+    HMw = R("HM", 0, 528)
     HMall = RX("HM", None, 3000, 3016, 1)
 
     ONES = bb("ones"); ms(ONES, 1.0)
     O128 = sub(ONES, 0, 128)
     IOT = bb("iot"); iota(IOT, [[1, 256]], 0, 0)
     PI_ = ib("pi", 1); iota(PI_, [[0, 1]], 0, 1, False)
-    J = fb("J", 320); iota(J, [[0, 20], [1, 16]], 0, 0)
-    J4 = fb("J4", 64); iota(J4, [[0, 16], [1, 4]], 0, 0)
-    tb = bb("tb", 128); BLK = bb("blk", 128); TRI = bb("tri", 128); TRU = bb("tru", 128)
+    J = bb("J"); iota(J, [[0, 16], [1, 16]], 0, 0)
+    J4 = bb("J4", 64); iota(J4, [[0, 16], [1, 4]], 0, 0)
+    tb = bb("tb", 128); BLK = bb("blk", 128); TRI = bb("tri", 128)
     ROW15 = bb("row15", 128); IDB = bb("idb", 128)
     gp = [[-16, 8], [0, 16]]
     asel(tb, O128, gp, A.is_ge, 0, 1)
     asel(BLK, tb, [[16, 8], [0, 16]], A.is_ge, 15, -1)
     asel(TRI, BLK, [[1, 128]], A.is_ge, 0, -1)
-    asel(TRU, BLK, [[-1, 128]], A.is_gt, 0, 1)
     asel(ROW15, O128, gp, A.is_equal, -15, 1)
     asel(IDB, O128, [[-1, 128]], A.is_equal, 0, 1)
-    RM = bb("rm", 2048)
-    for j in range(8):
-        asel(sub(RM, 256 * j, 256 * j + 256), ONES, [[-1, 16], [0, 16]], A.is_equal, -16 * j, 1)
-    JP = fb("jp", 64); iota(JP, [[1, 16], [0, 4]], 0, 0)
+    OH = hb("oh", 512); ms(OH, 1.0)
+    ROWS = hb("rows", 2048)
+    for b in range(4):
+        asel(sub(ROWS, 512 * b, 512 * b + 512), OH, [[-1, 4], [-16, 8], [0, 16]], A.is_equal, -4 * b, 1)
+    JM = bb("jm", 512); iota(JM, [[1, 32], [0, 16]], 0, 0)
+    JP = bb("jp", 64); iota(JP, [[1, 16], [0, 4]], 0, 0)
     DUMP = fb("dump", 64); iota(DUMP, [[1, 64]], 4352, 0)
-    iota(R("HM", 512, 2064), [[0, 1552]], 1 << 20, 0, False)
-    for k in range(4):
-        iota(R("UT", 1104 * k, 1104 * k + 1104), [[1, 1104]], 1104 * k, 0)
+    for k in range(2):
+        iota(R("UT", 1024 * k, 1024 * k + 1024), [[8192, 1024]], 8192 * 1024 * k, 0)
+    ms(R("UT", 2048, 2064), 2048.0 * 8192)
     RI = ib("ri", 1); ts(RI, PI_, 15, A.bitwise_and)
     RF = fb("rf", 1); cp(RF, RI)
     i2 = ib("i2", 1); ts(i2, RI, 2, A.arith_shift_right)
@@ -231,12 +243,11 @@ def build(T, rank):
         sc = fb(key + "sc", 1); ts(sc, col, last - 0.5, A.is_gt, 1.0 / MUL, A.max)
         x = bb(key + "x", n); y = bb(key + "y", n); o = bb(key, n)
         ts(x, jt, col, A.not_equal); ts(y, jt, c1, A.is_equal, MUL, A.mult); tt(o, x, y, A.max)
-        return o, sc
-    SP, SCL = picker("sp", L(J), RF, 15, 256)
-    SQ, SCQ = picker("sq", J4, RQ4, 3, 64)
-    SCQ16 = fb("scq16", 1); ts(SCQ16, SCQ, 1.0 / 16, A.mult)
-    ISC = fb("isc", 1); ts(ISC, RF, 14.5, A.is_lt, MUL, A.mult); ts(ISC, ISC, 1.0, A.max)
-    MH = fb("mh"); ts(MH, IOT, 0.5, A.add, ISC, A.mult)
+        return o, sc, x
+    SP, SCL, NOT16 = picker("sp", J, RF, 15, 256)
+    SQ, SCQ, NOT4 = picker("sq", J4, RQ4, 3, 64)
+    SCL8 = fb("scl8", 1); ts(SCL8, SCL, 1.0 / 8192, A.mult)
+    JH = hb("jh"); ts(JH, IOT, 0.5, A.add)
     C256 = bb("c256"); ms(C256, 256.0)
     CBIG = bb("cbig"); ms(CBIG, BIG)
     CE = fb("ce"); ms(CE, 2048.0)
@@ -248,64 +259,87 @@ def build(T, rank):
         y = buf(pool, key, 132); ms(y, 0.0)
         ts(sub(y, 3, 131, 4), sub(src, 3, 128, 4), c, A.mult)
         return [sub(y, 3 - r, 131 - r) for r in range(4)]
-    Q8n = quad("q8n", BLK, -8.0, "PB"); QH = quad("qhh", BLK, 1.0, "PH"); Q15 = quad("q15", ROW15, 1.0, "PH")
-    QF = quad("qf", ROW15, 1.0, "PF")
-    NB = scaled("nb", BLK, -16384.0); B4n = scaled("b4n", BLK, -4096.0)
+
+    def comb(key, src, pool):
+        y = buf(pool, key, 144); ms(y, 0.0); cp(sub(y, 15, 143, 16), sub(src, 0, 128, 16))
+        return [sub(y, 15 - k, 143 - k) for k in range(16)]
+
+    def rows(key, src):
+        y = bb(key, 2048)
+        for k in range(16):
+            asel(sub(y, 128 * k, 128 * k + 128), src, gp, A.is_equal, -k, 1)
+        return [sub(y, 128 * k, 128 * k + 128) for k in range(16)]
+    ROW0, ROW1 = sub(ROWS, 0, 128), sub(ROWS, 128, 256)
+    Q1 = quad("q1", BLK, 1.0, "PB"); Q16 = quad("q16", BLK, 16.0, "PB"); Q256 = quad("q256", BLK, 256.0, "PB")
+    Q15 = quad("q15", ROW15, 1.0, "PB"); QF = quad("qf", ROW15, 1.0, "PF")
+    QH = quad("qhh", BLK, 1.0, "PH"); Q0 = quad("q0", ROW0, 1.0, "PH")
+    QH5 = quad("qh5", BLK, 0.5, "PH"); QB5 = quad("qb5", BLK, 0.5, "PB")
+    ZK = comb("z", BLK, "PB"); Z15 = comb("z15", ROW15, "PB"); ZH = comb("zh", BLK, "PH")
+    B16 = scaled("b16", BLK, 16.0); B256 = scaled("b256", BLK, 256.0); B2 = scaled("b2", BLK, 2.0)
+    NB = scaled("nb", BLK, -65536.0); BF = scaled("bf", BLK, -16384.0); BP = scaled("bp", BLK, 16384.0)
+    IDN = scaled("idn", IDB, -1.0)
     BLKh = scaled("bh", BLK, 1.0, "PH"); IDH = scaled("idh", IDB, 1.0, "PH")
-    ID8K = scaled("id8k", IDB, 8192.0, "PF")
-    I16 = scaled("i16", IDB, 16.0); I16n = scaled("i16n", IDB, -16384.0); I4n = scaled("i4n", IDB, -4096.0)
-    zt = scaled("zt", TRI, -4096.0); zi = scaled("zi", IDB, 8192.0); ZM = bb("zm", 128); tt(ZM, zt, zi, A.add)
-    ZC = fb("zc", 1); ts(ZC, RF, 1.0, A.add, -4096.0, A.mult)
-    tri2 = bb("tri2", 128); tt(tri2, TRI, IDB, A.subtract); TRS = scaled("trs", tri2, -16384.0)
-    Z = bb("z", 144); ms(Z, 0.0); cp(sub(Z, 15, 143, 16), sub(BLK, 0, 128, 16))
-    ZK = [sub(Z, 15 - k, 143 - k) for k in range(16)]
-    MD = bb("md"); ts(MD, L(J), RF, A.not_equal, 2.0 ** 23, A.mult); ts(MD, MD, 32768.0, A.max)
+    zt = scaled("zt", TRI, -16384.0); zi = scaled("zi", IDB, 32768.0); ZM = bb("zm", 128); tt(ZM, zt, zi, A.add)
+    ZC = fb("zc", 1); ts(ZC, RF, 1.0, A.add, -16384.0, A.mult)
+    tri2 = bb("tri2", 128); tt(tri2, TRI, IDB, A.subtract); TRS = scaled("trs", tri2, -65536.0)
+    r1n = scaled("r1n", ROW1, -2.0, "PH"); R01 = hb("r01", 128); tt(R01, r1n, ROW0, A.add)
+    S0 = fb("s0m", 128); ms(S0, 0.0); cp(sub(S0, 0, 128, 16), sub(ROW15, 0, 128, 16))
+    c0 = fb("c0", 1); ts(c0, RF, 0.5, A.is_lt, -2048.0, A.mult)
+    SC0 = fb("sc0", 1); ts(SC0, c0, -262144.0, A.add)
+    lk = bb("lk", 128); ts(lk, TRS, 0.5, A.mult); lk2 = bb("lk2", 128); tt(lk2, lk, zi, A.add)
+    LK = rows("LK", lk2)
+    LT = rows("LT", scaled("lt", TRI, -1.0 / BIG))
+    THR = fb("thr", 1); ts(THR, RF, 4.0, A.min, -512.0 * 8192, A.mult); ts(THR, THR, 4096.0, A.add)
+    up = bb("up", 128); ms(up, 32768.0); dn = bb("dn", 128); ms(dn, -32768.0)
+    BI1 = bb("bi1", 128); asel(BI1, up, [[-16, 8], [0, 4], [-1, 4]], A.is_equal, 0, 1)
+    BI2 = bb("bi2", 128); asel(BI2, dn, [[-16, 8], [0, 4], [-1, 4]], A.is_equal, -1, 1)
+    AB = bb("ab", 128); asel(AB, dn, gp, A.is_equal, -4, 1)
+    MD = bb("md"); ts(MD, NOT16, -FAR, A.mult, 8192.0, A.add)
+    MN = bb("mn", 64); ts(MN, sub(NOT16, 0, 64), -FAR, A.mult)
+    MQ = bb("mq", 64); ts(MQ, NOT4, -FAR, A.mult, 262144.0, A.add)
+    MK = fb("mk", 64); ts(MK, sub(NOT16, 0, 64), -4097.0, A.mult, 4096.0, A.add)
+    DR = bb("dr"); ms(DR, FAR); ms(sub(DR, 0, 256, 16), -2 * FAR)
+    DQ = bb("dq", 64); ms(DQ, FAR); ms(sub(DQ, 0, 64, 4), -2 * FAR)
+    DZ = fb("dz"); ms(DZ, FAR)
+    j16 = fb("j16", 4); ts(j16, sub(J, 0, 4), 16.0, A.mult, RF, A.add)
+    DY = fb("dy", 64); ms(DY, FAR); ts(sub(DY, 0, 64, 16), j16, -1.0 / 8192, A.mult, 2048.0 - 4416.0 / 8192, A.add)
+    VC = fb("vc", 4); ts(VC, j16, 2.0, A.mult, 256.0, A.add)
+    if NLS:
+        ts(sub(VC, 0, NLS), sub(VC, 0, NLS), 1.0, A.add)
+    IO2 = bb("io2"); ts(IO2, IOT, 2.0, A.mult, -256.0, A.add)
+    f3 = fb("f3", 1); cp(f3, i3)
+    IOQ = bb("ioq", 64); ts(IOQ, sub(IOT, 0, 64), 4.0, A.mult, f3, A.add)
     MP = fb("mp", 64); ts(MP, JP, RF, A.is_equal)
     f2 = fb("f2", 1); ts(f2, i2, -2.0, A.mult, -1.0, A.add)
     SLB = fb("slb", 4); ts(SLB, sub(J, 0, 4), -8.0, A.mult, f2, A.add)
-    QB = quad("qb", BLK, 1.0, "PB"); QB5 = quad("qb5", BLK, 0.5, "PB")
-    B128n = scaled("b128n", BLK, -128.0); B16h = scaled("b16h", BLK, 16.0, "PH"); R15h = scaled("r15h", ROW15, 1.0, "PH")
-    EQ = fb("eq16", 16); ts(EQ, sub(J, 0, 16), RF, A.is_equal)
-    ROWS = bb("rows", 2048)
-    for r in range(16):
-        act(sub(ROWS, 128 * r, 128 * r + 128), BLK, F.Identity, bias=0.0, scale=sub(EQ, r, r + 1))
-    S01 = fb("s01", 128); ms(S01, 0.0); cp(sub(S01, 1, 128, 16), sub(ROW15, 0, 128, 16))
-    SHI = bb("shi", 128); ms(SHI, 0.0); cp(sub(SHI, 0, 128, 16), sub(ROW15, 0, 128, 16))
-    ts(sub(SHI, 1, 128, 16), sub(ROW15, 0, 128, 16), -1.0, A.mult)
-    CEN = fb("cen", 1); ts(CEN, i3, -512.0, A.mult, -255.5, A.add)
-    j16 = fb("j16", 4); ts(j16, sub(J, 0, 4), 16.0, A.mult, RF, A.add)
-    VC = fb("vc", 4); ts(VC, j16, 1280.0, A.add)
-    f3 = fb("f3", 1); cp(f3, i3)
-    IOQ = bb("ioq", 64); ts(IOQ, sub(IOT, 0, 64), 4.0, A.mult, f3, A.add)
-    SM = bb("sm", 320); ms(SM, 1.0); ms(sub(SM, 0, 320, 80), 0.0); ms(sub(SM, 16, 320, 80), -1024.0)
-    IN1 = fb("in1", 320)
+    PF_ = fb("pff", 1); cp(PF_, PI_)
+    RM = bb("rm", 2048)
+    PM = fb("pm", 4); ts(PM, sub(J, 0, 4), -32.0, A.mult, PF_, A.add)
     for j in range(4):
-        ts(sub(IN1, 80 * j, 80 * j + 16), sub(J, 0, 16), RF, A.not_equal, 2048.0, A.add)
-    IOU = ub("iou")
-    if "1" in AM:
-        cp(IOU, IOT)
-    Fb = bb("fb", 272); ms(sub(Fb, 0, 16), 0.0)
+        ts(sub(RM, 512 * j, 512 * j + 512), JM, sub(PM, j, j + 1), A.is_equal)
+    ES = bb("es", 272); ms(sub(ES, 0, 16), 0.0)
     T3 = bb("t3", 272); ms(sub(T3, 256, 272), 512.0)
-    SC = fb("sc", 272); ms(sub(SC, 256, 272), 1e13)
-    PAY = fb("pay", 272); ms(sub(PAY, 256, 272), 2048.0 * 8192 + 2048)
-    ms(R("X", 2048, 2064), BIG); ms(R("X", 2048, 2049), -BIG); ms(R("D", 2048, 2064), 0)
-    ms(R("B", 4096, 4352), 2048.0); ms(R("B", 4352, TW), 0.0)
-    ms(R("XB0", 4096, TW), BIG); ms(R("XB1", 4096, TW), BIG)
-    CN = {c: c for c in (-8.5, -8.0, -65536.0, -4095.0, -2047.0, 0.5, 128.0)}
+    SC = bb("sc", 32); ms(sub(SC, 16, 32), 512.0)
+    PAY = fb("pay", 272); ms(sub(PAY, 256, 272), 2048.0 - 8192.0)
+    ms(R("X", 2048, 2064), BIG); ms(R("D", 2048, 2064), 0); ms(R("HM", 0, 16), 1 << 20)
+    act(R("B", 4096, 4352), CE, F.Silu); ops[-1].pop("alt"); ops[-1]["dur"] += 1400
+    ms(R("B", 4352, TW), 0.0)
+    for x in ("XB0", "XB1"):
+        ms(R(x, 4096, 4288), BIG); ms(R(x, 4288, TW), BIG)
 
-    def wrap(key, src, n=256, plus=0.25):
+    def wrap(key, src, n, scale):
         s = fb("w_" + key, n); scan(s, sub(SP, 0, n), src, A.mult, A.add)
-        u = ub("u_" + key, n // 16); ts(u, sub(s, 15, n, 16), SCL, A.mult, plus, A.add)
+        u = ub("u_" + key, n // 16); lin(u, sub(s, 15, n, 16), scale, 0.25)
         return u
 
-    def qmm(bank, terms, first=True):
+    def qmm(bank, terms, first=True, last=True):
         for x, (l, r) in enumerate(terms):
             for k in range(4):
-                mm(P(bank, 0, 64), l[k], sub(r, k, 256, 4), first and x == 0 and k == 0, x == len(terms) - 1 and k == 3, k > 0)
+                mm(P(bank, 0, 64), l[k], sub(r, k, 256, 4), first and x == 0 and k == 0, last and x == len(terms) - 1 and k == 3, k > 0)
 
-    def qwrap(key, bank, plus=0.25, scale=None):
+    def qwrap(key, bank, plus=0.25):
         s = fb("w_" + key, 64); scan(s, SQ, P(bank, 0, 64), A.mult, A.add)
-        u = ub("u_" + key, 16); ts(u, sub(s, 3, 64, 4), scale or SCQ, A.mult, plus, A.add)
+        u = ub("u_" + key, 16); lin(u, sub(s, 3, 64, 4), SCQ, plus)
         return u
 
     WI = ib("wi")
@@ -315,165 +349,165 @@ def build(T, rank):
         o = sub(WI, b, 256, 8); i = RX("CV", T.CV[:, b, :], 0, 256, 32)
         o["reg"] = ("PI", WI["a"] + 32 * b, WI["a"] + 32 * b + 32)
         add("v", lambda g, o=o, i=i: g.vector.transpose(o["ap"], i["ap"]), [i], [o], 90.0)
-    WH = bb("wh"); cp(WH, WI)
-    WL = bb("wl"); tt(WL, WI, WH, A.subtract)
-    for r in range(16):
-        o = P(("pA", "pZ", "pK", "pC")[r % 4]); l = sub(ROWS, 128 * r, 128 * r + 128)
-        mm(o, l, WH, True, False); mm(o, l, WL, False, True)
-        d = R("B", r, 4096, 16); d["reg"] = ("B", 256 * r, 256 * r + 256)
-        act(d, o, F.Copy)
+    WH = hb("wh"); mv(WH, R("LN", 0, 256))
+    for r in range(8):
+        bank = ("pA", "pZ", "pK", "pC")[r % 4]
+        for h in range(2):
+            mm(P(bank, 256 * h, 256 * h + 256), sub(ROWS, 256 * r + 128 * h, 256 * r + 128 * h + 128), WH, True, True, h > 0)
+        mv(R("B", 512 * r, 512 * r + 512), P(bank, 0, 512))
     w1 = ib("w1"); ts(w1, WI, 2049, A.bitwise_and)
-    Fm = sub(Fb, 16, 272)
-    ts(Fm, w1, 0.0, A.is_equal)
-    OO = [ub("o0"), ub("o1")]
+    Fm = bb("fm"); ts(Fm, w1, 0.0, A.is_equal)
     for e in (1, 0):
-        u = fb("oa"); ts(u, w1, float(e), A.not_equal, 4096.0, A.mult)
-        v = fb("oc"); tt(v, u, WI, A.add)
-        ts(OO[e], v, 2049.0, A.min)
+        u = fb("oa%d" % e); ts(u, w1, float(e), A.not_equal, 2048.0, A.mult)
+        v = fb("oc%d" % e); tt(v, u, WI, A.max)
+        oo = ub("o%d" % e); mv(oo, v)
+        for c in range(16):
+            mv(R("XB%d" % e, 256 * c, 256 * c + 256), ind(Xw, sub(oo, 16 * c, 16 * c + 16)))
 
-    def table(name, win, off, engs):
-        n = len(engs); w = 256 // n
-        for c in range(n):
-            gat(engs[c], R(name, 16 * w * c, 16 * w * (c + 1)), ind(win, sub(off, w * c, w * (c + 1))))
-    table("XB1", Xw, OO[1], "ssssssssssssssss")
-    table("XB0", Xw, OO[0], "ssssssssssssssss")
+    def tiles(t):
+        n = str(t & 1)
+        return fb("cs" + n, 320), fb("ca" + n, 320), bb("cx" + n, 320), ib("cq" + n, 320), ub("qu" + n, 320)
 
-    CS = fb("cs", 320); CA = fb("ca", 320); CQ = fb("cq", 320); CX = bb("cx", 320)
+    def targets(q2, qu, off, at, n, key):
+        q = ib("qa" + key, n); tt(q, ind(Dw, off), at, A.add)
+        ts(q2, q, 4095, A.bitwise_and)
+        mv(qu, q2)
 
-    def select(b1, b2, b3, b4):
-        mm(P("pW"), TRI, Fm, True, False); mm(P("pW"), TRU, sub(Fb, 15, 271), False, True)
-        scan(L(T3), P("pW"), C256, A.add, A.min)
-        mm(P("pW", 256, 512), ROW15, L(T3), True, True)
-        s1 = fb("s1", 16); scan(s1, sub(SP, 0, 16), R("pW", 271, 512, 16), A.mult, A.add)
-        c1 = bb("c1"); act(c1, MH, F.Sign, bias=sub(s1, 15, 16), scale=-1.0)
-        scan(L(SC), SP, P("pW", 256, 512), A.mult, A.add)
-        qmm(b1, [(Q8n, c1)])
-        u1 = qwrap("l1", b1, 143.25)
-        q1 = bb("q1", 64); act(q1, P(b1, 0, 64), F.Identity, bias=CN[128.0])
-        iv = hb("iv"); ts(iv, IOT, sub(s1, 15, 16), A.subtract, 0.0, A.max)
-        c2 = hb("c2"); tt(c2, ind(SC, u1), MH, A.is_le)
-        mm(P(b2, 0, 64), IDB, q1, True, False); qmm(b2, [(QH, c2)], False)
-        u2 = qwrap("l2", b2)
-        q2 = bb("q2", 64); act(q2, P(b2, 0, 64), F.Copy)
-        c3 = hb("c3"); tt(c3, ind(T3, u2), IOT, A.is_le)
-        mm(P(b3, 0, 64), I16, q2, True, False); qmm(b3, [(Q15, iv), (QH, c3)], False)
-        u = qwrap("l3", b3)
-        o = P(b4)
-        mm(o, B128n, c1, True, False); mm(o, R15h, iv, False, False); mm(o, B16h, c2, False, False); mm(o, BLKh, c3, False, True)
-        act(L(CS), o, F.Identity, bias=2048.0)
+    def select(t):
+        CS, CA, CX, CQ, QU = tiles(t)
+        E = sub(ES, 16, 272)
+        scan(E, P("pW"), C256, A.add, A.min)
+        mm(P("pE", 0, 16), IDB, sub(MN, 0, 16), True, False); mm(P("pE", 0, 16), ROW15, sub(E, 15, 256, 16), False, True)
+        s1 = fb("s1", 1)
+        add("v", lambda g: g.vector.tensor_reduce(s1["ap"], P("pE", 0, 16)["ap"], AxisListType.X, A.max), [P("pE", 0, 16)], [s1], 80.0)
+        for k in range(16):
+            mm(P("pX", 0, 16), Z15[k], sub(E, k, 256, 16), k == 0, k == 15, k % 8 > 0)
+        mv(sub(SC, 0, 16), P("pX", 0, 16))
+        mm(P("pW"), IDB, E, True, False); mm(P("pW"), IDN, sub(ES, 15, 271), False, False, True)
+        mm(P("pW"), ROW15, sub(ES, 15, 271), False, True, True)
+        mv(L(T3), P("pW"))
+        c1 = bb("c1"); ts(c1, JH, s1, A.is_ge)
+        qmm("pE", [(Q1, c1)])
+        u1 = qwrap("l1", "pE")
+        iv = bb("iv"); ts(iv, IOT, s1, A.subtract, 0.0, A.max)
+        qmm("pX", [(Q16, c1)], True, False)
+        c2 = bb("c2"); tt(c2, ind(SC, u1), JH, A.is_le)
+        qmm("pX", [(Q1, c2)], False)
+        u2 = qwrap("l2", "pX")
+        qmm("pE", [(Q256, c1), (Q15, iv), (Q16, c2)], True, False)
+        o = P("pW")
+        mm(o, B256, c1, True, False); mm(o, ROW15, iv, False, False); mm(o, B16, c2, False, False)
+        c3 = bb("c3"); tt(c3, ind(T3, u2), JH, A.is_le)
+        qmm("pE", [(Q1, c3)], False)
+        u = qwrap("l3%d" % (t & 1), "pE")
+        mm(o, BLK, c3, False, True)
+        mv(L(CS), o)
+        lin(L(CA), ind(Bw, u), 8192.0, 0.0)
+        au = wrap("a", L(CA), 256, SCL8)
+        targets(L(CQ), L(QU), au, L(CS), 256, "l")
+        mv(L(CX), ind(XBw[t & 1], u) if t else ind(Xw, au))
         return u
 
-    def targets(out, off, at, n, key):
-        q = ib("qa" + key, n); tt(q, ind(Dw, off), at, A.add)
-        q2 = ib("qb" + key, n); ts(q2, q, 4095, A.bitwise_and)
-        cp(out, q2)
-
-    def cand(u, out, t):
-        gat("s" if t else "v", L(CA), ind(Bw, u))
-        if t and QW:
-            qmm("pW", [(QF, L(CA))]); au = qwrap("a", "pW")
-        else:
-            au = wrap("a0", L(CA))
-        targets(out, au, L(CS), 256, "l")
-        act(L(CX), ind(Xw, au), F.Copy)
-
-    def first(cut, key):
-        sg = bb("good"); act(sg, P("pA"), F.Sign, bias=CN[cut])
-        mm(P("pZ"), ZM, sg, False, True); mm(P("pS"), B4n, sg, False, True)
-        mx = hb("mx"); ts(mx, P("pZ"), ZC, A.add, -2048.0, A.max)
-        s2 = bb("s2"); act(s2, P("pS"), F.Relu, bias=-65536.0)
-        qmm("pK", [(QH, mx), (QB, s2)])
-        u = qwrap(key, "pK", 32768.25)
-        wf = fb("wf", 16); cp(wf, u)
-        o = P("pZ", 256, 512)
-        mm(o, BLKh, mx, True, False); mm(o, BLK, s2, False, True)
-        ru = ub("ru"); ts(ru, o, 32768.0, A.add)
-        r = None
-        if key == "at":
-            r = fb(key); act(r, o, F.Identity, bias=32768.0)
-        mm(P("pC"), BLKh, mx, r is None, False); mm(P("pC"), BLK, s2, False, False)
-        return r, u, wf, ru
-
-    def fallback(x):
-        hi = bb("hi"); act(hi, x, F.Relu, bias=-16.0)
-        mm(P("pS"), S01, x, True, False); mm(P("pS"), SHI, hi, False, False)
-
-    def preload(qu):
-        qh = hb("qh"); ts(qh, qu, -2048.0, A.add)
-        mm(P("pZ"), IDH, qh, True, False)
-
-    def rivals(ru, wf, other, key, plus):
+    def rivals(key, wf, c2, start):
+        mm(P("pC"), IDH, key, False, False)
         for c in range(16):
             n = 256 - 16 * c
-            ts(RX("FC", T.FC[:, c, 0:n], 256 * c, 256 * c + n, n), sub(ru, 16 * c, 256), sub(wf, c, c + 1), A.is_equal)
+            o = RX("FC", T.FC[:, c, 0:n], 256 * c, 256 * c + n, n)
+            if c2 is None:
+                ts(o, sub(key, 16 * c, 256), wf(c), A.is_equal)
+            else:
+                ts(o, sub(key, 16 * c, 256), wf(c), A.subtract, c2, A.is_equal)
             if c < 15:
                 mm(P("pC", 16 * c + 16, 256), NB, RX("FC", T.FC[:, c, 16:n], 256 * c + 16, 256 * c + n, n - 16), False, False)
             if c in (11, 15):
                 a = 0 if c == 11 else 12
                 mm(P("pC", 16 * a, 16 * c + 16), TRS, RX("FC", T.FC[:, a:c + 1, 0:16], 256 * a, 256 * c + 16, 16 * (c + 1 - a)), False, c == 15)
-        s = fb("w_" + key); scan(s, SP, P("pC"), A.mult, A.add)
-        x = fb("rx", 16); ts(x, sub(s, 15, 256, 16), SCL, A.mult, plus, A.add)
-        y = ib("ry", 16); tt(y, x, other, A.max)
-        z = ib("rz" + key, 16); ts(z, y, 8191, A.bitwise_and)
-        u = ub("u_" + key, 16); cp(u, z)
-        return z, u
+        s = fb("w_riv"); scan(s, start, P("pC"), A.min, A.max, FAR)
+        return sub(s, 15, 256, 16)
 
-    Qu = ub("qu")
-    sU = select("pE", "pX", "pS", "pE")
-    sW = (sub(fb("w_l3", 64), 3, 64, 4), SCQ)
-    cand(sU, Qu, 0)
-    s, a, Xa = L(CS), L(CA), L(CX)
+    mm(P("pW"), TRI, Fm, True, True)
+    sU = select(0)
+    srcU = None
     for t in range(4):
         e = t & 1
         XE_, XO = XBw[e], XBw[1 - e]
-        XT = bb("xt")
-        for h in range(2):
-            if "2" in AM[4 * h:4 * h + 4]:
-                mm(P("pW", 128 * h, 128 * h + 128), sub(Xa, 128 * h, 128 * h + 128), IDB, True, True)
-                act(sub(XT, 128 * h, 128 * h + 128), P("pW", 128 * h, 128 * h + 128), F.Copy)
+        CS, CA, CX, CQ, QU = tiles(t)
+        nc = 320 if t else 256
+        fuse = FUSE[min(t, 1)]
+        qh = hb("qh")
         if t == 0:
-            s0, a0, x0 = fb("s0"), fb("a0"), bb("x0")
-            act(s0, s, F.Copy); act(a0, a, F.Copy); act(x0, Xa, F.Copy)
-            s, a, Xa = s0, a0, x0
-        preload(Qu)
-        fallback(s)
-        for c in range(8):
-            xe = R("XE", 512 * c, 512 * c + 512); bank = P(("pE", "pX", "pW")[c % 3], 0, 512)
-            if AM[c] == "1":
-                act(xe, ind(Xa, sub(IOU, 32 * c, 32 * c + 32)), F.Copy)
-                tt(R("CM", 512 * c, 512 * c + 512), ind(XO, sub(Qu, 32 * c, 32 * c + 32)), xe, A.is_lt)
+            s, a, Xa = L(CS), L(CA), L(CX)
+            ts(qh, L(QU), -2048.0, A.add)
+            ts(sub(DZ, 0, 256, 16), sU, -1.0, A.mult, KOFF, A.add)
+        else:
+            s, a, Xa = fb("s"), fb("a"), bb("x")
+            mv(s, ind(CS, srcU)); mv(a, ind(CA, srcU)); mv(Xa, ind(CX, srcU)); lin(qh, ind(CQ, srcU), 1.0, -2048.0)
+            qmm("pW", [(QF, s)]); sU = qwrap("s", "pW")
+            ts(sub(DZ, 0, 256, 16), sU, -1.0, A.mult, KOFF, A.add)
+        GE = bb("ge"); act(GE, a, F.Sign, bias=THR)
+        for k in range(16 if fuse else 0):
+            cp(dict(R("XR", k, 16 * fuse, 16), reg=("XR", k, k + 1)), sub(CX, 0, fuse))
+        XT = bb("xt", 384)
+        blocks = [(0, 0), (128, 128), (256, 192)]
+        for h, (lo, at0) in enumerate(blocks):
+            if fuse < lo + 128 and lo < nc:
+                bank = P(("pE", "pX")[h % 2], 0, 128)
+                mm(bank, sub(CX, at0, at0 + 128), IDB, True, True)
+                mv(sub(XT, 128 * h, 128 * h + 128), bank)
+        nch = nc // 32
+        for c in list(range(fuse // 32, nch)) + list(range(fuse // 32)):
+            cm = R("CM", 512 * c, 512 * c + 512); src = ind(XO, sub(QU, 32 * c, 32 * c + 32))
+            if 32 * c < fuse:
+                tt(cm, src, dict(R("XR", 512 * c, 512 * c + 512), reg=("XR", 0, 16)), A.is_lt)
             else:
-                act(xe, ind(XO, sub(Qu, 32 * c, 32 * c + 32)), F.Copy)
-                mm(bank, sub(XT, 128 * (c // 4), 128 * (c // 4) + 128), sub(RM, 512 * (c % 4), 512 * (c % 4) + 512), True, True)
-                tt(R("CM", 512 * c, 512 * c + 512), xe, bank, A.is_lt)
+                xe = R("XE", 512 * c, 512 * c + 512); bank = P(("pE", "pX")[c % 2], 0, 512)
+                h = c // 4; j = (32 * c - blocks[h][1]) // 32
+                mv(xe, src)
+                mm(bank, sub(XT, 128 * h, 128 * h + 128), sub(RM, 512 * j, 512 * j + 512), True, True)
+                tt(cm, xe, bank, A.is_lt)
             if c % 2:
                 cm = R("CM", 512 * c - 512, 512 * c + 512)
                 for k in range(16):
                     mm(P("pA", 32 * c - 32, 32 * c + 32), ZK[k], sub(cm, k, 1024, 16), k == 0, k == 15, k % 8 > 0)
-        ivf = bb("ivf"); act(ivf, s, F.Relu, bias=CN[-4095.0])
-        dd = fb("dd"); act(dd, a, F.Abs, bias=CEN)
-        sF = fb("sF", 16); act(sF, sW[0], F.Identity, bias=0.25, scale=sW[1])
-        ds = bb("dsg"); act(ds, dd, F.Sign, bias=-256.0)
-        mm(P("pC"), IDB, MD, True, False); mm(P("pC"), I16n, ivf, False, False)
-        at, atU, wf, ru = first(-8.5, "at")
-        ncs = bb("ncs"); act(ncs, P("pS"), F.Sign, bias=-63000.0)
-        who = hb("who"); cp(who, ind(Bw, atU))
-        qmm("pX", [(QH, who)]); whoU = qwrap("who", "pX", 0.25, SCQ16)
-        Wu = ub("wu"); targets(Wu, whoU, at, 256, "w")
-        preload(Wu)
-        baseI, baseU = rivals(ru, wf, sF, "base", 8192.25)
-        E = bb("e"); act(E, P("pC"), F.Relu, scale=-1.0 / 16384)
-        base = fb("base"); act(base, ind(UTw, baseU), F.Copy)
-        fallback(base)
-        mm(P("pE"), I4n, ds, True, False); mm(P("pE"), I4n, ncs, False, False); mm(P("pE"), NB, E, False, True)
-        fl = bb("fl"); act(fl, P("pE"), F.Sign, bias=-4096.0)
-        mm(P("pX", 256, 512), ID8K, a, True, False); mm(P("pX", 256, 512), IDH, who, False, True)
-        act(L(PAY), P("pX", 256, 512), F.Copy)
+        mm(P("pZ"), IDH, qh, True, False)
+        mm(P("pS"), S0, s, True, False)
+        mm(P("pK", 0, 64), IDB, MQ, True, False)
+        mm(P("pC"), IDB, MD, True, False); mm(P("pC"), AB, GE, False, False)
+        sg = bb("sg", 320); act(sub(sg, 0, nc), P("pA", 0, nc), F.Sign, bias=-8.5)
+        if t:
+            sm = bb("sgm"); mv(sm, ind(sg, srcU))
+        else:
+            sm = L(sg)
+        mm(P("pZ"), ZM, sm, False, True); mm(P("pS"), BF, sm, False, True)
+        mx = hb("mx"); ts(mx, P("pZ"), ZC, A.add, -16384.0, A.max)
+        s2 = hb("s2"); ts(s2, P("pS"), SC0, A.add, -16384.0, A.max)
+        qmm("pK", [(QH, mx), (Q0, s2)], False)
+        mm(P("pS"), BLKh, mx, True, False); mm(P("pS"), R01, s2, False, True)
+        wa = fb("wa", 64); scan(wa, DQ, P("pK", 0, 64), A.min, A.max)
+        atU = ub("atU", 16); lin(atU, sub(wa, 3, 64, 4), 1.0, 2048.0)
+        key = hb("key"); lin(key, P("pS"), 1.0, 229376.0)
+        at = fb("at"); lin(at, P("pS"), 1.0, 264192.0)
+        who = hb("who"); mv(who, ind(Bw, atU))
+        qmm("pK", [(Q0, who)]); whoU = qwrap("who", "pK")
+        Wu = ub("wu"); targets(ib("qw"), Wu, whoU, at, 256, "w")
+        qw = hb("qwh"); ts(qw, Wu, -2048.0, A.add)
+        mm(P("pZ"), IDH, qw, True, False)
+        x = rivals(key, lambda c: sub(wa, 4 * c + 3, 4 * c + 4), None, DZ)
+        baseU = ub("baseU", 16); act(baseU, x, F.Abs, bias=-KOFF)
+        EN = bb("en"); act(EN, P("pC"), F.Sign, unit=True)
+        if t < 3:
+            cp(ind(XO, baseU), CBIG)
+        basen = fb("basen", 16); ts(basen, baseU, -1.0, A.mult, KOFF, A.add)
+        mm(P("pC"), IDB, MD, True, False); mm(P("pC"), AB, GE, False, False)
+        o = P("pA")
+        mm(o, BI1, GE, True, False); mm(o, BI2, GE, False, False); mm(o, IDH, key, False, False); mm(o, BP, EN, False, True)
+        fl = bb("fl"); act(fl, o, F.Sign, bias=3000.0 + 14 * 16384.0 - 65536.0)
+        tt(L(PAY), ind(Bw, baseU), a, A.add)
         pf = bb("pf"); scan(pf, fl, ONES, A.add, A.add)
-        acc = fb("acc", 4); junk = bb("junk")
+        acc = fb("acc", 4)
         for j in range(4):
-            act(junk, pf, F.Sign, bias=sub(SLB, j, j + 1), acc=sub(acc, j, j + 1))
-        ix = ub("ix", 4); ts(ix, acc, -0.5, A.mult, 128.25, A.add)
+            act(bb("junk%d" % j), pf, F.Sign, bias=sub(SLB, j, j + 1), acc=sub(acc, j, j + 1))
+        ix = ub("ix", 4); lin(ix, acc, -0.5, 128.25)
         G = fb("g", 64); SD = fb("sd%d" % t, 4); jf = fb("jf", 64)
         tt(G, ind(PAY, ix), MP, A.mult)
         for p in range(4):
@@ -482,95 +516,80 @@ def build(T, rank):
                 more=[R("RV", 16 * t + 4 * p, 16 * t + 4 * p + 1), sub(SD, p, p + 1)])
         snd = add("g", ("send", t, SD), [SD], [], 300.0, 4500.0, "r")
         for c in range(8):
-            cm = R("CM", 512 * c, 512 * c + 512); src = ind(Bw, sub(Wu, 32 * c, 32 * c + 32))
-            act(cm, src, F.Relu, bias=-2047.0)
+            act(R("CM", 512 * c, 512 * c + 512), ind(Bw, sub(Wu, 32 * c, 32 * c + 32)), F.Relu, bias=-2047.0)
+        mm(P("pZ"), BP, EN, False, False)
         for c in range(4):
             cm = R("CM", 1024 * c, 1024 * c + 1024)
             for k in range(16):
-                mm(P("pA", 64 * c, 64 * c + 64), ZK[k], sub(cm, k, 1024, 16), k == 0, False, k % 8 > 0)
-            mm(P("pA", 64 * c, 64 * c + 64), NB, sub(E, 64 * c, 64 * c + 64), False, True)
+                mm(P("pZ", 64 * c, 64 * c + 64), LK[k], sub(cm, k, 1024, 16), False, c == 3 and k == 15, k % 8 > 0)
         for u in (sU, baseU):
             act(ind(Bw, u), CE, F.Silu)
         if t < 3:
-            cp(ind(XE_, sU), CBIG)
-            cp(ind(XO, baseU), CBIG)
+            mm(P("pW"), TRI, ONES, True, False)
             for k in range(16):
-                mm(P("pW"), ZK[k], R(XO["nm"], k, 4096, 16), k == 0, k == 15, k % 2 > 0)
-            act(Fm, P("pW"), F.Relu, bias=1.0, scale=-1.0 / BIG)
-            lU = select("pW", "pW", "pW", "pX")
-            if not LATE_A:
-                cand(lU, L(CQ), 1)
-        k2, k2U, wf, ru = first(-8.0, "k2")
-        endI, endU = rivals(ru, wf, baseI, "end", 40960.25)
-        cp(ind(Bw, endU), a)
+                mm(P("pW"), LT[k], R(XO["nm"], k, 4096, 16), False, k == 15, k % 2 > 0)
+            select(t + 1)
+            cp(ind(XE_, sU), CBIG)
+        m2 = hb("m2"); ts(m2, P("pZ"), 14 * 16384.0 - 32768.0, A.add, -16384.0, A.max)
+        mm(P("pS"), BLKh, m2, True, True)
+        for k in range(16):
+            mm(P("pK", 0, 16), ZH[k], sub(m2, k, 256, 16), k == 0, k == 15, k % 8 > 0)
+        k2 = hb("k2"); lin(k2, P("pS"), 1.0, 245760.0)
+        x = rivals(k2, lambda c: dict(P("pK", c, c + 1), share=1), 245760.0, DR)
+        y = fb("ey", 16); tt(y, x, basen, A.max)
+        endU = ub("endU", 16); act(endU, y, F.Abs, bias=-KOFF)
         if t < 3:
-            if LATE_A:
-                cand(lU, L(CQ), 1)
             cp(ind(XE_, endU), Xa)
+        ts(ind(Bw, endU), a, 1.0 / 8192, A.mult, 0.0, A.add)
+        CS, CA, CX, CQ, QU = tiles(t + 1)
         raU = ub("raU", 4); rv = R("RV", 16 * t, 16 * t + 16, 4)
-        add("v", lambda g, o=raU, i=rv: g.vector.tensor_scalar(o["ap"], i["ap"], 1.0 / 8192, 0.1 - 512.0 * rank, A.mult, A.add),
+        add("v", lambda g, o=raU, i=rv: g.vector.tensor_scalar(o["ap"], i["ap"], 1.0 / 8192, 16.1 - 512.0 * rank, A.mult, A.add),
             [rv], [raU], 90.0, ext=("ar%d" % t, snd))
         pi = ib("rpi", 4); add("v", lambda g, o=pi, i=rv: g.vector.tensor_copy(o["ap"], i["ap"]), [rv, raU], [pi], 90.0)
         rvv = ib("rvv", 4); ts(rvv, pi, 8191, A.bitwise_and)
-        rvU = ub("rvU", 4); cp(rvU, rvv)
-        RS, RA, RQ, RXX = sub(CS, 256, 320), sub(CA, 256, 320), sub(CQ, 256, 320), sub(CX, 256, 320)
+        rvU = ub("rvU", 4); mv(rvU, rvv)
+        RS, RA = sub(CS, 256, 320), sub(CA, 256, 320)
         tt(RS, ind(HMw, raU), DUMP, A.min, [HMall])
-        hU = wrap("h", RS, 64)
-        act(RA, ind(UTs, rvU), F.Copy)
-        vm = fb("vm", 64); act(vm, RA, F.Identity, bias=-2048.0)
+        hU = wrap("h", RS, 64, SCL)
+        mv(RA, ind(UTw, rvU))
+        hc = fb("hc", 64); lin(hc, RS, -1.0 / 8192, 2048.0)
+        hm_ = fb("hmk", 64); tt(hm_, hc, MK, A.min)
         if t < 3:
-            act(RXX, ind(Xw, rvU), F.Copy)
-            targets(RQ, rvU, RS, 64, "r")
-            hF = fb("hF", 4); act(hF, sub(fb("w_h", 64), 15, 64, 16), F.Identity, bias=-0.25, scale=SCL)
-            H20 = ub("h20", 20)
-            cp(sub(H20, 0, 20, 5), hU)
+            mv(sub(CX, 256, 320), ind(Xw, rvU))
+            targets(sub(CQ, 256, 320), sub(QU, 256, 320), rvU, RS, 64, "r")
+        hy = fb("hy", 64); tt(hy, ind(Bw, hU), hm_, A.min)
+        hv = fb("hv", 64); scan(hv, DY, hy, A.min, A.max, FAR)
+        hkU = ub("hkU", 4); lin(hkU, sub(hv, 15, 64, 16), -8192.0, 2.0 ** 24)
+        ts(ind(Bw, hkU), RA, 1.0 / 8192, A.mult, 0.0, A.add)
+        if t < 2:
+            cp(ind(XO, hkU), sub(CX, 256, 320))
+        if t < 3:
+            hk = fb("hk", 4); lin(hk, sub(hv, 15, 64, 16), -8192.0, 2.0 ** 24)
+            hf = fb("hf", 4); lin(hf, sub(fb("w_h", 64), 15, 64, 16), SCL, -0.25)
+            ac2 = fb("ac2", 4)
             for j in range(4):
-                cp(sub(H20, 5 * j + 1, 5 * j + 5), hU)
-                ts(sub(IN1, 80 * j + 16, 80 * j + 80), RS, sub(hF, j, j + 1), A.is_ge, 2048.0, A.add)
-            hb_ = fb("hb", 4); act(hb_, hF, F.Identity, bias=0.25, scale=-1.0)
-            ac2 = fb("ac2", 4); jk2 = bb("jk2")
+                act(bb("junk%d" % j), L(CS), F.Sign, bias=sub(hf, j, j + 1), scale=-1.0, acc=sub(ac2, j, j + 1))
+            bad = fb("bad", 4); ts(bad, sub(hv, 15, 64, 16), 2048.0 - 4415.0 / 8192, A.is_lt, 1024.0, A.mult)
+            ac3 = fb("ac3", 4); tt(ac3, ac2, bad, A.add)
+            mm(P("pW", 0, 64), IDB, MN, True, False)
             for j in range(4):
-                act(jk2, L(CS), F.Sign, bias=sub(hb_, j, j + 1), acc=sub(ac2, j, j + 1))
-            PK = fb("pk", 4); act(PK, ac2, F.Identity, bias=1152.0, scale=-0.5)
-            PK5 = fb("pk5", 4); act(PK5, ac2, F.Identity, bias=1152.5, scale=-0.5)
-            vl = fb("vl", 4); tt(vl, VC, PK, A.subtract)
-            G5 = bb("g5", 320); tt(G5, ind(Bw, H20), IN1, A.is_ge)
-            sc = fb("msc", 320); scan(sc, SM, G5, A.mult, A.add)
-            rk = fb("rk", 4); tt(rk, sub(sc, 79, 320, 80), PK, A.add)
-            mm(P("pE", 0, 64), IDB, IOQ, True, False)
-            rk5 = fb("rk5", 4); tt(rk5, sub(sc, 79, 320, 80), PK5, A.add)
+                m = bb("mj%d" % j, 64); ts(m, RS, sub(hk, j, j + 1), A.is_gt)
+                mm(P("pW", 0, 64), B2, m, False, j == 3)
+            nw = fb("nw", 64); scan(nw, sub(DR, 0, 64), P("pW", 0, 64), A.min, A.max)
+            rk = fb("rk", 4); tt(rk, sub(nw, 15, 64, 16), ac3, A.add)
+            vl = fb("vl", 4); tt(vl, VC, ac2, A.subtract)
+            mm(P("pW", 0, 64), IDB, IOQ, True, False)
             terms = []
             for j in range(4):
-                eq = hb("eq%d" % j); ts(eq, IOT, sub(rk, j, j + 1), A.is_equal, sub(vl, j, j + 1), A.mult)
+                eq = hb("eq%d" % j); ts(eq, IO2, sub(rk, j, j + 1), A.is_equal, sub(vl, j, j + 1), A.mult)
                 if j < NLS:
-                    lt = bb("ls%d" % j); act(lt, IOT, F.Sign, bias=sub(rk5, j, j + 1), scale=-1.0)
-                    terms += [(QH, eq), (QB5, lt)]
+                    lt = bb("ls%d" % j); act(lt, IO2, F.Sign, bias=sub(rk, j, j + 1), scale=-1.0)
+                    terms += [(QH5, eq), (QB5, lt)]
                 else:
-                    lt = hb("lt%d" % j); ts(lt, IOT, sub(rk, j, j + 1), A.is_gt, -1.0, A.mult)
-                    terms += [(QH, eq), (QH, lt)]
-            qmm("pE", terms, False)
-            srcU = qwrap("src", "pE", 0.25 - 8 * NLS)
-            n = str((t + 1) & 1)
-            s_, a_, X_ = fb("s" + n), fb("a" + n), bb("x" + n)
-            act(X_, ind(CX, srcU), F.Copy)
-            cp(Qu, ind(CQ, srcU))
-        old = fb("old", 64); act(old, ind(Bw, hU), F.Copy)
-        ok = fb("ok", 64); act(ok, ind(Bw, hU), F.Relu, bias=-2047.0)
-        tv = fb("tv", 64); tt(tv, ok, vm, A.mult)
-        tt(ind(Bw, hU), old, tv, A.add)
-        if t < 2:
-            ox = bb("ox", 64); act(ox, ind(XO, hU), F.Copy)
-            nk = bb("nk", 64); act(nk, ok, F.Identity, bias=1.0, scale=-1.0)
-            xa = bb("xa", 64); tt(xa, ok, RXX, A.mult)
-            xb = bb("xb", 64); tt(xb, nk, ox, A.mult)
-            tt(ind(XO, hU), xa, xb, A.add)
-        if t < 3:
-            s, a, Xa = s_, a_, X_
-            act(s, ind(CS, srcU), F.Copy); act(a, ind(CA, srcU), F.Copy)
-            if QW:
-                qmm("pK", [(QF, s)]); sU = qwrap("s" + n, "pK"); sW = (sub(fb("w_s" + n, 64), 3, 64, 4), SCQ)
-            else:
-                sU = wrap("t" + n, s); sW = (sub(fb("w_t" + n), 15, 256, 16), SCL)
+                    lt = hb("lt%d" % j); ts(lt, IO2, sub(rk, j, j + 1), A.is_gt, -2.0, A.mult)
+                    terms += [(QH5, eq), (QH5, lt)]
+            qmm("pW", terms, False)
+            srcU = qwrap("src", "pW", 0.25 - 8 * NLS)
     for h in range(2):
         dma("ys"[h], T.y[:, 2048 * h:2048 * h + 2048], T.B[0::16, 2048 * h:2048 * h + 2048], [R("B", 2048 * h, 2048 * h + 2048)], [], 2500)
     return ops
@@ -593,7 +612,16 @@ def schedule(ops):
     fake = [[o["ext"][1]] if o["ext"] else [] for o in ops]
 
     lats = [o["lat"] for o in ops]
-    fwd = [[(j, lats[j]) for j in sorted(pred[i]) + fake[i]] for i in range(n)]
+    anc = [0] * n
+    fwd = []
+    for i in range(n):
+        far = 0
+        for j in pred[i]:
+            far |= anc[j]
+        fwd.append([(j, lats[j]) for j in sorted(pred[i]) + fake[i] if lats[j] or not far >> j & 1])
+        for j in pred[i]:
+            far |= 1 << j
+        anc[i] = far
     bwd = [[] for _ in range(n)]
     for i in range(n):
         for j, h in fwd[i]:

@@ -2,15 +2,24 @@ from concourse.bass import DstId, RemoteDMATransfer
 from concourse.mybir import AluOpType as A, AxisListType, ActivationFunctionType as F
 
 HT = "float16"
-FUSE = (0, 0)
-NLS = 2
+MODES = ("UUUU", "SSFFS")
+LAY = ((), ((128, 256),))
+MCH = (32,) * 8
+SPL = (((0, 16),), ((0, 16),))
+PARTS = (((0, 256),),) * 4
+CUT = 0
+LAST = True
+DIRECT = ""
+RMG = True
+XBW = (32, 32)
+NLS = 0
 BIG = 2.0 ** 60
 FAR = 2.0 ** 30
 TW = 4480
 MUL = 2.0 ** 30
 KOFF = 38912.0
 
-POOL = {"PF": ("float32", 11264), "PB": ("bfloat16", 22528), "PH": (HT, 8192), "PI": ("int32", 3072), "PU": ("uint16", 3072)}
+POOL = {"PF": ("float32", 11264), "PB": ("bfloat16", 22528), "PH": (HT, 9216), "PI": ("int32", 4096), "PU": ("uint16", 3072)}
 SCRATCH = {k: ("sbuf", [128, v[1]], v[0]) for k, v in POOL.items()}
 SCRATCH.update({
     "LB": ("sbuf", [128, 2, 8, 16], "int32"), "CV": ("sbuf", [128, 8, 32], "int32"), "LN": ("sbuf", [128, 256], "int32"),
@@ -25,24 +34,39 @@ for _b in ("pA", "pZ", "pK", "pS", "pC", "pE", "pW", "pX"):
 NDMA = 26
 SEMAPHORES = ["cv", "cs", "cp", "cg", "loc", "ar0", "ar1", "ar2", "ar3"] + ["d%d" % i for i in range(NDMA)]
 WID = {"float32": 4, "bfloat16": 2, "float16": 2, "int32": 4, "uint16": 2}
-CY = 0.9
-PEC = 0.46
+COSTS = ((1.0, 0.51, 1.56, 3.8, 210.0), (1.2, 0.61, 1.95, 5.2, 220.0), (0.9, 0.46, 1.35, 3.0, 200.0))
 HOP = 200.0
 HOP_SAME = 200.0
-GAT = 1.56
-SCA = 3.8
-TRIES = 12000
+AGAIN = 2
+SWEEPS = 5
+PANE = 14000.0
+FLIGHT = 3800.0
+TRIES = 2000
+MOVES = 500
+POLISH = 2000
 AIM = 0.8
+RUN = 0.25
 WIN = 8000
 AMP = 2000
-JUST = 10
-TOL = 40.0
-LEAN = 2500.0
+JUST = 4
+TOL = 80.0
+HEAT = 150.0
+SOFT = 0.005
+BACK = 3000.0
+LEAN = 1500.0
 SEED = 1
 KEPT = {}
 
 
 def build(T, rank):
+    runs = [record(T, rank, c) for c in COSTS]
+    for x in zip(*runs):
+        x[0]["times"] = [{e: a[1] for e, a in o["alt"].items()} if "alt" in o else {o["eng"]: o["dur"]} for o in x]
+    return runs[0]
+
+
+def record(T, rank, cost):
+    CY, PEC, GAT, SCA = cost[:4]
     ops = []
     place = {}
     top = {k: 0 for k in POOL}
@@ -128,6 +152,9 @@ def build(T, rank):
             if one["reg"][:2] != out["reg"][:2]:
                 ops[-1]["rd"].append(one["reg"])
                 ops[-1]["alt"] = {"v": (ops[-1]["fn"], ops[-1]["dur"]), "s": (alt, 20 + vcost(out, [out], 1.0))}
+        if abs(c) < 2 ** 24 and out["nm"] != "PH":
+            alt = lambda g: g.iota(out["ap"], [[0, out["n"]]], int(c), 0, allow_small_or_imprecise_dtypes=True)
+            ops[-1]["alt"] = dict(ops[-1].get("alt", {"v": (ops[-1]["fn"], ops[-1]["dur"])}), g=(alt, 130 + 2 * out["n"] * CY))
 
     def act(out, i, func, bias=None, scale=None, acc=None, more=(), unit=False):
         kw = {}
@@ -226,8 +253,6 @@ def build(T, rank):
     ROWS = hb("rows", 2048)
     for b in range(4):
         asel(sub(ROWS, 512 * b, 512 * b + 512), OH, [[-1, 4], [-16, 8], [0, 16]], A.is_equal, -4 * b, 1)
-    JM = bb("jm", 512); iota(JM, [[1, 32], [0, 16]], 0, 0)
-    JP = bb("jp", 64); iota(JP, [[1, 16], [0, 4]], 0, 0)
     DUMP = fb("dump", 64); iota(DUMP, [[1, 64]], 4352, 0)
     for k in range(2):
         iota(R("UT", 1024 * k, 1024 * k + 1024), [[8192, 1024]], 8192 * 1024 * k, 0)
@@ -247,6 +272,7 @@ def build(T, rank):
     SP, SCL, NOT16 = picker("sp", J, RF, 15, 256)
     SQ, SCQ, NOT4 = picker("sq", J4, RQ4, 3, 64)
     SCL8 = fb("scl8", 1); ts(SCL8, SCL, 1.0 / 8192, A.mult)
+    SCN = fb("scn", 1); ts(SCN, SCL, -1.0, A.mult)
     JH = hb("jh"); ts(JH, IOT, 0.5, A.add)
     C256 = bb("c256"); ms(C256, 256.0)
     CBIG = bb("cbig"); ms(CBIG, BIG)
@@ -265,30 +291,32 @@ def build(T, rank):
         return [sub(y, 15 - k, 143 - k) for k in range(16)]
 
     def rows(key, src):
-        y = bb(key, 2048)
-        for k in range(16):
-            asel(sub(y, 128 * k, 128 * k + 128), src, gp, A.is_equal, -k, 1)
+        y = bb(key, 2048); x = bb(key + "4", 512)
+        for k in range(4):
+            src(sub(x, 128 * k, 128 * k + 128))
+        for b in range(4):
+            asel(sub(y, 512 * b, 512 * b + 512), x, [[-1, 4], [-16, 8], [0, 16]], A.is_equal, -4 * b, 1)
         return [sub(y, 128 * k, 128 * k + 128) for k in range(16)]
     ROW0, ROW1 = sub(ROWS, 0, 128), sub(ROWS, 128, 256)
     Q1 = quad("q1", BLK, 1.0, "PB"); Q16 = quad("q16", BLK, 16.0, "PB"); Q256 = quad("q256", BLK, 256.0, "PB")
-    Q15 = quad("q15", ROW15, 1.0, "PB"); QF = quad("qf", ROW15, 1.0, "PF")
-    QH = quad("qhh", BLK, 1.0, "PH"); Q0 = quad("q0", ROW0, 1.0, "PH")
-    QH5 = quad("qh5", BLK, 0.5, "PH"); QB5 = quad("qb5", BLK, 0.5, "PB")
+    Q15 = quad("q15", ROW15, 1.0, "PB")
+    if "S" in MODES[0] + MODES[1]:
+        BH5 = scaled("bh5", BLK, 0.5); ZK5 = comb("zk5", BH5, "PB")
+    QH = quad("qhh", BLK, 1.0, "PH"); Q0 = quad("q0", ROW0, 1.0, "PH") if "w" not in DIRECT else None
+    QH5 = quad("qh5", BLK, 0.5, "PH"); QB5 = quad("qb5", BLK, 0.5, "PB") if NLS else None
     ZK = comb("z", BLK, "PB"); Z15 = comb("z15", ROW15, "PB"); ZH = comb("zh", BLK, "PH")
-    B16 = scaled("b16", BLK, 16.0); B256 = scaled("b256", BLK, 256.0); B2 = scaled("b2", BLK, 2.0)
-    NB = scaled("nb", BLK, -65536.0); BF = scaled("bf", BLK, -16384.0); BP = scaled("bp", BLK, 16384.0)
+    B16 = scaled("b16", BLK, 16.0); B256 = scaled("b256", BLK, 256.0)
+    NB = scaled("nb", BLK, -65536.0); BP = scaled("bp", BLK, 16384.0)
     IDN = scaled("idn", IDB, -1.0)
     BLKh = scaled("bh", BLK, 1.0, "PH"); IDH = scaled("idh", IDB, 1.0, "PH")
-    zt = scaled("zt", TRI, -16384.0); zi = scaled("zi", IDB, 32768.0); ZM = bb("zm", 128); tt(ZM, zt, zi, A.add)
+    ZM = bb("zm", 128); asel(ZM, scaled("zt", TRI, -16384.0), [[-1, 128]], A.not_equal, 0, 1, 16384.0)
     ZC = fb("zc", 1); ts(ZC, RF, 1.0, A.add, -16384.0, A.mult)
-    tri2 = bb("tri2", 128); tt(tri2, TRI, IDB, A.subtract); TRS = scaled("trs", tri2, -65536.0)
-    r1n = scaled("r1n", ROW1, -2.0, "PH"); R01 = hb("r01", 128); tt(R01, r1n, ROW0, A.add)
-    S0 = fb("s0m", 128); ms(S0, 0.0); cp(sub(S0, 0, 128, 16), sub(ROW15, 0, 128, 16))
-    c0 = fb("c0", 1); ts(c0, RF, 0.5, A.is_lt, -2048.0, A.mult)
-    SC0 = fb("sc0", 1); ts(SC0, c0, -262144.0, A.add)
-    lk = bb("lk", 128); ts(lk, TRS, 0.5, A.mult); lk2 = bb("lk2", 128); tt(lk2, lk, zi, A.add)
-    LK = rows("LK", lk2)
-    LT = rows("LT", scaled("lt", TRI, -1.0 / BIG))
+    ZD = fb("zd", 1); ts(ZD, RF, -16384.0, A.mult)
+    TRS = bb("trs", 128); asel(TRS, NB, [[1, 128]], A.is_gt, 0, -1)
+    BK = scaled("bk", BLK, 16000.0); IDF = scaled("idf", IDB, 1.0, "PF")
+    IDM = scaled("idm", IDB, -1.0, "PF"); IDL = scaled("idl", IDB, -2.0 ** 23, "PF")
+    LK = rows("LK", lambda o: ts(o, ZM, 2.0, A.mult))
+    LT = rows("LT", lambda o: ts(o, TRI, -1.0 / BIG, A.mult))
     THR = fb("thr", 1); ts(THR, RF, 4.0, A.min, -512.0 * 8192, A.mult); ts(THR, THR, 4096.0, A.add)
     up = bb("up", 128); ms(up, 32768.0); dn = bb("dn", 128); ms(dn, -32768.0)
     BI1 = bb("bi1", 128); asel(BI1, up, [[-16, 8], [0, 4], [-1, 4]], A.is_equal, 0, 1)
@@ -296,27 +324,33 @@ def build(T, rank):
     AB = bb("ab", 128); asel(AB, dn, gp, A.is_equal, -4, 1)
     MD = bb("md"); ts(MD, NOT16, -FAR, A.mult, 8192.0, A.add)
     MN = bb("mn", 64); ts(MN, sub(NOT16, 0, 64), -FAR, A.mult)
-    MQ = bb("mq", 64); ts(MQ, NOT4, -FAR, A.mult, 262144.0, A.add)
+    MQ = bb("mq", 64); ts(MQ, NOT4, -FAR, A.mult, 286720.0, A.add)
     MK = fb("mk", 64); ts(MK, sub(NOT16, 0, 64), -4097.0, A.mult, 4096.0, A.add)
     DR = bb("dr"); ms(DR, FAR); ms(sub(DR, 0, 256, 16), -2 * FAR)
-    DQ = bb("dq", 64); ms(DQ, FAR); ms(sub(DQ, 0, 64, 4), -2 * FAR)
+    DQ = fb("dq", 64); ms(DQ, FAR)
     DZ = fb("dz"); ms(DZ, FAR)
     j16 = fb("j16", 4); ts(j16, sub(J, 0, 4), 16.0, A.mult, RF, A.add)
     DY = fb("dy", 64); ms(DY, FAR); ts(sub(DY, 0, 64, 16), j16, -1.0 / 8192, A.mult, 2048.0 - 4416.0 / 8192, A.add)
     VC = fb("vc", 4); ts(VC, j16, 2.0, A.mult, 256.0, A.add)
     if NLS:
         ts(sub(VC, 0, NLS), sub(VC, 0, NLS), 1.0, A.add)
-    IO2 = bb("io2"); ts(IO2, IOT, 2.0, A.mult, -256.0, A.add)
+    IO2 = hb("io2"); ts(IO2, IOT, 2.0, A.mult, -319.0, A.add)
     f3 = fb("f3", 1); cp(f3, i3)
     IOQ = bb("ioq", 64); ts(IOQ, sub(IOT, 0, 64), 4.0, A.mult, f3, A.add)
-    MP = fb("mp", 64); ts(MP, JP, RF, A.is_equal)
-    f2 = fb("f2", 1); ts(f2, i2, -2.0, A.mult, -1.0, A.add)
-    SLB = fb("slb", 4); ts(SLB, sub(J, 0, 4), -8.0, A.mult, f2, A.add)
-    PF_ = fb("pff", 1); cp(PF_, PI_)
+    MP = fb("mp", 64); ts(MP, sub(NOT16, 0, 64), -1.0, A.mult, 1.0, A.add)
+    DS = bb("dsum", 64); ts(DS, sub(J, 0, 64), 1.0, A.min)
+    SLB = fb("slb", 1); ts(SLB, RF, -2.0, A.mult, -1.0, A.add)
     RM = bb("rm", 2048)
-    PM = fb("pm", 4); ts(PM, sub(J, 0, 4), -32.0, A.mult, PF_, A.add)
-    for j in range(4):
-        ts(sub(RM, 512 * j, 512 * j + 512), JM, sub(PM, j, j + 1), A.is_equal)
+    if RMG:
+        OB = bb("ob", 512); ms(OB, 1.0)
+        for j in range(4):
+            asel(sub(RM, 512 * j, 512 * j + 512), OB, [[-1, 32], [0, 16]], A.is_equal, -32 * j, 1)
+    else:
+        JM = bb("jm", 512); iota(JM, [[1, 32], [0, 16]], 0, 0)
+        PF_ = fb("pff", 1); cp(PF_, PI_)
+        PM = fb("pm", 4); ts(PM, sub(J, 0, 4), -32.0, A.mult, PF_, A.add)
+        for j in range(4):
+            ts(sub(RM, 512 * j, 512 * j + 512), JM, sub(PM, j, j + 1), A.is_equal)
     ES = bb("es", 272); ms(sub(ES, 0, 16), 0.0)
     T3 = bb("t3", 272); ms(sub(T3, 256, 272), 512.0)
     SC = bb("sc", 32); ms(sub(SC, 16, 32), 512.0)
@@ -332,10 +366,14 @@ def build(T, rank):
         u = ub("u_" + key, n // 16); lin(u, sub(s, 15, n, 16), scale, 0.25)
         return u
 
-    def qmm(bank, terms, first=True, last=True):
+    def qmm(bank, terms, first=True, last=True, lo=0, hi=256):
         for x, (l, r) in enumerate(terms):
             for k in range(4):
-                mm(P(bank, 0, 64), l[k], sub(r, k, 256, 4), first and x == 0 and k == 0, last and x == len(terms) - 1 and k == 3, k > 0)
+                mm(P(bank, lo // 4, hi // 4), l[k], sub(r, lo + k, hi, 4), first and x == 0 and k == 0, last and x == len(terms) - 1 and k == 3, k > 0)
+
+    def zmm(bank, l, r, lo=0, hi=256):
+        for k in range(16):
+            mm(P(bank, lo // 16, hi // 16), l[k], sub(r, lo + k, hi, 16), k == 0, k == 15, k % 8 > 0)
 
     def qwrap(key, bank, plus=0.25):
         s = fb("w_" + key, 64); scan(s, SQ, P(bank, 0, 64), A.mult, A.add)
@@ -358,11 +396,12 @@ def build(T, rank):
     w1 = ib("w1"); ts(w1, WI, 2049, A.bitwise_and)
     Fm = bb("fm"); ts(Fm, w1, 0.0, A.is_equal)
     for e in (1, 0):
-        u = fb("oa%d" % e); ts(u, w1, float(e), A.not_equal, 2048.0, A.mult)
-        v = fb("oc%d" % e); tt(v, u, WI, A.max)
-        oo = ub("o%d" % e); mv(oo, v)
-        for c in range(16):
-            mv(R("XB%d" % e, 256 * c, 256 * c + 256), ind(Xw, sub(oo, 16 * c, 16 * c + 16)))
+        u = ib("oa%d" % e); lin(u, WI, 4097.0, 4096.0 * e)
+        v = ib("oc%d" % e); ts(v, u, 8191, A.bitwise_and)
+        oo = ub("o%d" % e); ts(oo, v, 2048.0, A.min)
+        w = XBW[e]
+        for c in range(256 // w):
+            mv(R("XB%d" % e, 16 * w * c, 16 * w * c + 16 * w), ind(Xw, sub(oo, w * c, w * c + w)))
 
     def tiles(t):
         n = str(t & 1)
@@ -379,17 +418,21 @@ def build(T, rank):
         scan(E, P("pW"), C256, A.add, A.min)
         mm(P("pE", 0, 16), IDB, sub(MN, 0, 16), True, False); mm(P("pE", 0, 16), ROW15, sub(E, 15, 256, 16), False, True)
         s1 = fb("s1", 1)
-        add("v", lambda g: g.vector.tensor_reduce(s1["ap"], P("pE", 0, 16)["ap"], AxisListType.X, A.max), [P("pE", 0, 16)], [s1], 80.0)
+        add("v", lambda g: g.vector.tensor_reduce(s1["ap"], P("pE", 0, 16)["ap"], AxisListType.X, A.max, negate=True), [P("pE", 0, 16)], [s1], 20 + 64 * CY)
         for k in range(16):
             mm(P("pX", 0, 16), Z15[k], sub(E, k, 256, 16), k == 0, k == 15, k % 8 > 0)
         mv(sub(SC, 0, 16), P("pX", 0, 16))
         mm(P("pW"), IDB, E, True, False); mm(P("pW"), IDN, sub(ES, 15, 271), False, False, True)
         mm(P("pW"), ROW15, sub(ES, 15, 271), False, True, True)
         mv(L(T3), P("pW"))
-        c1 = bb("c1"); ts(c1, JH, s1, A.is_ge)
-        qmm("pE", [(Q1, c1)])
-        u1 = qwrap("l1", "pE")
-        iv = bb("iv"); ts(iv, IOT, s1, A.subtract, 0.0, A.max)
+        c1 = bb("c1"); ts(c1, JH, s1, A.add, 0.0, A.is_ge)
+        if "1" in DIRECT:
+            zmm("pE", ZK, c1)
+            u1 = ub("u_l1", 16); mv(u1, P("pE", 0, 16))
+        else:
+            qmm("pE", [(Q1, c1)])
+            u1 = qwrap("l1", "pE")
+        iv = bb("iv"); act(iv, IOT, F.Relu, bias=s1)
         qmm("pX", [(Q16, c1)], True, False)
         c2 = bb("c2"); tt(c2, ind(SC, u1), JH, A.is_le)
         qmm("pX", [(Q1, c2)], False)
@@ -433,66 +476,104 @@ def build(T, rank):
         XE_, XO = XBw[e], XBw[1 - e]
         CS, CA, CX, CQ, QU = tiles(t)
         nc = 320 if t else 256
-        fuse = FUSE[min(t, 1)]
-        qh = hb("qh")
+        qh = hb("qh", 320); ts(sub(qh, 0, nc), sub(QU, 0, nc), -2048.0, A.add)
         if t == 0:
             s, a, Xa = L(CS), L(CA), L(CX)
-            ts(qh, L(QU), -2048.0, A.add)
-            ts(sub(DZ, 0, 256, 16), sU, -1.0, A.mult, KOFF, A.add)
+            for o in (sub(DQ, 0, 64, 4), sub(DZ, 0, 256, 16)):
+                ts(o, sU, -1.0, A.mult, KOFF, A.add)
         else:
             s, a, Xa = fb("s"), fb("a"), bb("x")
-            mv(s, ind(CS, srcU)); mv(a, ind(CA, srcU)); mv(Xa, ind(CX, srcU)); lin(qh, ind(CQ, srcU), 1.0, -2048.0)
-            qmm("pW", [(QF, s)]); sU = qwrap("s", "pW")
-            ts(sub(DZ, 0, 256, 16), sU, -1.0, A.mult, KOFF, A.add)
+            mv(s, ind(CS, srcU)); mv(a, ind(CA, srcU)); mv(Xa, ind(CX, srcU))
+            sU = wrap("s", s, 256, SCL)
+            for o in (sub(DQ, 0, 64, 4), sub(DZ, 0, 256, 16)):
+                lin(o, sub(fb("w_s"), 15, 256, 16), SCN, KOFF)
+        parts = PARTS[t]
         GE = bb("ge"); act(GE, a, F.Sign, bias=THR)
-        for k in range(16 if fuse else 0):
-            cp(dict(R("XR", k, 16 * fuse, 16), reg=("XR", k, k + 1)), sub(CX, 0, fuse))
+        mode = MODES[min(t, 1)]
+        for lo, hi in LAY[min(t, 1)]:
+            for k in range(16):
+                asel(dict(R("XR", 16 * lo + k, 16 * hi, 16), reg=("XR", 16 * lo + k, 16 * lo + k + 1)), sub(CX, lo, hi), [[0, hi - lo]], A.is_ge, 0, 0)
         XT = bb("xt", 384)
         blocks = [(0, 0), (128, 128), (256, 192)]
         for h, (lo, at0) in enumerate(blocks):
-            if fuse < lo + 128 and lo < nc:
+            if mode[2 * h:2 * h + 2].strip("F"):
                 bank = P(("pE", "pX")[h % 2], 0, 128)
                 mm(bank, sub(CX, at0, at0 + 128), IDB, True, True)
                 mv(sub(XT, 128 * h, 128 * h + 128), bank)
-        nch = nc // 32
-        for c in list(range(fuse // 32, nch)) + list(range(fuse // 32)):
+        sg = bb("sg", 320); mx = hb("mx"); wa = fb("wa", 64); atU = ub("atU", 16); key = hb("key"); at = fb("at"); who = hb("who")
+        whoU = ub("whoU", 16); Wu = ub("wu"); qw = hb("qwh"); my = fb("my", 320)
+
+        def first(lo, hi):
+            S = lambda x, d=1: sub(x, lo // d, hi // d)
+            mm(P("pS", lo, hi), BK, S(ONES), True, False)
+            mm(P("pK", lo // 4, hi // 4), IDB, S(MQ, 4), True, False)
+            if t:
+                lin(S(mx), ind(my, S(srcU, 16)), 1.0, -16384.0)
+            qmm("pK", [(QH, mx)], False, True, lo, hi)
+            mm(P("pS", lo, hi), BLKh, S(mx), False, True)
+            scan(S(wa, 4), S(DQ, 4), P("pK", lo // 4, hi // 4), A.min, A.max, FAR)
+            act(S(atU, 16), sub(wa, lo // 4 + 3, hi // 4, 4), F.Abs, bias=-KOFF)
+            lin(S(key), P("pS", lo, hi), 1.0, -10240.0)
+            tt(S(at), P("pS", lo, hi), S(s), A.max)
+            mv(S(who), ind(Bw, S(atU, 16)))
+            if "w" in DIRECT:
+                zmm("pK", ZH, who, lo, hi)
+                lin(S(whoU, 16), P("pK", lo // 16, hi // 16), 1.0 / 16, 0.0)
+            else:
+                qmm("pK", [(Q0, who)], True, True, lo, hi)
+                x = fb("w_who", 64); scan(S(x, 4), S(SQ, 4), P("pK", lo // 4, hi // 4), A.mult, A.add)
+                lin(S(whoU, 16), sub(x, lo // 4 + 3, hi // 4, 4), SCQ, 0.25)
+            targets(S(ib("qw")), S(Wu), S(whoU, 16), S(at), hi - lo, "w%d" % lo)
+            ts(S(qw), S(Wu), -2048.0, A.add)
+        todo = []
+        for lo, hi in parts:
+            mine = [c for c in list(range(lo // 32, hi // 32)) + list(range(8, nc // 32)) if c not in todo]
+            todo += sorted(mine, key=lambda c: (mode[c // 2] == "F", c)) + [(lo, hi)]
+        for c in todo:
+            if isinstance(c, tuple):
+                spans = [c] if c[0] or not t else [(0, 320)] if c[1] == 256 else [c, (256, 320)]
+                for lo, hi in spans:
+                    act(sub(sg, lo, hi), P("pA", lo, hi), F.Sign, bias=-8.5)
+                if c[1] == 256 and (CUT == 0 or t == 0):
+                    ops[-1]["cut"] = 1
+                for lo, hi in spans:
+                    mm(P("pZ", lo, hi), IDH, sub(qh, lo, hi), True, False)
+                    mm(P("pZ", lo, hi), ZM, sub(sg, lo, hi), False, True)
+                    if t:
+                        act(sub(my, lo, hi), P("pZ", lo, hi), F.Relu, bias=ZD)
+                    else:
+                        ts(sub(mx, lo, hi), P("pZ", lo, hi), ZC, A.add, -16384.0, A.max)
+                first(*c)
+                continue
             cm = R("CM", 512 * c, 512 * c + 512); src = ind(XO, sub(QU, 32 * c, 32 * c + 32))
-            if 32 * c < fuse:
-                tt(cm, src, dict(R("XR", 512 * c, 512 * c + 512), reg=("XR", 0, 16)), A.is_lt)
+            kind = mode[c // 2]
+            if kind == "F":
+                lo = [x[0] for x in LAY[min(t, 1)] if x[0] <= 32 * c < x[1]][0]
+                tt(cm, src, dict(R("XR", 512 * c, 512 * c + 512), reg=("XR", 16 * lo, 16 * lo + 16)), A.is_lt)
             else:
                 xe = R("XE", 512 * c, 512 * c + 512); bank = P(("pE", "pX")[c % 2], 0, 512)
                 h = c // 4; j = (32 * c - blocks[h][1]) // 32
-                mv(xe, src)
-                mm(bank, sub(XT, 128 * h, 128 * h + 128), sub(RM, 512 * j, 512 * j + 512), True, True)
-                tt(cm, xe, bank, A.is_lt)
+                mm(bank, sub(XT, 128 * h, 128 * h + 128), sub(RM, 512 * j, 512 * j + 512), True, kind != "S")
+                if kind == "P":
+                    mv(xe, bank)
+                    tt(cm, src, xe, A.is_lt)
+                elif kind == "U":
+                    mv(xe, src)
+                    tt(cm, xe, bank, A.is_lt)
+                else:
+                    mv(xe, src)
+                    mm(bank, IDN, xe, False, True)
+                    act(cm, bank, F.Sign, bias=-2.0 ** -110)
             if c % 2:
-                cm = R("CM", 512 * c - 512, 512 * c + 512)
+                cm = R("CM", 512 * c - 512, 512 * c + 512); o = P("pA", 32 * c - 32, 32 * c + 32)
+                if kind == "S":
+                    mm(o, BH5, sub(ONES, 0, 64), True, False)
                 for k in range(16):
-                    mm(P("pA", 32 * c - 32, 32 * c + 32), ZK[k], sub(cm, k, 1024, 16), k == 0, k == 15, k % 8 > 0)
-        mm(P("pZ"), IDH, qh, True, False)
-        mm(P("pS"), S0, s, True, False)
-        mm(P("pK", 0, 64), IDB, MQ, True, False)
+                    mm(o, (ZK5 if kind == "S" else ZK)[k], sub(cm, k, 1024, 16), k == 0 and kind != "S", k == 15, k % 8 > 0)
         mm(P("pC"), IDB, MD, True, False); mm(P("pC"), AB, GE, False, False)
-        sg = bb("sg", 320); act(sub(sg, 0, nc), P("pA", 0, nc), F.Sign, bias=-8.5)
-        if t:
-            sm = bb("sgm"); mv(sm, ind(sg, srcU))
-        else:
-            sm = L(sg)
-        mm(P("pZ"), ZM, sm, False, True); mm(P("pS"), BF, sm, False, True)
-        mx = hb("mx"); ts(mx, P("pZ"), ZC, A.add, -16384.0, A.max)
-        s2 = hb("s2"); ts(s2, P("pS"), SC0, A.add, -16384.0, A.max)
-        qmm("pK", [(QH, mx), (Q0, s2)], False)
-        mm(P("pS"), BLKh, mx, True, False); mm(P("pS"), R01, s2, False, True)
-        wa = fb("wa", 64); scan(wa, DQ, P("pK", 0, 64), A.min, A.max)
-        atU = ub("atU", 16); lin(atU, sub(wa, 3, 64, 4), 1.0, 2048.0)
-        key = hb("key"); lin(key, P("pS"), 1.0, 229376.0)
-        at = fb("at"); lin(at, P("pS"), 1.0, 264192.0)
-        who = hb("who"); mv(who, ind(Bw, atU))
-        qmm("pK", [(Q0, who)]); whoU = qwrap("who", "pK")
-        Wu = ub("wu"); targets(ib("qw"), Wu, whoU, at, 256, "w")
-        qw = hb("qwh"); ts(qw, Wu, -2048.0, A.add)
-        mm(P("pZ"), IDH, qw, True, False)
-        x = rivals(key, lambda c: sub(wa, 4 * c + 3, 4 * c + 4), None, DZ)
+        for lo, hi in parts:
+            mm(P("pZ", lo, hi), IDH, sub(qw, lo, hi), lo == 0, False)
+        x = rivals(key, lambda c: sub(wa, 4 * c + 3, 4 * c + 4), -KOFF - 2048.0, DZ)
         baseU = ub("baseU", 16); act(baseU, x, F.Abs, bias=-KOFF)
         EN = bb("en"); act(EN, P("pC"), F.Sign, unit=True)
         if t < 3:
@@ -502,34 +583,41 @@ def build(T, rank):
         o = P("pA")
         mm(o, BI1, GE, True, False); mm(o, BI2, GE, False, False); mm(o, IDH, key, False, False); mm(o, BP, EN, False, True)
         fl = bb("fl"); act(fl, o, F.Sign, bias=3000.0 + 14 * 16384.0 - 65536.0)
-        tt(L(PAY), ind(Bw, baseU), a, A.add)
-        pf = bb("pf"); scan(pf, fl, ONES, A.add, A.add)
+        mm(P("pS"), IDF, a, True, False); mm(P("pS"), IDH, who, False, True)
+        mv(L(PAY), P("pS"))
+        pf = hb("pf"); scan(pf, fl, ONES, A.add, A.add)
         acc = fb("acc", 4)
         for j in range(4):
-            act(bb("junk%d" % j), pf, F.Sign, bias=sub(SLB, j, j + 1), acc=sub(acc, j, j + 1))
+            o = P(("pA", "pS")[j % 2], 256, 512)
+            mm(o, sub(ROWS, 128 * j, 128 * j + 128), pf, True, True)
+            act(bb("junk%d" % j), o, F.Sign, bias=SLB, acc=sub(acc, j, j + 1))
         ix = ub("ix", 4); lin(ix, acc, -0.5, 128.25)
-        G = fb("g", 64); SD = fb("sd%d" % t, 4); jf = fb("jf", 64)
+        G = fb("g", 64); SD = fb("sd", 64)
         tt(G, ind(PAY, ix), MP, A.mult)
-        for p in range(4):
-            c = 16 * t + 4 * rank
-            act(sub(jf, 16 * p, 16 * p + 16), sub(G, p, 64, 4), F.Copy, acc=R("RV", c, c + 1) if p == rank else sub(SD, p, p + 1),
-                more=[R("RV", 16 * t + 4 * p, 16 * t + 4 * p + 1), sub(SD, p, p + 1)])
-        snd = add("g", ("send", t, SD), [SD], [], 300.0, 4500.0, "r")
-        for c in range(8):
-            act(R("CM", 512 * c, 512 * c + 512), ind(Bw, sub(Wu, 32 * c, 32 * c + 32)), F.Relu, bias=-2047.0)
+        scan(SD, sub(DS, 0, 64), G, A.mult, A.add)
+        c = 16 * t + 4 * rank
+        mine = dict(R("RV", c, c + 4), reg=("RV", 16 * t, 16 * t + 16))
+        mv(mine, sub(SD, 15, 64, 16))
+        snd = add("g", ("send", t), [mine], [], 300.0, FLIGHT, "r")
+        c = 0
+        for w in MCH:
+            act(R("CM", 16 * c, 16 * (c + w)), ind(Bw, sub(Wu, c, c + w)), F.Relu, bias=-2047.0)
+            c += w
         mm(P("pZ"), BP, EN, False, False)
         for c in range(4):
             cm = R("CM", 1024 * c, 1024 * c + 1024)
             for k in range(16):
                 mm(P("pZ", 64 * c, 64 * c + 64), LK[k], sub(cm, k, 1024, 16), False, c == 3 and k == 15, k % 8 > 0)
         for u in (sU, baseU):
-            act(ind(Bw, u), CE, F.Silu)
+            for lo, hi in SPL[0]:
+                act(ind(Bw, sub(u, lo, hi)), sub(CE, 0, 16 * (hi - lo)), F.Silu)
         if t < 3:
             mm(P("pW"), TRI, ONES, True, False)
             for k in range(16):
                 mm(P("pW"), LT[k], R(XO["nm"], k, 4096, 16), False, k == 15, k % 2 > 0)
             select(t + 1)
-            cp(ind(XE_, sU), CBIG)
+            for lo, hi in SPL[1]:
+                cp(ind(XE_, sub(sU, lo, hi)), sub(CBIG, 0, 16 * (hi - lo)))
         m2 = hb("m2"); ts(m2, P("pZ"), 14 * 16384.0 - 32768.0, A.add, -16384.0, A.max)
         mm(P("pS"), BLKh, m2, True, True)
         for k in range(16):
@@ -540,9 +628,10 @@ def build(T, rank):
         endU = ub("endU", 16); act(endU, y, F.Abs, bias=-KOFF)
         if t < 3:
             cp(ind(XE_, endU), Xa)
-        ts(ind(Bw, endU), a, 1.0 / 8192, A.mult, 0.0, A.add)
+        if t < 3 or not LAST:
+            ts(ind(Bw, endU), a, 1.0 / 8192, A.mult, 0.0, A.add)
         CS, CA, CX, CQ, QU = tiles(t + 1)
-        raU = ub("raU", 4); rv = R("RV", 16 * t, 16 * t + 16, 4)
+        raU = ub("raU", 4); rv = dict(R("RV", 16 * t + rank, 16 * t + 16, 4), reg=("RV", 16 * t, 16 * t + 16))
         add("v", lambda g, o=raU, i=rv: g.vector.tensor_scalar(o["ap"], i["ap"], 1.0 / 8192, 16.1 - 512.0 * rank, A.mult, A.add),
             [rv], [raU], 90.0, ext=("ar%d" % t, snd))
         pi = ib("rpi", 4); add("v", lambda g, o=pi, i=rv: g.vector.tensor_copy(o["ap"], i["ap"]), [rv, raU], [pi], 90.0)
@@ -553,40 +642,49 @@ def build(T, rank):
         hU = wrap("h", RS, 64, SCL)
         mv(RA, ind(UTw, rvU))
         hc = fb("hc", 64); lin(hc, RS, -1.0 / 8192, 2048.0)
-        hm_ = fb("hmk", 64); tt(hm_, hc, MK, A.min)
         if t < 3:
             mv(sub(CX, 256, 320), ind(Xw, rvU))
             targets(sub(CQ, 256, 320), sub(QU, 256, 320), rvU, RS, 64, "r")
-        hy = fb("hy", 64); tt(hy, ind(Bw, hU), hm_, A.min)
-        hv = fb("hv", 64); scan(hv, DY, hy, A.min, A.max, FAR)
+        if CUT == 1 and t < 3:
+            ops[-1]["cut"] = 1
+        hv = fb("hv", 64)
+        if t < 3:
+            hz = fb("hz", 64); tt(hz, ind(Bw, hU), hc, A.min)
+            mm(P("pW", 0, 64), IDB, MN, True, False); mm(P("pW", 0, 64), IDF, hz, False, True)
+            scan(hv, DY, P("pW", 0, 64), A.min, A.max, FAR)
+        else:
+            hm_ = fb("hmk", 64); tt(hm_, hc, MK, A.min)
+            hy = fb("hy", 64); tt(hy, ind(Bw, hU), hm_, A.min)
+            scan(hv, DY, hy, A.min, A.max, FAR)
         hkU = ub("hkU", 4); lin(hkU, sub(hv, 15, 64, 16), -8192.0, 2.0 ** 24)
         ts(ind(Bw, hkU), RA, 1.0 / 8192, A.mult, 0.0, A.add)
+        if t == 3 and LAST:
+            ts(ind(Bw, endU), a, 1.0 / 8192, A.mult, 0.0, A.add)
         if t < 2:
             cp(ind(XO, hkU), sub(CX, 256, 320))
         if t < 3:
-            hk = fb("hk", 4); lin(hk, sub(hv, 15, 64, 16), -8192.0, 2.0 ** 24)
             hf = fb("hf", 4); lin(hf, sub(fb("w_h", 64), 15, 64, 16), SCL, -0.25)
-            ac2 = fb("ac2", 4)
+            hn = fb("hn", 4); lin(hn, sub(fb("w_h", 64), 15, 64, 16), SCL8, -2048.0)
+            ac2 = fb("ac2", 4); ac3 = fb("ac3", 4)
             for j in range(4):
                 act(bb("junk%d" % j), L(CS), F.Sign, bias=sub(hf, j, j + 1), scale=-1.0, acc=sub(ac2, j, j + 1))
-            bad = fb("bad", 4); ts(bad, sub(hv, 15, 64, 16), 2048.0 - 4415.0 / 8192, A.is_lt, 1024.0, A.mult)
-            ac3 = fb("ac3", 4); tt(ac3, ac2, bad, A.add)
-            mm(P("pW", 0, 64), IDB, MN, True, False)
             for j in range(4):
-                m = bb("mj%d" % j, 64); ts(m, RS, sub(hk, j, j + 1), A.is_gt)
-                mm(P("pW", 0, 64), B2, m, False, j == 3)
-            nw = fb("nw", 64); scan(nw, sub(DR, 0, 64), P("pW", 0, 64), A.min, A.max)
-            rk = fb("rk", 4); tt(rk, sub(nw, 15, 64, 16), ac3, A.add)
-            vl = fb("vl", 4); tt(vl, VC, ac2, A.subtract)
+                act(bb("jun%d" % j, 64), hz, F.Sign, bias=sub(hn, j, j + 1), acc=sub(ac3, j, j + 1))
+            mm(P("pK", 4, 8), IDF, VC, True, False); mm(P("pK", 4, 8), IDM, ac2, False, False, True)
+            mm(P("pK", 0, 4), IDL, hn, False, False, True); mm(P("pK", 0, 4), IDL, sub(hv, 15, 64, 16), False, False)
+            mm(P("pK", 0, 4), IDF, ac2, False, False, True); mm(P("pK", 0, 4), IDF, ac3, False, True)
+            rk = [dict(P("pK", j, j + 1), share=1) for j in range(8)]
+            if NLS:
+                rs = fb("rk", 4); cp(rs, dict(P("pK", 0, 4), share=1))
             mm(P("pW", 0, 64), IDB, IOQ, True, False)
             terms = []
             for j in range(4):
-                eq = hb("eq%d" % j); ts(eq, IO2, sub(rk, j, j + 1), A.is_equal, sub(vl, j, j + 1), A.mult)
+                eq = hb("eq%d" % j); ts(eq, IO2, rk[j], A.is_equal, rk[4 + j], A.mult)
                 if j < NLS:
-                    lt = bb("ls%d" % j); act(lt, IO2, F.Sign, bias=sub(rk, j, j + 1), scale=-1.0)
+                    lt = bb("ls%d" % j); act(lt, IO2, F.Sign, bias=sub(rs, j, j + 1), scale=-1.0)
                     terms += [(QH5, eq), (QB5, lt)]
                 else:
-                    lt = hb("lt%d" % j); ts(lt, IO2, sub(rk, j, j + 1), A.is_gt, -2.0, A.mult)
+                    lt = hb("lt%d" % j); ts(lt, IO2, rk[j], A.is_gt, -2.0, A.mult)
                     terms += [(QH5, eq), (QH5, lt)]
             qmm("pW", terms, False)
             srcU = qwrap("src", "pW", 0.25 - 8 * NLS)
@@ -595,7 +693,7 @@ def build(T, rank):
     return ops
 
 
-def schedule(ops):
+def schedule_whole(ops):
     n = len(ops)
     hist = {}
     pred = [set() for _ in range(n)]
@@ -770,6 +868,411 @@ def schedule(ops):
     return pred, order, start, end
 
 
+def schedule(ops):
+    n = len(ops)
+    hist = {}
+    pred = [set() for _ in range(n)]
+    for i, o in enumerate(ops):
+        for w, regs in ((False, o["rd"]), (True, o["wr"])):
+            for (nm, lo, hi) in regs:
+                for (j, l2, h2, w2) in hist.get(nm, []):
+                    if j != i and (w or w2) and l2 < hi and lo < h2:
+                        pred[i].add(j)
+        for (nm, lo, hi) in o["wr"]:
+            hist[nm] = [x for x in hist.get(nm, []) if not (lo <= x[1] and x[2] <= hi)] + [(i, lo, hi, True)]
+        for (nm, lo, hi) in o["rd"]:
+            hist.setdefault(nm, []).append((i, lo, hi, False))
+    if "best" not in KEPT:
+        KEPT["best"] = search(ops, pred)
+    best = KEPT["best"]
+    for i in range(n):
+        if "alt" in ops[i]:
+            ops[i]["eng"] = best[2][i]
+            ops[i]["fn"], ops[i]["dur"] = ops[i]["alt"][best[2][i]]
+    start = list(best[0])
+    loads = [i for i in range(n) if ops[i]["eng"] == "y" and not pred[i]]
+    for i, x in zip(loads, sorted(start[i] for i in loads)):
+        start[i] = x
+    end = [start[i] + ops[i]["dur"] + ops[i]["lat"] for i in range(n)]
+    order = {}
+    for i in sorted(range(n), key=lambda k: (start[k], k)):
+        order.setdefault(ops[i]["eng"], []).append(i)
+    return pred, order, start, end
+
+
+def search(ops, pred):
+    n = len(ops)
+    lats = [o["lat"] for o in ops]
+    anc = [0] * n
+    fwd = []
+    for i in range(n):
+        far = 0
+        for j in pred[i]:
+            far |= anc[j]
+        fwd.append([(j, lats[j]) for j in sorted(pred[i]) + ([ops[i]["ext"][1]] if ops[i]["ext"] else []) if lats[j] or not far >> j & 1])
+        for j in pred[i]:
+            far |= 1 << j
+        anc[i] = far
+    alts = [[(e, x[1]) for e, x in sorted(o["alt"].items())] if "alt" in o else [(o["eng"], o["dur"])] for o in ops]
+    tail = list(lats)
+    for i in range(n - 1, -1, -1):
+        d = min(x[1] for x in alts[i])
+        for j, h in fwd[i]:
+            tail[j] = max(tail[j], tail[i] + d + h + (0.0 if ops[i]["eng"] == ops[j]["eng"] == "p" else HOP))
+    st = [0.0] * n
+    en = [0.0] * n
+    eng = [None] * n
+    seed = [SEED]
+
+    def rnd():
+        seed[0] = (seed[0] * 1103515245 + 12345) % 2147483648
+        return seed[0] / 2147483648.0
+
+    def place(lst, t, d):
+        lo = 0
+        hi = len(lst)
+        if not hi or lst[-1][1] <= t:
+            return t, hi
+        while lo < hi:
+            m = (lo + hi) // 2
+            if lst[m][1] <= t:
+                lo = m + 1
+            else:
+                hi = m
+        while lo < len(lst) and t + d > lst[lo][0]:
+            t = lst[lo][1]
+            lo += 1
+        return t, lo
+
+    def put(seq, base, lean, bound):
+        busy = {e: list(base[e]) for e in base}
+        worst = 0.0
+        total = 0.0
+        for i in seq:
+            pick = None
+            for e, d in alts[i]:
+                t = 0.0
+                for j, h in fwd[i]:
+                    x = en[j] + h + (0.0 if e == "p" == eng[j] else HOP)
+                    if x > t:
+                        t = x
+                t, lo = place(busy[e], t, d)
+                c = t + d + (lean[i] if e == "v" else 0.0)
+                if pick is None or c < pick[0]:
+                    pick = (c, e, t, d, lo)
+            c, e, t, d, lo = pick
+            busy[e].insert(lo, (t, t + d))
+            st[i] = t
+            en[i] = t = t + d
+            eng[i] = e
+            total += t
+            t += tail[i]
+            if t > worst:
+                worst = t
+                if t > bound:
+                    return None
+        return worst + SOFT * total / len(seq), worst
+
+    def ordered(a, b, key):
+        for i in range(a, b):
+            for j, h in fwd[i]:
+                if j >= a and key[j] >= key[i]:
+                    key[i] = key[j] + 0.001
+        return sorted(range(a, b), key=lambda k: key[k])
+
+    def pull(todo, a, key):
+        while todo:
+            k = todo.pop()
+            for j, h in fwd[k]:
+                if j >= a and key[j] >= key[k]:
+                    key[j] = key[k] - 0.001
+                    todo.append(j)
+
+    def blocks(a, b):
+        last = {}
+        before = {}
+        for i in sorted(range(a, b), key=lambda k: st[k]):
+            before[i] = last.get(eng[i])
+            last[eng[i]] = i
+        out = []
+        i = max(range(a, b), key=lambda k: en[k] + tail[k])
+        while i >= a:
+            d = None
+            for j, h in fwd[i]:
+                x = en[j] + h + (0.0 if eng[i] == "p" == eng[j] else HOP)
+                if d is None or x > d[0]:
+                    d = (x, j)
+            if d is not None and d[0] >= st[i] - 0.01:
+                i = d[1]
+            elif before[i] is not None:
+                out.append((before[i], i))
+                i = before[i]
+            else:
+                break
+        return out
+
+    def late(a, b):
+        busy = {e: [] for e in "vspgy"}
+        back = {i: tail[i] for i in range(a, b)}
+        for i in sorted(range(a, b), key=lambda k: (-en[k], -k)):
+            d = en[i] - st[i]
+            t, lo = place(busy[eng[i]], back[i], d)
+            busy[eng[i]].insert(lo, (t, t + d))
+            back[i] = -t - d
+            for j, h in fwd[i]:
+                if j >= a:
+                    back[j] = max(back[j], t + d + h + (0.0 if eng[i] == "p" == eng[j] else HOP))
+        return back
+
+    def improve(a, b, base, key, lean, tries):
+        cur = put(ordered(a, b, key), base, lean, 1e18)
+        keep = (st[a:b], en[a:b], eng[a:b])
+        best = (cur, keep)
+        bs = blocks(a, b)
+        for it in range(tries):
+            key = dict(zip(range(a, b), keep[0]))
+            l2 = dict(zip(range(a, b), [-1e9 if e == "v" else 1e9 for e in keep[2]]))
+            if rnd() < RUN:
+                lo = a + int(rnd() * (b - a)); d = (rnd() - 0.6) * 6000 * rnd()
+                todo = list(range(lo, min(b, lo + 3 + int(40 * rnd() ** 2))))
+                for i in todo:
+                    key[i] += d
+                    if len(alts[i]) > 1 and rnd() < 0.2:
+                        l2[i] = LEAN * (2.5 * rnd() - 0.5)
+                if d < 0:
+                    pull(todo, a, key)
+            elif bs and rnd() < AIM:
+                for x in range(1 + int(2.5 * rnd() ** 2)):
+                    p, i = bs[int(rnd() * len(bs))]
+                    u = rnd()
+                    if u < 0.25 and len(alts[p]) > 1:
+                        l2[p] = -l2[p]
+                    elif u < 0.4 and len(alts[i]) > 1:
+                        l2[i] = -l2[i]
+                    elif u < 0.75:
+                        key[p] = key[i] + 1 + 1500 * rnd() ** 2
+                    else:
+                        key[i] = key[p] - 1 - 1500 * rnd() ** 2
+                        pull([i], a, key)
+            else:
+                lo = keep[0][int(rnd() * (b - a))] - 1000; hi = lo + 1500 + WIN * rnd(); amp = 100 + AMP * rnd()
+                for i in range(a, b):
+                    if lo <= key[i] < hi:
+                        key[i] += amp * (rnd() - 0.5)
+                        if len(alts[i]) > 1 and rnd() < 0.3:
+                            l2[i] = LEAN * (2.5 * rnd() - 0.5)
+            tol = TOL * (1.0 - it / tries)
+            if it % JUST == 0:
+                put(ordered(a, b, key), base, l2, 1e18)
+                l2 = dict(zip(range(a, b), [-1e9 if e == "v" else 1e9 for e in eng[a:b]]))
+                key = late(a, b)
+            r = put(ordered(a, b, key), base, l2, cur[1] + tol + 300.0)
+            if r is not None and r[0] <= cur[0] + tol:
+                cur = r
+                keep = (st[a:b], en[a:b], eng[a:b])
+                bs = blocks(a, b)
+                if r[0] < best[0][0]:
+                    best = (r, keep)
+        st[a:b], en[a:b], eng[a:b] = best[1]
+
+    def refine(b, since, until, tries):
+        whole = sorted(range(b), key=lambda k: (st[k], k))
+        head = [i for i in whole if st[i] < since]
+        act = [i for i in whole if since <= st[i] < until]
+        rest = [i for i in whole if st[i] >= until]
+        loc = {i: x for x, i in enumerate(act)}
+        m = len(act)
+        deg = [len([j for j, h in fwd[i] if j in loc]) for i in act]
+        alt = [dict(alts[i]) for i in act]
+        on = [eng[i] for i in act]
+        seq = {e: [x for x in range(m) if on[x] == e] for e in "vspgy"}
+        sets = []
+        for c in range(len(COSTS)):
+            end, free = play(head, c)
+            rel = [max([end[j] + h for j, h in edges[c][i] if j not in loc] + [0.0]) for i in act]
+            nxt = [[] for i in act]
+            for x, i in enumerate(act):
+                for j, h in edges[c][i]:
+                    if j in loc:
+                        nxt[loc[j]].append((x, h))
+            tl = list(tails[c])
+            then = {e: -1e18 for e in "vspgy"}
+            for i in reversed(rest):
+                then[eng[i]] = d = max(tl[i], then[eng[i]]) + ops[i]["times"][c][eng[i]]
+                for j, h in edges[c][i]:
+                    if d + h > tl[j]:
+                        tl[j] = d + h
+            sets.append((rel, free, nxt, [tl[i] for i in act], [ops[i]["times"][c] for i in act], tails[0][0] / tails[c][0], then))
+
+        def times(bound):
+            left = list(deg)
+            after = [-1] * m
+            for e in seq:
+                q = seq[e]
+                for x, y in zip(q, q[1:]):
+                    after[x] = y
+                    left[y] += 1
+            todo = [x for x in range(m) if not left[x]]
+            nxt = sets[0][2]
+            for x in todo:
+                for y, h in nxt[x]:
+                    left[y] -= 1
+                    if not left[y]:
+                        todo.append(y)
+                y = after[x]
+                if y >= 0:
+                    left[y] -= 1
+                    if not left[y]:
+                        todo.append(y)
+            if len(todo) < m:
+                return None
+            total = 0.0
+            waits = []
+            parts = []
+            for c, (rel, free, nxt, tl, dur, scale, then) in enumerate(sets):
+                t0 = list(rel)
+                by = [-1] * m
+                for e in seq:
+                    if seq[e]:
+                        t0[seq[e][0]] = max(t0[seq[e][0]], free[e])
+                worst = 0.0
+                last = -1
+                for x in todo:
+                    t = t0[x] + dur[x][on[x]]
+                    if t + tl[x] > worst:
+                        worst = t + tl[x]
+                        last = x
+                    for y, h in nxt[x]:
+                        if t + h > t0[y]:
+                            t0[y] = t + h
+                            by[y] = x
+                    y = after[x]
+                    if y < 0:
+                        if t + then[on[x]] > worst:
+                            worst = t + then[on[x]]
+                            last = x
+                    elif t > t0[y]:
+                        t0[y] = t
+                        by[y] = -2 - x
+                parts.append((worst + SOFT * sum(t0) / m) * scale / len(sets))
+                if bound and sum(parts) + sum(bound[1][c + 1:]) - 400.0 * (len(sets) - 1 - c) > bound[0]:
+                    return None
+                if c == 0:
+                    first = t0
+                while last != -1:
+                    p = by[last]
+                    if p < -1:
+                        p = -2 - p
+                        waits.append((p, last))
+                    last = p
+            return sum(parts), first, waits, parts
+        cur = times(None)
+        best = (cur, list(on))
+        for it in range(tries):
+            if not cur[2]:
+                break
+            p, i = cur[2][int(rnd() * len(cur[2]))]
+            u = rnd()
+            x = p if rnd() < 0.5 else i
+            if u < 0.1:
+                x = int(rnd() * m)
+            e = on[x]
+            q = seq[e]
+            k = q.index(x)
+            if u < 0.35 and len(alt[x]) > 1:
+                e2 = [z for z in alt[x] if z != e][int(rnd() * (len(alt[x]) - 1))]
+                q2 = seq[e2]
+                k2 = 0
+                lim = cur[1][x] + (rnd() - 0.5) * 1200
+                while k2 < len(q2) and cur[1][q2[k2]] < lim:
+                    k2 += 1
+            else:
+                e2 = e
+                q2 = q
+                step = 1 + int(6 * rnd() ** 2)
+                k2 = max(0, k - step) if x == i else min(len(q) - 1, k + step)
+            del q[k]
+            q2.insert(k2, x)
+            on[x] = e2
+            lim = cur[0] + HEAT * (1.0 - it / tries) * rnd() ** 2
+            r = times((lim, cur[3]))
+            if r is not None and r[0] <= lim:
+                cur = r
+                if r[0] < best[0][0]:
+                    best = (r, list(on))
+            else:
+                del q2[k2]
+                q.insert(k, x)
+                on[x] = e
+        for x, i in enumerate(act):
+            eng[i] = best[1][x]
+        whole = head + [act[x] for x in sorted(range(m), key=lambda k: (best[0][1][k], k))] + rest
+        for i, t in play(whole, 0)[0].items():
+            en[i] = t
+            st[i] = t - ops[i]["times"][0][eng[i]]
+        return best[0][0]
+
+    def play(seq, c):
+        end = {}
+        free = {e: 0.0 for e in "vspgy"}
+        for i in seq:
+            end[i] = free[eng[i]] = max([free[eng[i]]] + [end[j] + h for j, h in edges[c][i]]) + ops[i]["times"][c][eng[i]]
+        return end, free
+    edges = [[[(j, h + (0.0 if ops[i]["eng"] == ops[j]["eng"] == "p" else c[4])) for j, h in fwd[i]] for i in range(n)] for c in COSTS]
+    tails = []
+    for c in range(len(COSTS)):
+        tl = list(lats)
+        for i in range(n - 1, -1, -1):
+            for j, h in edges[c][i]:
+                tl[j] = max(tl[j], tl[i] + min(ops[i]["times"][c].values()) + h)
+        tails.append(tl)
+
+    cuts = [0] + [i + 1 for i in range(n) if "cut" in ops[i]] + [n]
+    sig = [(o["eng"], round(o["dur"]), len(o["rd"]), o["wr"][0][0][:2] if o["wr"] else "") for o in ops]
+    base = {e: [] for e in "vspgy"}
+    for s in range(len(cuts) - 1):
+        a, b = cuts[s], cuts[s + 1]
+        key = {i: -tail[i] - alts[i][0][1] for i in range(a, b)}
+        lean = {i: LEAN for i in range(a, b)}
+        if s >= 2:
+            p = cuts[s - 1]
+            k2 = {}
+            l2 = {}
+            at = st[p]
+            for i in range(a, b):
+                q = p
+                while q < a and q < p + 12 and sig[q] != sig[i]:
+                    q += 1
+                if q < a and sig[q] == sig[i]:
+                    at = st[q]
+                    l2[i] = -1e9 if eng[q] == "v" else 1e9
+                    p = q + 1
+                else:
+                    l2[i] = LEAN
+                k2[i] = at
+            if put(ordered(a, b, k2), base, l2, 1e18)[0] < put(ordered(a, b, key), base, lean, 1e18)[0]:
+                key, lean = k2, l2
+        since = max(en[:a] + [0.0]) - BACK
+        was = (list(st), list(en), list(eng))
+        best = None
+        for x in range(AGAIN):
+            st[:], en[:], eng[:] = was
+            improve(a, b, base, dict(key), lean, TRIES)
+            r = refine(b, since, 1e18, MOVES)
+            if best is None or r < best[0]:
+                best = (r, list(st), list(en), list(eng))
+        st[:], en[:], eng[:] = best[1:]
+        base = {e: sorted((st[i], en[i]) for i in range(b) if eng[i] == e) for e in "vspgy"}
+    for x in range(SWEEPS):
+        t = -PANE * rnd()
+        while t < max(en):
+            refine(n, t, t + PANE, POLISH)
+            t += PANE / 2
+    whole = sorted(range(n), key=lambda k: (st[k], k))
+    KEPT["spans"] = [max(t + lats[i] for i, t in play(whole, c)[0].items()) for c in range(len(COSTS))]
+    return st, en, eng
+
+
 def rank_program(g, core, T, topo):
     rank = T.rank_of(core)
     if rank is None:
@@ -820,7 +1323,8 @@ def rank_program(g, core, T, topo):
                 tick[i] = (CNT[e], c)
         if comp:
             total[CNT[e]] = c
-    peers = [p for p in range(len(T.cores)) if p != rank]
+    peers = [p for p in T.cores if p != core]
+    use = [x for x in topo.engines(core, peers[0]) if all(x in topo.engines(core, p) for p in peers)]
     sent = 0
     for i in sorted(range(len(ops)), key=lambda k: (start[k], k)):
         o = ops[i]
@@ -828,19 +1332,14 @@ def rank_program(g, core, T, topo):
         for j in need[i]:
             q.wait_ge(T.sem[tick[j][0]], tick[j][1])
         if o["ext"]:
-            q.wait_ge(T.sem[o["ext"][0]], 2 * len(peers))
+            q.wait_ge(T.sem[o["ext"][0]], len(use) * len(peers))
         if o["kind"] == "r":
-            t, sd = o["fn"][1], o["fn"][2]
-            trs = []
-            for x, p in enumerate(peers):
-                dst = T.cores[p]
-                rid, pid, _ = topo.addr(dst)
-                en = topo.engines(core, dst)
-                c = 16 * t + 4 * rank
-                trs.append(RemoteDMATransfer(dst_ids=[DstId(rid=rid, pnc=pid)], dma_engine_mask=(1 << en[2 * x]) | (1 << en[2 * x + 1]),
-                                             remote_sem=T.sem["ar%d" % t], src=T.PF[:, sd["a"] + p:sd["a"] + p + 1], dst=T.RV[:, c:c + 1]))
-            g.remote_dma_fused(trs, local_sem=T.sem.loc)
-            sent += 2 * len(peers)
+            t = o["fn"][1]
+            mine = T.RV[:, 16 * t + 4 * rank:16 * t + 4 * rank + 4]
+            to = [DstId(rid=topo.addr(p)[0], pnc=topo.addr(p)[1]) for p in peers]
+            g.remote_dma_fused([RemoteDMATransfer(dst_ids=to, dma_engine_mask=sum(1 << x for x in use), remote_sem=T.sem["ar%d" % t],
+                                                  srcs=[mine], dsts=[mine] * len(peers))], local_sem=T.sem.loc)
+            sent += len(use)
         else:
             ins = o["fn"](g)
             if o["kind"] == "d":

from concourse.bass import DstId, RemoteDMATransfer
from concourse.mybir import AluOpType as A, AxisListType, ActivationFunctionType as F

HT = "float16"
MODES = ("UUUU", "SSFFS")
LAY = ((), ((128, 256),))
MCH = (32,) * 8
SPL = (((0, 16),), ((0, 16),))
PARTS = (((0, 256),),) * 4
CUT = 0
LAST = True
DIRECT = ""
RMG = True
XBW = (32, 32)
NLS = 0
BIG = 2.0 ** 60
FAR = 2.0 ** 30
TW = 4480
MUL = 2.0 ** 30
KOFF = 38912.0

POOL = {"PF": ("float32", 11264), "PB": ("bfloat16", 22528), "PH": (HT, 9216), "PI": ("int32", 4096), "PU": ("uint16", 3072)}
SCRATCH = {k: ("sbuf", [128, v[1]], v[0]) for k, v in POOL.items()}
SCRATCH.update({
    "LB": ("sbuf", [128, 2, 8, 16], "int32"), "CV": ("sbuf", [128, 8, 32], "int32"), "LN": ("sbuf", [128, 256], "int32"),
    "X": ("sbuf", [128, 2064], "bfloat16"), "D": ("sbuf", [128, 2064], "int32"), "HM": ("sbuf", [128, 528], "int32"),
    "UT": ("sbuf", [128, 2064], "float32"), "B": ("sbuf", [128, TW], "float32"),
    "XB0": ("sbuf", [128, TW], "bfloat16"), "XB1": ("sbuf", [128, TW], "bfloat16"),
    "XE": ("sbuf", [128, 5120], "bfloat16"), "CM": ("sbuf", [128, 5120], "bfloat16"), "XR": ("sbuf", [128, 4096], "bfloat16"),
    "FC": ("sbuf", [128, 16, 256], "bfloat16"), "RV": ("sbuf", [128, 64], "float32"),
})
for _b in ("pA", "pZ", "pK", "pS", "pC", "pE", "pW", "pX"):
    SCRATCH[_b] = ("psum", [128, 512], "float32")
NDMA = 26
SEMAPHORES = ["cv", "cs", "cp", "cg", "loc", "ar0", "ar1", "ar2", "ar3"] + ["d%d" % i for i in range(NDMA)]
WID = {"float32": 4, "bfloat16": 2, "float16": 2, "int32": 4, "uint16": 2}
COSTS = ((1.0, 0.51, 1.56, 3.8, 210.0), (1.2, 0.61, 1.95, 5.2, 220.0), (0.9, 0.46, 1.35, 3.0, 200.0))
HOP = 200.0
HOP_SAME = 200.0
AGAIN = 2
SWEEPS = 5
PANE = 14000.0
FLIGHT = 3800.0
TRIES = 2000
MOVES = 500
POLISH = 2000
AIM = 0.8
RUN = 0.25
WIN = 8000
AMP = 2000
JUST = 4
TOL = 80.0
HEAT = 150.0
SOFT = 0.005
BACK = 3000.0
LEAN = 1500.0
SEED = 1
KEPT = {}


def build(T, rank):
    runs = [record(T, rank, c) for c in COSTS]
    for x in zip(*runs):
        x[0]["times"] = [{e: a[1] for e, a in o["alt"].items()} if "alt" in o else {o["eng"]: o["dur"]} for o in x]
    return runs[0]


def record(T, rank, cost):
    CY, PEC, GAT, SCA = cost[:4]
    ops = []
    place = {}
    top = {k: 0 for k in POOL}

    def R(name, a, b, st=1):
        d = SCRATCH[name]
        ap = T[name][:, a:b] if st == 1 else T[name][:, a:b:st]
        return {"ap": ap, "reg": (name, a, b), "n": len(range(a, b, st)), "w": WID[d[2]], "ps": d[0] == "psum", "nm": name, "a": a}

    def RX(name, ap, lo, hi, n):
        d = SCRATCH[name]
        return {"ap": ap, "reg": (name, lo, hi), "n": n, "w": WID[d[2]], "ps": False, "nm": name, "a": lo}

    def buf(pool, key, n):
        if key not in place:
            place[key] = (pool, top[pool], n)
            top[pool] += (n + 15) // 16 * 16
            assert top[pool] <= POOL[pool][1], pool
        assert place[key][0] == pool and place[key][2] >= n, key
        return R(pool, place[key][1], place[key][1] + n)

    def sub(r, a, b, st=1):
        return R(r["nm"], r["a"] + a, r["a"] + b, st)

    def ind(win, off):
        return {"ap": win["ap"].indirect(off["ap"]), "reg": win["reg"], "off": off, "n": 16 * off["n"], "w": 4, "ps": False}

    def add(eng, fn, rd, wr, dur, lat=0.0, kind="c", ext=None):
        reads = []
        writes = []
        for r in rd:
            if isinstance(r, dict):
                (writes if r["ps"] and "share" not in r else reads).append((r["reg"][0], 0, 512) if r["ps"] else r["reg"])
                if "off" in r:
                    reads.append(r["off"]["reg"])
        for r in wr:
            writes.append((r["reg"][0], 0, 512) if r["ps"] else r["reg"])
            if "off" in r:
                reads.append(r["off"]["reg"])
        ops.append({"eng": eng, "fn": fn, "rd": reads, "wr": writes, "dur": dur, "lat": lat, "kind": kind, "ext": ext})
        return len(ops) - 1

    def val(x):
        return x["ap"] if isinstance(x, dict) else x

    def vcost(out, ins, rate):
        if "off" in out:
            return 50 + out["n"] * SCA * CY
        if "off" in ins[0]:
            return 50 + out["n"] * GAT * CY
        return 20 + max(64, out["n"] * rate) * CY

    def half(*s):
        return 0.5 if all(x["w"] == 2 for x in s) else 1.0

    def cp(out, i):
        add("v", lambda g: g.vector.tensor_copy(out["ap"], i["ap"]), [i], [out], vcost(out, [i], half(out, i)))

    def ts(out, i, s1, op0, s2=None, op1=None):
        if op1 is None:
            fn = lambda g: g.vector.tensor_scalar(out["ap"], i["ap"], val(s1), None, op0)
        else:
            fn = lambda g: g.vector.tensor_scalar(out["ap"], i["ap"], val(s1), val(s2), op0, op1)
        add("v", fn, [i, s1, s2], [out], vcost(out, [i], half(out, i)))
        form = {(A.mult, None): (s1, 0.0), (A.add, None): (1.0, s1), (A.mult, A.add): (s1, s2)}.get((op0, op1))
        if form and "off" not in out and i["nm"] not in ("PI", "PU", "RV"):
            alt = lambda g: g.scalar.activation(out["ap"], i["ap"], F.Identity, bias=val(form[1]), scale=val(form[0]))
            ops[-1]["alt"] = {"v": (fn, ops[-1]["dur"]), "s": (alt, 20 + vcost(out, [i], 1.0))}

    def tt(out, i0, i1, op, more=()):
        add("v", lambda g: g.vector.tensor_tensor(out["ap"], i0["ap"], i1["ap"], op), [i0, i1] + list(more), [out],
            vcost(out, [i0], 1.0 if i0["ps"] or i1["ps"] else 2.0))

    def scan(out, d0, d1, op0, op1, init=0.0):
        add("v", lambda g: g.vector.tensor_tensor_scan(out["ap"], d0["ap"], d1["ap"], init, op0, op1), [d0, d1], [out],
            vcost(out, [d0], half(out, d0, d1)))

    def ms(out, c):
        add("v", lambda g: g.vector.memset(out["ap"], c), [], [out], vcost(out, [out], half(out)))
        if "ones" in place and out["n"] <= 256 and out["nm"] in ("PF", "PB", "PH", "X", "B", "UT", "XB0", "XB1"):
            one = buf("PB", "ones", out["n"])
            alt = lambda g: g.scalar.activation(out["ap"], one["ap"], F.Identity, bias=0.0, scale=c)
            if one["reg"][:2] != out["reg"][:2]:
                ops[-1]["rd"].append(one["reg"])
                ops[-1]["alt"] = {"v": (ops[-1]["fn"], ops[-1]["dur"]), "s": (alt, 20 + vcost(out, [out], 1.0))}
        if abs(c) < 2 ** 24 and out["nm"] != "PH":
            alt = lambda g: g.iota(out["ap"], [[0, out["n"]]], int(c), 0, allow_small_or_imprecise_dtypes=True)
            ops[-1]["alt"] = dict(ops[-1].get("alt", {"v": (ops[-1]["fn"], ops[-1]["dur"])}), g=(alt, 130 + 2 * out["n"] * CY))

    def act(out, i, func, bias=None, scale=None, acc=None, more=(), unit=False):
        kw = {}
        if bias is not None:
            kw["bias"] = val(bias)
        if scale is not None:
            kw["scale"] = val(scale)
        if acc is not None:
            kw["accum_out"] = acc["ap"]
        add("s", lambda g: g.scalar.activation(out["ap"], i["ap"], func, **kw), [i, bias, scale],
            [out] + ([acc] if acc else []) + list(more), 20 + vcost(out, [i], 1.0))
        o, x, fn = out["ap"], i["ap"], None
        if acc is not None:
            if func == F.Copy:
                fn = lambda g: g.vector.tensor_reduce(acc["ap"], x, AxisListType.X, A.add)
        elif func in (F.Copy, F.Silu):
            fn = lambda g: g.vector.tensor_copy(o, x)
        elif func == F.Identity:
            fn = lambda g: g.vector.tensor_scalar(o, x, 1.0 if scale is None else val(scale), val(bias), A.mult, A.add)
        elif func == F.Relu and scale is None:
            fn = lambda g: g.vector.tensor_scalar(o, x, val(bias), 0.0, A.add, A.max)
        elif func == F.Sign and unit:
            fn = lambda g: g.vector.tensor_scalar(o, x, -1.0, 1.0, A.max, A.min)
        if fn:
            ops[-1]["alt"] = {"s": (ops[-1]["fn"], ops[-1]["dur"]), "v": (fn, vcost(out, [i], half(out, i)))}

    def mv(out, i):
        act(out, i, F.Copy)

    def lin(out, i, scale, bias):
        act(out, i, F.Identity, bias=bias, scale=scale)

    def mm(out, l, r, start, stop, join=False):
        add("p", lambda g: g.tensor.matmul(out["ap"], l["ap"], r["ap"], start, stop), [l, r], [out],
            max(64, r["n"]) * PEC * (4 if l["w"] == 4 else 1))
        if join:
            b = ops.pop(); x = ops[-1]
            x["fn"] = lambda g, f1=x["fn"], f2=b["fn"]: (f1(g), f2(g))[1]
            x["rd"] = sorted(set(x["rd"] + b["rd"])); x["wr"] = sorted(set(x["wr"] + b["wr"])); x["dur"] += b["dur"]

    def iota(out, pat, base, cm, small=True):
        if small:
            fn = lambda g: g.iota(out["ap"], pat, base, cm, allow_small_or_imprecise_dtypes=True)
        else:
            fn = lambda g: g.iota(out["ap"], pat, base, cm)
        add("g", fn, [], [out], 130 + 2 * out["n"] * CY)

    def asel(out, i, pat, op, base, cm, fill=0.0):
        add("g", lambda g: g.affine_select(out["ap"], i["ap"], pat, op, fill, base, cm), [i], [out], 170 + 2 * out["n"] * CY)

    def dma(q, out, i, rd, wr, lat):
        if q == "y":
            fn = lambda g: g.sync.dma_start(out, i)
        else:
            fn = lambda g: g.scalar.dma_start(out, i)
        add(q, fn, rd, wr, 60.0, lat, "d")

    fb = lambda k, n=256: buf("PF", k, n)
    bb = lambda k, n=256: buf("PB", k, n)
    hb = lambda k, n=256: buf("PH", k, n)
    ib = lambda k, n=256: buf("PI", k, n)
    ub = lambda k, n=256: buf("PU", k, n)
    P = lambda k, a=0, b=256: R(k, a, b)
    L = lambda r: sub(r, 0, 256)
    Bw = R("B", 0, TW)
    XBw = [R("XB0", 0, TW), R("XB1", 0, TW)]
    Xw = R("X", 0, 2064)
    Dw = R("D", 0, 2064)
    UTw = R("UT", 0, 2064)

    for h in range(2):
        dma("ys"[h], T.LB[:, h], T.board[h::2, :], [], [RX("LB", None, 128 * h, 128 * h + 128, 128)], 2200)
    dma("y", T.LN[:], T.board[:], [], [R("LN", 0, 256)], 2600)
    dma("y", T.X[:, 0:2048], T.xs[:], [], [R("X", 0, 2048)], 4800)
    dma("y", T.D[:, 0:2048], T.ds[:], [], [R("D", 0, 2048)], 8000)
    for i in range(16):
        dma("y", T.HM[i::16, 16:528], T.hm[:, 512 * rank:512 * rank + 512], [], [RX("HM", None, 3000 + i, 3001 + i, 1)], 9000)
    HMw = R("HM", 0, 528)
    HMall = RX("HM", None, 3000, 3016, 1)

    ONES = bb("ones"); ms(ONES, 1.0)
    O128 = sub(ONES, 0, 128)
    IOT = bb("iot"); iota(IOT, [[1, 256]], 0, 0)
    PI_ = ib("pi", 1); iota(PI_, [[0, 1]], 0, 1, False)
    J = bb("J"); iota(J, [[0, 16], [1, 16]], 0, 0)
    J4 = bb("J4", 64); iota(J4, [[0, 16], [1, 4]], 0, 0)
    tb = bb("tb", 128); BLK = bb("blk", 128); TRI = bb("tri", 128)
    ROW15 = bb("row15", 128); IDB = bb("idb", 128)
    gp = [[-16, 8], [0, 16]]
    asel(tb, O128, gp, A.is_ge, 0, 1)
    asel(BLK, tb, [[16, 8], [0, 16]], A.is_ge, 15, -1)
    asel(TRI, BLK, [[1, 128]], A.is_ge, 0, -1)
    asel(ROW15, O128, gp, A.is_equal, -15, 1)
    asel(IDB, O128, [[-1, 128]], A.is_equal, 0, 1)
    OH = hb("oh", 512); ms(OH, 1.0)
    ROWS = hb("rows", 2048)
    for b in range(4):
        asel(sub(ROWS, 512 * b, 512 * b + 512), OH, [[-1, 4], [-16, 8], [0, 16]], A.is_equal, -4 * b, 1)
    DUMP = fb("dump", 64); iota(DUMP, [[1, 64]], 4352, 0)
    for k in range(2):
        iota(R("UT", 1024 * k, 1024 * k + 1024), [[8192, 1024]], 8192 * 1024 * k, 0)
    ms(R("UT", 2048, 2064), 2048.0 * 8192)
    RI = ib("ri", 1); ts(RI, PI_, 15, A.bitwise_and)
    RF = fb("rf", 1); cp(RF, RI)
    i2 = ib("i2", 1); ts(i2, RI, 2, A.arith_shift_right)
    RQ4 = fb("rq4", 1); cp(RQ4, i2)
    i3 = ib("i3", 1); ts(i3, RI, 3, A.bitwise_and)

    def picker(key, jt, col, last, n):
        c1 = fb(key + "c1", 1); ts(c1, col, 1.0, A.add)
        sc = fb(key + "sc", 1); ts(sc, col, last - 0.5, A.is_gt, 1.0 / MUL, A.max)
        x = bb(key + "x", n); y = bb(key + "y", n); o = bb(key, n)
        ts(x, jt, col, A.not_equal); ts(y, jt, c1, A.is_equal, MUL, A.mult); tt(o, x, y, A.max)
        return o, sc, x
    SP, SCL, NOT16 = picker("sp", J, RF, 15, 256)
    SQ, SCQ, NOT4 = picker("sq", J4, RQ4, 3, 64)
    SCL8 = fb("scl8", 1); ts(SCL8, SCL, 1.0 / 8192, A.mult)
    SCN = fb("scn", 1); ts(SCN, SCL, -1.0, A.mult)
    JH = hb("jh"); ts(JH, IOT, 0.5, A.add)
    C256 = bb("c256"); ms(C256, 256.0)
    CBIG = bb("cbig"); ms(CBIG, BIG)
    CE = fb("ce"); ms(CE, 2048.0)

    def scaled(key, src, c, pool="PB"):
        o = buf(pool, key, 128); ts(o, src, c, A.mult); return o

    def quad(key, src, c, pool):
        y = buf(pool, key, 132); ms(y, 0.0)
        ts(sub(y, 3, 131, 4), sub(src, 3, 128, 4), c, A.mult)
        return [sub(y, 3 - r, 131 - r) for r in range(4)]

    def comb(key, src, pool):
        y = buf(pool, key, 144); ms(y, 0.0); cp(sub(y, 15, 143, 16), sub(src, 0, 128, 16))
        return [sub(y, 15 - k, 143 - k) for k in range(16)]

    def rows(key, src):
        y = bb(key, 2048); x = bb(key + "4", 512)
        for k in range(4):
            src(sub(x, 128 * k, 128 * k + 128))
        for b in range(4):
            asel(sub(y, 512 * b, 512 * b + 512), x, [[-1, 4], [-16, 8], [0, 16]], A.is_equal, -4 * b, 1)
        return [sub(y, 128 * k, 128 * k + 128) for k in range(16)]
    ROW0, ROW1 = sub(ROWS, 0, 128), sub(ROWS, 128, 256)
    Q1 = quad("q1", BLK, 1.0, "PB"); Q16 = quad("q16", BLK, 16.0, "PB"); Q256 = quad("q256", BLK, 256.0, "PB")
    Q15 = quad("q15", ROW15, 1.0, "PB")
    if "S" in MODES[0] + MODES[1]:
        BH5 = scaled("bh5", BLK, 0.5); ZK5 = comb("zk5", BH5, "PB")
    QH = quad("qhh", BLK, 1.0, "PH"); Q0 = quad("q0", ROW0, 1.0, "PH") if "w" not in DIRECT else None
    QH5 = quad("qh5", BLK, 0.5, "PH"); QB5 = quad("qb5", BLK, 0.5, "PB") if NLS else None
    ZK = comb("z", BLK, "PB"); Z15 = comb("z15", ROW15, "PB"); ZH = comb("zh", BLK, "PH")
    B16 = scaled("b16", BLK, 16.0); B256 = scaled("b256", BLK, 256.0)
    NB = scaled("nb", BLK, -65536.0); BP = scaled("bp", BLK, 16384.0)
    IDN = scaled("idn", IDB, -1.0)
    BLKh = scaled("bh", BLK, 1.0, "PH"); IDH = scaled("idh", IDB, 1.0, "PH")
    ZM = bb("zm", 128); asel(ZM, scaled("zt", TRI, -16384.0), [[-1, 128]], A.not_equal, 0, 1, 16384.0)
    ZC = fb("zc", 1); ts(ZC, RF, 1.0, A.add, -16384.0, A.mult)
    ZD = fb("zd", 1); ts(ZD, RF, -16384.0, A.mult)
    TRS = bb("trs", 128); asel(TRS, NB, [[1, 128]], A.is_gt, 0, -1)
    BK = scaled("bk", BLK, 16000.0); IDF = scaled("idf", IDB, 1.0, "PF")
    IDM = scaled("idm", IDB, -1.0, "PF"); IDL = scaled("idl", IDB, -2.0 ** 23, "PF")
    LK = rows("LK", lambda o: ts(o, ZM, 2.0, A.mult))
    LT = rows("LT", lambda o: ts(o, TRI, -1.0 / BIG, A.mult))
    THR = fb("thr", 1); ts(THR, RF, 4.0, A.min, -512.0 * 8192, A.mult); ts(THR, THR, 4096.0, A.add)
    up = bb("up", 128); ms(up, 32768.0); dn = bb("dn", 128); ms(dn, -32768.0)
    BI1 = bb("bi1", 128); asel(BI1, up, [[-16, 8], [0, 4], [-1, 4]], A.is_equal, 0, 1)
    BI2 = bb("bi2", 128); asel(BI2, dn, [[-16, 8], [0, 4], [-1, 4]], A.is_equal, -1, 1)
    AB = bb("ab", 128); asel(AB, dn, gp, A.is_equal, -4, 1)
    MD = bb("md"); ts(MD, NOT16, -FAR, A.mult, 8192.0, A.add)
    MN = bb("mn", 64); ts(MN, sub(NOT16, 0, 64), -FAR, A.mult)
    MQ = bb("mq", 64); ts(MQ, NOT4, -FAR, A.mult, 286720.0, A.add)
    MK = fb("mk", 64); ts(MK, sub(NOT16, 0, 64), -4097.0, A.mult, 4096.0, A.add)
    DR = bb("dr"); ms(DR, FAR); ms(sub(DR, 0, 256, 16), -2 * FAR)
    DQ = fb("dq", 64); ms(DQ, FAR)
    DZ = fb("dz"); ms(DZ, FAR)
    j16 = fb("j16", 4); ts(j16, sub(J, 0, 4), 16.0, A.mult, RF, A.add)
    DY = fb("dy", 64); ms(DY, FAR); ts(sub(DY, 0, 64, 16), j16, -1.0 / 8192, A.mult, 2048.0 - 4416.0 / 8192, A.add)
    VC = fb("vc", 4); ts(VC, j16, 2.0, A.mult, 256.0, A.add)
    if NLS:
        ts(sub(VC, 0, NLS), sub(VC, 0, NLS), 1.0, A.add)
    IO2 = hb("io2"); ts(IO2, IOT, 2.0, A.mult, -319.0, A.add)
    f3 = fb("f3", 1); cp(f3, i3)
    IOQ = bb("ioq", 64); ts(IOQ, sub(IOT, 0, 64), 4.0, A.mult, f3, A.add)
    MP = fb("mp", 64); ts(MP, sub(NOT16, 0, 64), -1.0, A.mult, 1.0, A.add)
    DS = bb("dsum", 64); ts(DS, sub(J, 0, 64), 1.0, A.min)
    SLB = fb("slb", 1); ts(SLB, RF, -2.0, A.mult, -1.0, A.add)
    RM = bb("rm", 2048)
    if RMG:
        OB = bb("ob", 512); ms(OB, 1.0)
        for j in range(4):
            asel(sub(RM, 512 * j, 512 * j + 512), OB, [[-1, 32], [0, 16]], A.is_equal, -32 * j, 1)
    else:
        JM = bb("jm", 512); iota(JM, [[1, 32], [0, 16]], 0, 0)
        PF_ = fb("pff", 1); cp(PF_, PI_)
        PM = fb("pm", 4); ts(PM, sub(J, 0, 4), -32.0, A.mult, PF_, A.add)
        for j in range(4):
            ts(sub(RM, 512 * j, 512 * j + 512), JM, sub(PM, j, j + 1), A.is_equal)
    ES = bb("es", 272); ms(sub(ES, 0, 16), 0.0)
    T3 = bb("t3", 272); ms(sub(T3, 256, 272), 512.0)
    SC = bb("sc", 32); ms(sub(SC, 16, 32), 512.0)
    PAY = fb("pay", 272); ms(sub(PAY, 256, 272), 2048.0 - 8192.0)
    ms(R("X", 2048, 2064), BIG); ms(R("D", 2048, 2064), 0); ms(R("HM", 0, 16), 1 << 20)
    act(R("B", 4096, 4352), CE, F.Silu); ops[-1].pop("alt"); ops[-1]["dur"] += 1400
    ms(R("B", 4352, TW), 0.0)
    for x in ("XB0", "XB1"):
        ms(R(x, 4096, 4288), BIG); ms(R(x, 4288, TW), BIG)

    def wrap(key, src, n, scale):
        s = fb("w_" + key, n); scan(s, sub(SP, 0, n), src, A.mult, A.add)
        u = ub("u_" + key, n // 16); lin(u, sub(s, 15, n, 16), scale, 0.25)
        return u

    def qmm(bank, terms, first=True, last=True, lo=0, hi=256):
        for x, (l, r) in enumerate(terms):
            for k in range(4):
                mm(P(bank, lo // 4, hi // 4), l[k], sub(r, lo + k, hi, 4), first and x == 0 and k == 0, last and x == len(terms) - 1 and k == 3, k > 0)

    def zmm(bank, l, r, lo=0, hi=256):
        for k in range(16):
            mm(P(bank, lo // 16, hi // 16), l[k], sub(r, lo + k, hi, 16), k == 0, k == 15, k % 8 > 0)

    def qwrap(key, bank, plus=0.25):
        s = fb("w_" + key, 64); scan(s, SQ, P(bank, 0, 64), A.mult, A.add)
        u = ub("u_" + key, 16); lin(u, sub(s, 3, 64, 4), SCQ, plus)
        return u

    WI = ib("wi")
    for h in range(2):
        cp(RX("CV", T.CV[:, :, 16 * h:16 * h + 16], 0, 256, 128), RX("LB", T.LB[:, h], 128 * h, 128 * h + 128, 128))
    for b in range(8):
        o = sub(WI, b, 256, 8); i = RX("CV", T.CV[:, b, :], 0, 256, 32)
        o["reg"] = ("PI", WI["a"] + 32 * b, WI["a"] + 32 * b + 32)
        add("v", lambda g, o=o, i=i: g.vector.transpose(o["ap"], i["ap"]), [i], [o], 90.0)
    WH = hb("wh"); mv(WH, R("LN", 0, 256))
    for r in range(8):
        bank = ("pA", "pZ", "pK", "pC")[r % 4]
        for h in range(2):
            mm(P(bank, 256 * h, 256 * h + 256), sub(ROWS, 256 * r + 128 * h, 256 * r + 128 * h + 128), WH, True, True, h > 0)
        mv(R("B", 512 * r, 512 * r + 512), P(bank, 0, 512))
    w1 = ib("w1"); ts(w1, WI, 2049, A.bitwise_and)
    Fm = bb("fm"); ts(Fm, w1, 0.0, A.is_equal)
    for e in (1, 0):
        u = ib("oa%d" % e); lin(u, WI, 4097.0, 4096.0 * e)
        v = ib("oc%d" % e); ts(v, u, 8191, A.bitwise_and)
        oo = ub("o%d" % e); ts(oo, v, 2048.0, A.min)
        w = XBW[e]
        for c in range(256 // w):
            mv(R("XB%d" % e, 16 * w * c, 16 * w * c + 16 * w), ind(Xw, sub(oo, w * c, w * c + w)))

    def tiles(t):
        n = str(t & 1)
        return fb("cs" + n, 320), fb("ca" + n, 320), bb("cx" + n, 320), ib("cq" + n, 320), ub("qu" + n, 320)

    def targets(q2, qu, off, at, n, key):
        q = ib("qa" + key, n); tt(q, ind(Dw, off), at, A.add)
        ts(q2, q, 4095, A.bitwise_and)
        mv(qu, q2)

    def select(t):
        CS, CA, CX, CQ, QU = tiles(t)
        E = sub(ES, 16, 272)
        scan(E, P("pW"), C256, A.add, A.min)
        mm(P("pE", 0, 16), IDB, sub(MN, 0, 16), True, False); mm(P("pE", 0, 16), ROW15, sub(E, 15, 256, 16), False, True)
        s1 = fb("s1", 1)
        add("v", lambda g: g.vector.tensor_reduce(s1["ap"], P("pE", 0, 16)["ap"], AxisListType.X, A.max, negate=True), [P("pE", 0, 16)], [s1], 20 + 64 * CY)
        for k in range(16):
            mm(P("pX", 0, 16), Z15[k], sub(E, k, 256, 16), k == 0, k == 15, k % 8 > 0)
        mv(sub(SC, 0, 16), P("pX", 0, 16))
        mm(P("pW"), IDB, E, True, False); mm(P("pW"), IDN, sub(ES, 15, 271), False, False, True)
        mm(P("pW"), ROW15, sub(ES, 15, 271), False, True, True)
        mv(L(T3), P("pW"))
        c1 = bb("c1"); ts(c1, JH, s1, A.add, 0.0, A.is_ge)
        if "1" in DIRECT:
            zmm("pE", ZK, c1)
            u1 = ub("u_l1", 16); mv(u1, P("pE", 0, 16))
        else:
            qmm("pE", [(Q1, c1)])
            u1 = qwrap("l1", "pE")
        iv = bb("iv"); act(iv, IOT, F.Relu, bias=s1)
        qmm("pX", [(Q16, c1)], True, False)
        c2 = bb("c2"); tt(c2, ind(SC, u1), JH, A.is_le)
        qmm("pX", [(Q1, c2)], False)
        u2 = qwrap("l2", "pX")
        qmm("pE", [(Q256, c1), (Q15, iv), (Q16, c2)], True, False)
        o = P("pW")
        mm(o, B256, c1, True, False); mm(o, ROW15, iv, False, False); mm(o, B16, c2, False, False)
        c3 = bb("c3"); tt(c3, ind(T3, u2), JH, A.is_le)
        qmm("pE", [(Q1, c3)], False)
        u = qwrap("l3%d" % (t & 1), "pE")
        mm(o, BLK, c3, False, True)
        mv(L(CS), o)
        lin(L(CA), ind(Bw, u), 8192.0, 0.0)
        au = wrap("a", L(CA), 256, SCL8)
        targets(L(CQ), L(QU), au, L(CS), 256, "l")
        mv(L(CX), ind(XBw[t & 1], u) if t else ind(Xw, au))
        return u

    def rivals(key, wf, c2, start):
        mm(P("pC"), IDH, key, False, False)
        for c in range(16):
            n = 256 - 16 * c
            o = RX("FC", T.FC[:, c, 0:n], 256 * c, 256 * c + n, n)
            if c2 is None:
                ts(o, sub(key, 16 * c, 256), wf(c), A.is_equal)
            else:
                ts(o, sub(key, 16 * c, 256), wf(c), A.subtract, c2, A.is_equal)
            if c < 15:
                mm(P("pC", 16 * c + 16, 256), NB, RX("FC", T.FC[:, c, 16:n], 256 * c + 16, 256 * c + n, n - 16), False, False)
            if c in (11, 15):
                a = 0 if c == 11 else 12
                mm(P("pC", 16 * a, 16 * c + 16), TRS, RX("FC", T.FC[:, a:c + 1, 0:16], 256 * a, 256 * c + 16, 16 * (c + 1 - a)), False, c == 15)
        s = fb("w_riv"); scan(s, start, P("pC"), A.min, A.max, FAR)
        return sub(s, 15, 256, 16)

    mm(P("pW"), TRI, Fm, True, True)
    sU = select(0)
    srcU = None
    for t in range(4):
        e = t & 1
        XE_, XO = XBw[e], XBw[1 - e]
        CS, CA, CX, CQ, QU = tiles(t)
        nc = 320 if t else 256
        qh = hb("qh", 320); ts(sub(qh, 0, nc), sub(QU, 0, nc), -2048.0, A.add)
        if t == 0:
            s, a, Xa = L(CS), L(CA), L(CX)
            for o in (sub(DQ, 0, 64, 4), sub(DZ, 0, 256, 16)):
                ts(o, sU, -1.0, A.mult, KOFF, A.add)
        else:
            s, a, Xa = fb("s"), fb("a"), bb("x")
            mv(s, ind(CS, srcU)); mv(a, ind(CA, srcU)); mv(Xa, ind(CX, srcU))
            sU = wrap("s", s, 256, SCL)
            for o in (sub(DQ, 0, 64, 4), sub(DZ, 0, 256, 16)):
                lin(o, sub(fb("w_s"), 15, 256, 16), SCN, KOFF)
        parts = PARTS[t]
        GE = bb("ge"); act(GE, a, F.Sign, bias=THR)
        mode = MODES[min(t, 1)]
        for lo, hi in LAY[min(t, 1)]:
            for k in range(16):
                asel(dict(R("XR", 16 * lo + k, 16 * hi, 16), reg=("XR", 16 * lo + k, 16 * lo + k + 1)), sub(CX, lo, hi), [[0, hi - lo]], A.is_ge, 0, 0)
        XT = bb("xt", 384)
        blocks = [(0, 0), (128, 128), (256, 192)]
        for h, (lo, at0) in enumerate(blocks):
            if mode[2 * h:2 * h + 2].strip("F"):
                bank = P(("pE", "pX")[h % 2], 0, 128)
                mm(bank, sub(CX, at0, at0 + 128), IDB, True, True)
                mv(sub(XT, 128 * h, 128 * h + 128), bank)
        sg = bb("sg", 320); mx = hb("mx"); wa = fb("wa", 64); atU = ub("atU", 16); key = hb("key"); at = fb("at"); who = hb("who")
        whoU = ub("whoU", 16); Wu = ub("wu"); qw = hb("qwh"); my = fb("my", 320)

        def first(lo, hi):
            S = lambda x, d=1: sub(x, lo // d, hi // d)
            mm(P("pS", lo, hi), BK, S(ONES), True, False)
            mm(P("pK", lo // 4, hi // 4), IDB, S(MQ, 4), True, False)
            if t:
                lin(S(mx), ind(my, S(srcU, 16)), 1.0, -16384.0)
            qmm("pK", [(QH, mx)], False, True, lo, hi)
            mm(P("pS", lo, hi), BLKh, S(mx), False, True)
            scan(S(wa, 4), S(DQ, 4), P("pK", lo // 4, hi // 4), A.min, A.max, FAR)
            act(S(atU, 16), sub(wa, lo // 4 + 3, hi // 4, 4), F.Abs, bias=-KOFF)
            lin(S(key), P("pS", lo, hi), 1.0, -10240.0)
            tt(S(at), P("pS", lo, hi), S(s), A.max)
            mv(S(who), ind(Bw, S(atU, 16)))
            if "w" in DIRECT:
                zmm("pK", ZH, who, lo, hi)
                lin(S(whoU, 16), P("pK", lo // 16, hi // 16), 1.0 / 16, 0.0)
            else:
                qmm("pK", [(Q0, who)], True, True, lo, hi)
                x = fb("w_who", 64); scan(S(x, 4), S(SQ, 4), P("pK", lo // 4, hi // 4), A.mult, A.add)
                lin(S(whoU, 16), sub(x, lo // 4 + 3, hi // 4, 4), SCQ, 0.25)
            targets(S(ib("qw")), S(Wu), S(whoU, 16), S(at), hi - lo, "w%d" % lo)
            ts(S(qw), S(Wu), -2048.0, A.add)
        todo = []
        for lo, hi in parts:
            mine = [c for c in list(range(lo // 32, hi // 32)) + list(range(8, nc // 32)) if c not in todo]
            todo += sorted(mine, key=lambda c: (mode[c // 2] == "F", c)) + [(lo, hi)]
        for c in todo:
            if isinstance(c, tuple):
                spans = [c] if c[0] or not t else [(0, 320)] if c[1] == 256 else [c, (256, 320)]
                for lo, hi in spans:
                    act(sub(sg, lo, hi), P("pA", lo, hi), F.Sign, bias=-8.5)
                if c[1] == 256 and (CUT == 0 or t == 0):
                    ops[-1]["cut"] = 1
                for lo, hi in spans:
                    mm(P("pZ", lo, hi), IDH, sub(qh, lo, hi), True, False)
                    mm(P("pZ", lo, hi), ZM, sub(sg, lo, hi), False, True)
                    if t:
                        act(sub(my, lo, hi), P("pZ", lo, hi), F.Relu, bias=ZD)
                    else:
                        ts(sub(mx, lo, hi), P("pZ", lo, hi), ZC, A.add, -16384.0, A.max)
                first(*c)
                continue
            cm = R("CM", 512 * c, 512 * c + 512); src = ind(XO, sub(QU, 32 * c, 32 * c + 32))
            kind = mode[c // 2]
            if kind == "F":
                lo = [x[0] for x in LAY[min(t, 1)] if x[0] <= 32 * c < x[1]][0]
                tt(cm, src, dict(R("XR", 512 * c, 512 * c + 512), reg=("XR", 16 * lo, 16 * lo + 16)), A.is_lt)
            else:
                xe = R("XE", 512 * c, 512 * c + 512); bank = P(("pE", "pX")[c % 2], 0, 512)
                h = c // 4; j = (32 * c - blocks[h][1]) // 32
                mm(bank, sub(XT, 128 * h, 128 * h + 128), sub(RM, 512 * j, 512 * j + 512), True, kind != "S")
                if kind == "P":
                    mv(xe, bank)
                    tt(cm, src, xe, A.is_lt)
                elif kind == "U":
                    mv(xe, src)
                    tt(cm, xe, bank, A.is_lt)
                else:
                    mv(xe, src)
                    mm(bank, IDN, xe, False, True)
                    act(cm, bank, F.Sign, bias=-2.0 ** -110)
            if c % 2:
                cm = R("CM", 512 * c - 512, 512 * c + 512); o = P("pA", 32 * c - 32, 32 * c + 32)
                if kind == "S":
                    mm(o, BH5, sub(ONES, 0, 64), True, False)
                for k in range(16):
                    mm(o, (ZK5 if kind == "S" else ZK)[k], sub(cm, k, 1024, 16), k == 0 and kind != "S", k == 15, k % 8 > 0)
        mm(P("pC"), IDB, MD, True, False); mm(P("pC"), AB, GE, False, False)
        for lo, hi in parts:
            mm(P("pZ", lo, hi), IDH, sub(qw, lo, hi), lo == 0, False)
        x = rivals(key, lambda c: sub(wa, 4 * c + 3, 4 * c + 4), -KOFF - 2048.0, DZ)
        baseU = ub("baseU", 16); act(baseU, x, F.Abs, bias=-KOFF)
        EN = bb("en"); act(EN, P("pC"), F.Sign, unit=True)
        if t < 3:
            cp(ind(XO, baseU), CBIG)
        basen = fb("basen", 16); ts(basen, baseU, -1.0, A.mult, KOFF, A.add)
        mm(P("pC"), IDB, MD, True, False); mm(P("pC"), AB, GE, False, False)
        o = P("pA")
        mm(o, BI1, GE, True, False); mm(o, BI2, GE, False, False); mm(o, IDH, key, False, False); mm(o, BP, EN, False, True)
        fl = bb("fl"); act(fl, o, F.Sign, bias=3000.0 + 14 * 16384.0 - 65536.0)
        mm(P("pS"), IDF, a, True, False); mm(P("pS"), IDH, who, False, True)
        mv(L(PAY), P("pS"))
        pf = hb("pf"); scan(pf, fl, ONES, A.add, A.add)
        acc = fb("acc", 4)
        for j in range(4):
            o = P(("pA", "pS")[j % 2], 256, 512)
            mm(o, sub(ROWS, 128 * j, 128 * j + 128), pf, True, True)
            act(bb("junk%d" % j), o, F.Sign, bias=SLB, acc=sub(acc, j, j + 1))
        ix = ub("ix", 4); lin(ix, acc, -0.5, 128.25)
        G = fb("g", 64); SD = fb("sd", 64)
        tt(G, ind(PAY, ix), MP, A.mult)
        scan(SD, sub(DS, 0, 64), G, A.mult, A.add)
        c = 16 * t + 4 * rank
        mine = dict(R("RV", c, c + 4), reg=("RV", 16 * t, 16 * t + 16))
        mv(mine, sub(SD, 15, 64, 16))
        snd = add("g", ("send", t), [mine], [], 300.0, FLIGHT, "r")
        c = 0
        for w in MCH:
            act(R("CM", 16 * c, 16 * (c + w)), ind(Bw, sub(Wu, c, c + w)), F.Relu, bias=-2047.0)
            c += w
        mm(P("pZ"), BP, EN, False, False)
        for c in range(4):
            cm = R("CM", 1024 * c, 1024 * c + 1024)
            for k in range(16):
                mm(P("pZ", 64 * c, 64 * c + 64), LK[k], sub(cm, k, 1024, 16), False, c == 3 and k == 15, k % 8 > 0)
        for u in (sU, baseU):
            for lo, hi in SPL[0]:
                act(ind(Bw, sub(u, lo, hi)), sub(CE, 0, 16 * (hi - lo)), F.Silu)
        if t < 3:
            mm(P("pW"), TRI, ONES, True, False)
            for k in range(16):
                mm(P("pW"), LT[k], R(XO["nm"], k, 4096, 16), False, k == 15, k % 2 > 0)
            select(t + 1)
            for lo, hi in SPL[1]:
                cp(ind(XE_, sub(sU, lo, hi)), sub(CBIG, 0, 16 * (hi - lo)))
        m2 = hb("m2"); ts(m2, P("pZ"), 14 * 16384.0 - 32768.0, A.add, -16384.0, A.max)
        mm(P("pS"), BLKh, m2, True, True)
        for k in range(16):
            mm(P("pK", 0, 16), ZH[k], sub(m2, k, 256, 16), k == 0, k == 15, k % 8 > 0)
        k2 = hb("k2"); lin(k2, P("pS"), 1.0, 245760.0)
        x = rivals(k2, lambda c: dict(P("pK", c, c + 1), share=1), 245760.0, DR)
        y = fb("ey", 16); tt(y, x, basen, A.max)
        endU = ub("endU", 16); act(endU, y, F.Abs, bias=-KOFF)
        if t < 3:
            cp(ind(XE_, endU), Xa)
        if t < 3 or not LAST:
            ts(ind(Bw, endU), a, 1.0 / 8192, A.mult, 0.0, A.add)
        CS, CA, CX, CQ, QU = tiles(t + 1)
        raU = ub("raU", 4); rv = dict(R("RV", 16 * t + rank, 16 * t + 16, 4), reg=("RV", 16 * t, 16 * t + 16))
        add("v", lambda g, o=raU, i=rv: g.vector.tensor_scalar(o["ap"], i["ap"], 1.0 / 8192, 16.1 - 512.0 * rank, A.mult, A.add),
            [rv], [raU], 90.0, ext=("ar%d" % t, snd))
        pi = ib("rpi", 4); add("v", lambda g, o=pi, i=rv: g.vector.tensor_copy(o["ap"], i["ap"]), [rv, raU], [pi], 90.0)
        rvv = ib("rvv", 4); ts(rvv, pi, 8191, A.bitwise_and)
        rvU = ub("rvU", 4); mv(rvU, rvv)
        RS, RA = sub(CS, 256, 320), sub(CA, 256, 320)
        tt(RS, ind(HMw, raU), DUMP, A.min, [HMall])
        hU = wrap("h", RS, 64, SCL)
        mv(RA, ind(UTw, rvU))
        hc = fb("hc", 64); lin(hc, RS, -1.0 / 8192, 2048.0)
        if t < 3:
            mv(sub(CX, 256, 320), ind(Xw, rvU))
            targets(sub(CQ, 256, 320), sub(QU, 256, 320), rvU, RS, 64, "r")
        if CUT == 1 and t < 3:
            ops[-1]["cut"] = 1
        hv = fb("hv", 64)
        if t < 3:
            hz = fb("hz", 64); tt(hz, ind(Bw, hU), hc, A.min)
            mm(P("pW", 0, 64), IDB, MN, True, False); mm(P("pW", 0, 64), IDF, hz, False, True)
            scan(hv, DY, P("pW", 0, 64), A.min, A.max, FAR)
        else:
            hm_ = fb("hmk", 64); tt(hm_, hc, MK, A.min)
            hy = fb("hy", 64); tt(hy, ind(Bw, hU), hm_, A.min)
            scan(hv, DY, hy, A.min, A.max, FAR)
        hkU = ub("hkU", 4); lin(hkU, sub(hv, 15, 64, 16), -8192.0, 2.0 ** 24)
        ts(ind(Bw, hkU), RA, 1.0 / 8192, A.mult, 0.0, A.add)
        if t == 3 and LAST:
            ts(ind(Bw, endU), a, 1.0 / 8192, A.mult, 0.0, A.add)
        if t < 2:
            cp(ind(XO, hkU), sub(CX, 256, 320))
        if t < 3:
            hf = fb("hf", 4); lin(hf, sub(fb("w_h", 64), 15, 64, 16), SCL, -0.25)
            hn = fb("hn", 4); lin(hn, sub(fb("w_h", 64), 15, 64, 16), SCL8, -2048.0)
            ac2 = fb("ac2", 4); ac3 = fb("ac3", 4)
            for j in range(4):
                act(bb("junk%d" % j), L(CS), F.Sign, bias=sub(hf, j, j + 1), scale=-1.0, acc=sub(ac2, j, j + 1))
            for j in range(4):
                act(bb("jun%d" % j, 64), hz, F.Sign, bias=sub(hn, j, j + 1), acc=sub(ac3, j, j + 1))
            mm(P("pK", 4, 8), IDF, VC, True, False); mm(P("pK", 4, 8), IDM, ac2, False, False, True)
            mm(P("pK", 0, 4), IDL, hn, False, False, True); mm(P("pK", 0, 4), IDL, sub(hv, 15, 64, 16), False, False)
            mm(P("pK", 0, 4), IDF, ac2, False, False, True); mm(P("pK", 0, 4), IDF, ac3, False, True)
            rk = [dict(P("pK", j, j + 1), share=1) for j in range(8)]
            if NLS:
                rs = fb("rk", 4); cp(rs, dict(P("pK", 0, 4), share=1))
            mm(P("pW", 0, 64), IDB, IOQ, True, False)
            terms = []
            for j in range(4):
                eq = hb("eq%d" % j); ts(eq, IO2, rk[j], A.is_equal, rk[4 + j], A.mult)
                if j < NLS:
                    lt = bb("ls%d" % j); act(lt, IO2, F.Sign, bias=sub(rs, j, j + 1), scale=-1.0)
                    terms += [(QH5, eq), (QB5, lt)]
                else:
                    lt = hb("lt%d" % j); ts(lt, IO2, rk[j], A.is_gt, -2.0, A.mult)
                    terms += [(QH5, eq), (QH5, lt)]
            qmm("pW", terms, False)
            srcU = qwrap("src", "pW", 0.25 - 8 * NLS)
    for h in range(2):
        dma("ys"[h], T.y[:, 2048 * h:2048 * h + 2048], T.B[0::16, 2048 * h:2048 * h + 2048], [R("B", 2048 * h, 2048 * h + 2048)], [], 2500)
    return ops


def schedule_whole(ops):
    n = len(ops)
    hist = {}
    pred = [set() for _ in range(n)]
    for i, o in enumerate(ops):
        for w, regs in ((False, o["rd"]), (True, o["wr"])):
            for (nm, lo, hi) in regs:
                for (j, l2, h2, w2) in hist.get(nm, []):
                    if j != i and (w or w2) and l2 < hi and lo < h2:
                        pred[i].add(j)
        for (nm, lo, hi) in o["wr"]:
            hist[nm] = [x for x in hist.get(nm, []) if not (lo <= x[1] and x[2] <= hi)] + [(i, lo, hi, True)]
        for (nm, lo, hi) in o["rd"]:
            hist.setdefault(nm, []).append((i, lo, hi, False))
    fake = [[o["ext"][1]] if o["ext"] else [] for o in ops]

    lats = [o["lat"] for o in ops]
    anc = [0] * n
    fwd = []
    for i in range(n):
        far = 0
        for j in pred[i]:
            far |= anc[j]
        fwd.append([(j, lats[j]) for j in sorted(pred[i]) + fake[i] if lats[j] or not far >> j & 1])
        for j in pred[i]:
            far |= 1 << j
        anc[i] = far
    bwd = [[] for _ in range(n)]
    for i in range(n):
        for j, h in fwd[i]:
            bwd[j].append((i, h))
    alts = [[(e, x[1]) for e, x in sorted(o["alt"].items())] if "alt" in o else [(o["eng"], o["dur"])] for o in ops]

    def put(seq, edges, rel, fixed, lean):
        busy = {e: [] for e in "vspgy"}
        st = [0.0] * n
        en = [0.0] * n
        eng = [None] * n
        for i in seq:
            pick = None
            for e, d in alts[i]:
                if fixed and fixed[i] != e:
                    continue
                t = rel[i]
                same = 0.0 if e == "p" else HOP_SAME
                for j, h in edges[i]:
                    x = en[j] + h + (same if eng[j] == e else HOP)
                    if x > t:
                        t = x
                lst = busy[e]
                lo = 0
                hi = len(lst)
                while lo < hi:
                    m = (lo + hi) // 2
                    if lst[m][1] <= t:
                        lo = m + 1
                    else:
                        hi = m
                while lo < len(lst) and t + d > lst[lo][0]:
                    t = lst[lo][1]
                    lo += 1
                c = t + d + (lean[i] if e == "v" else 0.0)
                if pick is None or c < pick[0]:
                    pick = (c, e, t, d, lo)
            c, e, t, d, lo = pick
            busy[e].insert(lo, (t, t + d))
            st[i] = t
            en[i] = t + d
            eng[i] = e
        return st, en, eng
    zero = [0.0] * n
    span = lambda en: max(en[i] + lats[i] for i in range(n))
    seed = [SEED]

    def rnd():
        seed[0] = (seed[0] * 1103515245 + 12345) % 2147483648
        return seed[0] / 2147483648.0

    def ordered(key):
        for i in range(n):
            for j, h in fwd[i]:
                if key[j] >= key[i]:
                    key[i] = key[j] + 0.001
        return sorted(range(n), key=lambda k: key[k])

    def settle(key, lean):
        r1 = put(ordered(key), fwd, zero, None, lean)
        r2 = put(sorted(range(n), key=lambda k: (-r1[1][k], -k)), bwd, lats, r1[2], zero)
        r3 = put(ordered([-x for x in r2[1]]), fwd, zero, r1[2], zero)
        return r1 if span(r1[1]) < span(r3[1]) else r3

    def blocks(r):
        st, en, eng = r
        last = {}
        before = {}
        for i in sorted(range(n), key=lambda k: st[k]):
            before[i] = last.get(eng[i])
            last[eng[i]] = i
        out = []
        i = max(range(n), key=lambda k: en[k] + lats[k])
        while True:
            d = None
            for j, h in fwd[i]:
                x = en[j] + h + ((0.0 if eng[i] == "p" else HOP_SAME) if eng[j] == eng[i] else HOP)
                if d is None or x > d[0]:
                    d = (x, j)
            if d is not None and d[0] >= st[i] - 0.01:
                i = d[1]
            elif before[i] is not None:
                out.append((before[i], i))
                i = before[i]
            else:
                return out
    if "best" not in KEPT:
        bl = [0.0] * n
        for i in range(n - 1, -1, -1):
            bl[i] += ops[i]["dur"] + (0.0 if bwd[i] else lats[i])
            for j, h in fwd[i]:
                bl[j] = max(bl[j], bl[i] + h + HOP)
        flex = [i for i in range(n) if len(alts[i]) > 1]
        lean = [LEAN] * n
        best = settle([-x for x in bl], lean)
        cur = best
        for it in range(TRIES):
            lo = rnd() * span(cur[1]) - 2000; hi = lo + 1500 + WIN * rnd(); amp = 100 + AMP * rnd()
            key = [x + (amp * (rnd() - 0.5) if lo <= x < hi else 0.0) for x in cur[0]]
            l2 = [(-1e9 if cur[2][i] == "v" else 1e9) for i in range(n)]
            if rnd() < AIM:
                if KEPT.get("of") is not cur:
                    KEPT["of"] = cur
                    KEPT["blocks"] = blocks(cur)
                bs = KEPT["blocks"]
                key = list(cur[0])
                for x in range(1 + int(2.5 * rnd() ** 2)):
                    b, i = bs[int(rnd() * len(bs))]
                    u = rnd()
                    if u < 0.25 and len(alts[b]) > 1:
                        l2[b] = -l2[b]
                    elif u < 0.4 and len(alts[i]) > 1:
                        l2[i] = -l2[i]
                    elif u < 0.75:
                        key[b] = key[i] + 1 + 1500 * rnd() ** 2
                    else:
                        d = key[i] - key[b] + 1 + 1500 * rnd() ** 2
                        todo = [i]
                        key[i] -= d
                        while todo:
                            k = todo.pop()
                            for j, h in fwd[k]:
                                if key[j] >= key[k]:
                                    key[j] = key[k] - 0.001
                                    todo.append(j)
            else:
                for i in flex:
                    if lo <= cur[0][i] < hi and rnd() < 0.3:
                        l2[i] = LEAN * (2.5 * rnd() - 0.5)
            r = settle(key, l2) if it % JUST == 0 else put(ordered(key), fwd, zero, None, l2)
            if span(r[1]) <= span(cur[1]) + TOL * (1.0 - it / TRIES):
                cur = r
                if span(r[1]) < span(best[1]):
                    best = r
        KEPT["best"] = best
    best = KEPT["best"]
    for i in range(n):
        if "alt" in ops[i]:
            ops[i]["eng"] = best[2][i]
            ops[i]["fn"], ops[i]["dur"] = ops[i]["alt"][best[2][i]]
    start = best[0]
    end = [best[1][i] + lats[i] for i in range(n)]
    order = {}
    for i in sorted(range(n), key=lambda k: (start[k], k)):
        order.setdefault(ops[i]["eng"], []).append(i)
    return pred, order, start, end


def schedule(ops):
    n = len(ops)
    hist = {}
    pred = [set() for _ in range(n)]
    for i, o in enumerate(ops):
        for w, regs in ((False, o["rd"]), (True, o["wr"])):
            for (nm, lo, hi) in regs:
                for (j, l2, h2, w2) in hist.get(nm, []):
                    if j != i and (w or w2) and l2 < hi and lo < h2:
                        pred[i].add(j)
        for (nm, lo, hi) in o["wr"]:
            hist[nm] = [x for x in hist.get(nm, []) if not (lo <= x[1] and x[2] <= hi)] + [(i, lo, hi, True)]
        for (nm, lo, hi) in o["rd"]:
            hist.setdefault(nm, []).append((i, lo, hi, False))
    if "best" not in KEPT:
        KEPT["best"] = search(ops, pred)
    best = KEPT["best"]
    for i in range(n):
        if "alt" in ops[i]:
            ops[i]["eng"] = best[2][i]
            ops[i]["fn"], ops[i]["dur"] = ops[i]["alt"][best[2][i]]
    start = list(best[0])
    loads = [i for i in range(n) if ops[i]["eng"] == "y" and not pred[i]]
    for i, x in zip(loads, sorted(start[i] for i in loads)):
        start[i] = x
    end = [start[i] + ops[i]["dur"] + ops[i]["lat"] for i in range(n)]
    order = {}
    for i in sorted(range(n), key=lambda k: (start[k], k)):
        order.setdefault(ops[i]["eng"], []).append(i)
    return pred, order, start, end


def search(ops, pred):
    n = len(ops)
    lats = [o["lat"] for o in ops]
    anc = [0] * n
    fwd = []
    for i in range(n):
        far = 0
        for j in pred[i]:
            far |= anc[j]
        fwd.append([(j, lats[j]) for j in sorted(pred[i]) + ([ops[i]["ext"][1]] if ops[i]["ext"] else []) if lats[j] or not far >> j & 1])
        for j in pred[i]:
            far |= 1 << j
        anc[i] = far
    alts = [[(e, x[1]) for e, x in sorted(o["alt"].items())] if "alt" in o else [(o["eng"], o["dur"])] for o in ops]
    tail = list(lats)
    for i in range(n - 1, -1, -1):
        d = min(x[1] for x in alts[i])
        for j, h in fwd[i]:
            tail[j] = max(tail[j], tail[i] + d + h + (0.0 if ops[i]["eng"] == ops[j]["eng"] == "p" else HOP))
    st = [0.0] * n
    en = [0.0] * n
    eng = [None] * n
    seed = [SEED]

    def rnd():
        seed[0] = (seed[0] * 1103515245 + 12345) % 2147483648
        return seed[0] / 2147483648.0

    def place(lst, t, d):
        lo = 0
        hi = len(lst)
        if not hi or lst[-1][1] <= t:
            return t, hi
        while lo < hi:
            m = (lo + hi) // 2
            if lst[m][1] <= t:
                lo = m + 1
            else:
                hi = m
        while lo < len(lst) and t + d > lst[lo][0]:
            t = lst[lo][1]
            lo += 1
        return t, lo

    def put(seq, base, lean, bound):
        busy = {e: list(base[e]) for e in base}
        worst = 0.0
        total = 0.0
        for i in seq:
            pick = None
            for e, d in alts[i]:
                t = 0.0
                for j, h in fwd[i]:
                    x = en[j] + h + (0.0 if e == "p" == eng[j] else HOP)
                    if x > t:
                        t = x
                t, lo = place(busy[e], t, d)
                c = t + d + (lean[i] if e == "v" else 0.0)
                if pick is None or c < pick[0]:
                    pick = (c, e, t, d, lo)
            c, e, t, d, lo = pick
            busy[e].insert(lo, (t, t + d))
            st[i] = t
            en[i] = t = t + d
            eng[i] = e
            total += t
            t += tail[i]
            if t > worst:
                worst = t
                if t > bound:
                    return None
        return worst + SOFT * total / len(seq), worst

    def ordered(a, b, key):
        for i in range(a, b):
            for j, h in fwd[i]:
                if j >= a and key[j] >= key[i]:
                    key[i] = key[j] + 0.001
        return sorted(range(a, b), key=lambda k: key[k])

    def pull(todo, a, key):
        while todo:
            k = todo.pop()
            for j, h in fwd[k]:
                if j >= a and key[j] >= key[k]:
                    key[j] = key[k] - 0.001
                    todo.append(j)

    def blocks(a, b):
        last = {}
        before = {}
        for i in sorted(range(a, b), key=lambda k: st[k]):
            before[i] = last.get(eng[i])
            last[eng[i]] = i
        out = []
        i = max(range(a, b), key=lambda k: en[k] + tail[k])
        while i >= a:
            d = None
            for j, h in fwd[i]:
                x = en[j] + h + (0.0 if eng[i] == "p" == eng[j] else HOP)
                if d is None or x > d[0]:
                    d = (x, j)
            if d is not None and d[0] >= st[i] - 0.01:
                i = d[1]
            elif before[i] is not None:
                out.append((before[i], i))
                i = before[i]
            else:
                break
        return out

    def late(a, b):
        busy = {e: [] for e in "vspgy"}
        back = {i: tail[i] for i in range(a, b)}
        for i in sorted(range(a, b), key=lambda k: (-en[k], -k)):
            d = en[i] - st[i]
            t, lo = place(busy[eng[i]], back[i], d)
            busy[eng[i]].insert(lo, (t, t + d))
            back[i] = -t - d
            for j, h in fwd[i]:
                if j >= a:
                    back[j] = max(back[j], t + d + h + (0.0 if eng[i] == "p" == eng[j] else HOP))
        return back

    def improve(a, b, base, key, lean, tries):
        cur = put(ordered(a, b, key), base, lean, 1e18)
        keep = (st[a:b], en[a:b], eng[a:b])
        best = (cur, keep)
        bs = blocks(a, b)
        for it in range(tries):
            key = dict(zip(range(a, b), keep[0]))
            l2 = dict(zip(range(a, b), [-1e9 if e == "v" else 1e9 for e in keep[2]]))
            if rnd() < RUN:
                lo = a + int(rnd() * (b - a)); d = (rnd() - 0.6) * 6000 * rnd()
                todo = list(range(lo, min(b, lo + 3 + int(40 * rnd() ** 2))))
                for i in todo:
                    key[i] += d
                    if len(alts[i]) > 1 and rnd() < 0.2:
                        l2[i] = LEAN * (2.5 * rnd() - 0.5)
                if d < 0:
                    pull(todo, a, key)
            elif bs and rnd() < AIM:
                for x in range(1 + int(2.5 * rnd() ** 2)):
                    p, i = bs[int(rnd() * len(bs))]
                    u = rnd()
                    if u < 0.25 and len(alts[p]) > 1:
                        l2[p] = -l2[p]
                    elif u < 0.4 and len(alts[i]) > 1:
                        l2[i] = -l2[i]
                    elif u < 0.75:
                        key[p] = key[i] + 1 + 1500 * rnd() ** 2
                    else:
                        key[i] = key[p] - 1 - 1500 * rnd() ** 2
                        pull([i], a, key)
            else:
                lo = keep[0][int(rnd() * (b - a))] - 1000; hi = lo + 1500 + WIN * rnd(); amp = 100 + AMP * rnd()
                for i in range(a, b):
                    if lo <= key[i] < hi:
                        key[i] += amp * (rnd() - 0.5)
                        if len(alts[i]) > 1 and rnd() < 0.3:
                            l2[i] = LEAN * (2.5 * rnd() - 0.5)
            tol = TOL * (1.0 - it / tries)
            if it % JUST == 0:
                put(ordered(a, b, key), base, l2, 1e18)
                l2 = dict(zip(range(a, b), [-1e9 if e == "v" else 1e9 for e in eng[a:b]]))
                key = late(a, b)
            r = put(ordered(a, b, key), base, l2, cur[1] + tol + 300.0)
            if r is not None and r[0] <= cur[0] + tol:
                cur = r
                keep = (st[a:b], en[a:b], eng[a:b])
                bs = blocks(a, b)
                if r[0] < best[0][0]:
                    best = (r, keep)
        st[a:b], en[a:b], eng[a:b] = best[1]

    def refine(b, since, until, tries):
        whole = sorted(range(b), key=lambda k: (st[k], k))
        head = [i for i in whole if st[i] < since]
        act = [i for i in whole if since <= st[i] < until]
        rest = [i for i in whole if st[i] >= until]
        loc = {i: x for x, i in enumerate(act)}
        m = len(act)
        deg = [len([j for j, h in fwd[i] if j in loc]) for i in act]
        alt = [dict(alts[i]) for i in act]
        on = [eng[i] for i in act]
        seq = {e: [x for x in range(m) if on[x] == e] for e in "vspgy"}
        sets = []
        for c in range(len(COSTS)):
            end, free = play(head, c)
            rel = [max([end[j] + h for j, h in edges[c][i] if j not in loc] + [0.0]) for i in act]
            nxt = [[] for i in act]
            for x, i in enumerate(act):
                for j, h in edges[c][i]:
                    if j in loc:
                        nxt[loc[j]].append((x, h))
            tl = list(tails[c])
            then = {e: -1e18 for e in "vspgy"}
            for i in reversed(rest):
                then[eng[i]] = d = max(tl[i], then[eng[i]]) + ops[i]["times"][c][eng[i]]
                for j, h in edges[c][i]:
                    if d + h > tl[j]:
                        tl[j] = d + h
            sets.append((rel, free, nxt, [tl[i] for i in act], [ops[i]["times"][c] for i in act], tails[0][0] / tails[c][0], then))

        def times(bound):
            left = list(deg)
            after = [-1] * m
            for e in seq:
                q = seq[e]
                for x, y in zip(q, q[1:]):
                    after[x] = y
                    left[y] += 1
            todo = [x for x in range(m) if not left[x]]
            nxt = sets[0][2]
            for x in todo:
                for y, h in nxt[x]:
                    left[y] -= 1
                    if not left[y]:
                        todo.append(y)
                y = after[x]
                if y >= 0:
                    left[y] -= 1
                    if not left[y]:
                        todo.append(y)
            if len(todo) < m:
                return None
            total = 0.0
            waits = []
            parts = []
            for c, (rel, free, nxt, tl, dur, scale, then) in enumerate(sets):
                t0 = list(rel)
                by = [-1] * m
                for e in seq:
                    if seq[e]:
                        t0[seq[e][0]] = max(t0[seq[e][0]], free[e])
                worst = 0.0
                last = -1
                for x in todo:
                    t = t0[x] + dur[x][on[x]]
                    if t + tl[x] > worst:
                        worst = t + tl[x]
                        last = x
                    for y, h in nxt[x]:
                        if t + h > t0[y]:
                            t0[y] = t + h
                            by[y] = x
                    y = after[x]
                    if y < 0:
                        if t + then[on[x]] > worst:
                            worst = t + then[on[x]]
                            last = x
                    elif t > t0[y]:
                        t0[y] = t
                        by[y] = -2 - x
                parts.append((worst + SOFT * sum(t0) / m) * scale / len(sets))
                if bound and sum(parts) + sum(bound[1][c + 1:]) - 400.0 * (len(sets) - 1 - c) > bound[0]:
                    return None
                if c == 0:
                    first = t0
                while last != -1:
                    p = by[last]
                    if p < -1:
                        p = -2 - p
                        waits.append((p, last))
                    last = p
            return sum(parts), first, waits, parts
        cur = times(None)
        best = (cur, list(on))
        for it in range(tries):
            if not cur[2]:
                break
            p, i = cur[2][int(rnd() * len(cur[2]))]
            u = rnd()
            x = p if rnd() < 0.5 else i
            if u < 0.1:
                x = int(rnd() * m)
            e = on[x]
            q = seq[e]
            k = q.index(x)
            if u < 0.35 and len(alt[x]) > 1:
                e2 = [z for z in alt[x] if z != e][int(rnd() * (len(alt[x]) - 1))]
                q2 = seq[e2]
                k2 = 0
                lim = cur[1][x] + (rnd() - 0.5) * 1200
                while k2 < len(q2) and cur[1][q2[k2]] < lim:
                    k2 += 1
            else:
                e2 = e
                q2 = q
                step = 1 + int(6 * rnd() ** 2)
                k2 = max(0, k - step) if x == i else min(len(q) - 1, k + step)
            del q[k]
            q2.insert(k2, x)
            on[x] = e2
            lim = cur[0] + HEAT * (1.0 - it / tries) * rnd() ** 2
            r = times((lim, cur[3]))
            if r is not None and r[0] <= lim:
                cur = r
                if r[0] < best[0][0]:
                    best = (r, list(on))
            else:
                del q2[k2]
                q.insert(k, x)
                on[x] = e
        for x, i in enumerate(act):
            eng[i] = best[1][x]
        whole = head + [act[x] for x in sorted(range(m), key=lambda k: (best[0][1][k], k))] + rest
        for i, t in play(whole, 0)[0].items():
            en[i] = t
            st[i] = t - ops[i]["times"][0][eng[i]]
        return best[0][0]

    def play(seq, c):
        end = {}
        free = {e: 0.0 for e in "vspgy"}
        for i in seq:
            end[i] = free[eng[i]] = max([free[eng[i]]] + [end[j] + h for j, h in edges[c][i]]) + ops[i]["times"][c][eng[i]]
        return end, free
    edges = [[[(j, h + (0.0 if ops[i]["eng"] == ops[j]["eng"] == "p" else c[4])) for j, h in fwd[i]] for i in range(n)] for c in COSTS]
    tails = []
    for c in range(len(COSTS)):
        tl = list(lats)
        for i in range(n - 1, -1, -1):
            for j, h in edges[c][i]:
                tl[j] = max(tl[j], tl[i] + min(ops[i]["times"][c].values()) + h)
        tails.append(tl)

    cuts = [0] + [i + 1 for i in range(n) if "cut" in ops[i]] + [n]
    sig = [(o["eng"], round(o["dur"]), len(o["rd"]), o["wr"][0][0][:2] if o["wr"] else "") for o in ops]
    base = {e: [] for e in "vspgy"}
    for s in range(len(cuts) - 1):
        a, b = cuts[s], cuts[s + 1]
        key = {i: -tail[i] - alts[i][0][1] for i in range(a, b)}
        lean = {i: LEAN for i in range(a, b)}
        if s >= 2:
            p = cuts[s - 1]
            k2 = {}
            l2 = {}
            at = st[p]
            for i in range(a, b):
                q = p
                while q < a and q < p + 12 and sig[q] != sig[i]:
                    q += 1
                if q < a and sig[q] == sig[i]:
                    at = st[q]
                    l2[i] = -1e9 if eng[q] == "v" else 1e9
                    p = q + 1
                else:
                    l2[i] = LEAN
                k2[i] = at
            if put(ordered(a, b, k2), base, l2, 1e18)[0] < put(ordered(a, b, key), base, lean, 1e18)[0]:
                key, lean = k2, l2
        since = max(en[:a] + [0.0]) - BACK
        was = (list(st), list(en), list(eng))
        best = None
        for x in range(AGAIN):
            st[:], en[:], eng[:] = was
            improve(a, b, base, dict(key), lean, TRIES)
            r = refine(b, since, 1e18, MOVES)
            if best is None or r < best[0]:
                best = (r, list(st), list(en), list(eng))
        st[:], en[:], eng[:] = best[1:]
        base = {e: sorted((st[i], en[i]) for i in range(b) if eng[i] == e) for e in "vspgy"}
    for x in range(SWEEPS):
        t = -PANE * rnd()
        while t < max(en):
            refine(n, t, t + PANE, POLISH)
            t += PANE / 2
    whole = sorted(range(n), key=lambda k: (st[k], k))
    KEPT["spans"] = [max(t + lats[i] for i, t in play(whole, c)[0].items()) for c in range(len(COSTS))]
    return st, en, eng


def rank_program(g, core, T, topo):
    rank = T.rank_of(core)
    if rank is None:
        return
    ops = build(T, rank)
    pred, order, start, end = schedule(ops)
    Q = {"v": g.vector, "s": g.scalar, "p": g.tensor, "g": g, "y": g.sync}
    CNT = {"v": "cv", "s": "cs", "p": "cp", "g": "cg"}
    pos = {}
    for e in order:
        for x, i in enumerate(order[e]):
            pos[i] = x
    need = {}
    marked = set()
    for e in order:
        seen = {}
        for i in order[e]:
            w = []
            best = {}
            for j in pred[i]:
                ej = ops[j]["eng"]
                if ops[j]["kind"] == "d":
                    if ("d", j) not in seen:
                        seen[("d", j)] = 1
                        w.append(j)
                elif ops[j]["kind"] == "c" and not (ej == "p" and e == "p"):
                    if pos[j] > seen.get(ej, -1) and pos[j] > pos.get(best.get(ej, -1), -1):
                        best[ej] = j
            for ej, j in best.items():
                seen[ej] = pos[j]
                w.append(j)
                marked.add(j)
            need[i] = w
    tick = {}
    total = {}
    nd = 0
    for e in order:
        comp = [i for i in order[e] if ops[i]["kind"] == "c"]
        if comp:
            marked.add(comp[-1])
        c = 0
        for i in order[e]:
            if ops[i]["kind"] == "d":
                tick[i] = ("d%d" % nd, 16)
                nd += 1
            elif i in marked:
                c += 1
                tick[i] = (CNT[e], c)
        if comp:
            total[CNT[e]] = c
    peers = [p for p in T.cores if p != core]
    use = [x for x in topo.engines(core, peers[0]) if all(x in topo.engines(core, p) for p in peers)]
    sent = 0
    for i in sorted(range(len(ops)), key=lambda k: (start[k], k)):
        o = ops[i]
        q = Q[o["eng"]]
        for j in need[i]:
            q.wait_ge(T.sem[tick[j][0]], tick[j][1])
        if o["ext"]:
            q.wait_ge(T.sem[o["ext"][0]], len(use) * len(peers))
        if o["kind"] == "r":
            t = o["fn"][1]
            mine = T.RV[:, 16 * t + 4 * rank:16 * t + 4 * rank + 4]
            to = [DstId(rid=topo.addr(p)[0], pnc=topo.addr(p)[1]) for p in peers]
            g.remote_dma_fused([RemoteDMATransfer(dst_ids=to, dma_engine_mask=sum(1 << x for x in use), remote_sem=T.sem["ar%d" % t],
                                                  srcs=[mine], dsts=[mine] * len(peers))], local_sem=T.sem.loc)
            sent += len(use)
        else:
            ins = o["fn"](g)
            if o["kind"] == "d":
                ins.then_inc(T.sem[tick[i][0]], 16)
            elif i in marked:
                ins.then_inc(T.sem[tick[i][0]], 1)
    g.wait_ge(T.sem.loc, sent)
    for k, c in total.items():
        g.wait_ge(T.sem[k], c)
    for i in tick:
        if ops[i]["kind"] == "d":
            g.wait_ge(T.sem[tick[i][0]], 16)
